import numpy as np, ml_dtypes
CORES = [1,5,17,21,33,37,49,53]
N = 8
import mx_ref
BF = ml_dtypes.bfloat16
def gentries(a):
    return np.ascontiguousarray(a.reshape(8, 16, -1).transpose(0, 2, 1)).reshape(8, -1)
def gtable(e):
    e = np.asarray(e); return np.ascontiguousarray(e.reshape(8, -1, 16).transpose(0, 2, 1)).reshape(128, -1).astype(np.int32)
def gcols(t, e):
    v = np.concatenate([t.reshape(8, 16, -1, 4), np.zeros((8, 16, 1, 4), BF)], axis=2)
    return np.ascontiguousarray(np.stack([v[g][:, e[g]] for g in range(8)])).reshape(128, -1)
def tile(rs):
    return np.stack(rs, axis=2).reshape(128, -1).astype(BF)
def pick(q, e):
    c = np.concatenate([q[0].reshape(128, -1, 4), np.zeros((128, 1, 4), np.uint8)], axis=1); s = np.concatenate([q[1], np.ones((16, 1), np.uint8)], axis=1)
    return (np.ascontiguousarray(c[:, e].reshape(128, -1)), np.ascontiguousarray(s[:, e]))
def join(*qs):
    return (np.concatenate([q[0] for q in qs], axis=1), np.concatenate([q[1] for q in qs], axis=1))
def put(q, e, v):
    c, s = q[0].reshape(128, -1, 4).copy(), q[1].copy(); c[:, e] = v[0].reshape(128, -1, 4); s[:, e] = v[1]
    return (c.reshape(128, -1), s)
def pk(c, s):
    return (np.ascontiguousarray(c), mx_ref.live(s))
def emit(q):
    return q[0], q[1]
def packed(v, rng):
    q = [mx_ref.quantize(np.ascontiguousarray(v[r])) for r in range(N)]
    return np.stack([a for a, b in q]), np.stack([mx_ref.plane(b, rng) for a, b in q])
def values_of_codes():
    e, c = np.zeros((128, 128, 4), np.float32), np.zeros((128, 2, 4), np.uint8)
    e[np.arange(128), np.arange(128), 0] = 1
    c[:127, :, 0] = np.arange(256).reshape(2, 128).T[:127]
    return mx_ref.matmul(mx_ref.quantize(e.reshape(128, 512).astype(BF)), (c.reshape(128, 8), np.full((16, 2), 127, np.uint8))).T.reshape(-1).astype(np.float64)
CODE_VALUE, SCALE_VALUE = values_of_codes(), 2.0 ** (np.arange(256) - 127.0)
def decode(q):
    return (CODE_VALUE[q[0]].reshape(16, 8, -1, 4) * SCALE_VALUE[q[1]][:, None, :, None] + 0.0).reshape(128, -1).astype(np.float32)
def f(rng, *shape):
    return mx_ref.flush((rng.standard_normal(shape, dtype=np.float32) * np.exp2(rng.integers(-2, 3, shape[:-1] + (1,)))).astype(BF))
def wide(rng, *shape, cols=0):
    v = rng.standard_normal(shape, dtype=np.float32) * np.exp2(rng.integers(-12, 13, shape)).astype(np.float32)
    if cols: v *= np.repeat(np.exp2(rng.integers(-cols, cols + 1, shape[:-2] + (1, shape[-1] // 4))) * (rng.random(shape[:-2] + (1, shape[-1] // 4)) > 0.0625), 4, axis=-1).astype(np.float32)
    return mx_ref.flush(v.astype(BF))
C, H = 320, 160
STEP = [1, 2, 4]
def numbers_of(rng):
    return {"x": np.array(f(rng, N, 128, 4 * C)), "u": np.array(f(rng, N, 128, 512)), "v": np.array(f(rng, N, 128, 512))}
def stored(k):
    return {"nl": np.stack([gtable(k[r]) for r in range(N)])}
def lists(rng):
    return stored(rng.permuted(np.tile(np.arange(C), (N, 8, 1)), axis=2))
def layers(rng, still=()):
    w = np.array(f(rng, N, 128, 2048)).reshape(N, 8, 16, 4, 8, 16, 4)
    for i in still:
        w[:, :, i] = 0
        w[:, :, :, :, :, i] = 0
    return w
def weights(rng, w):
    c, p = packed(np.ascontiguousarray(w).reshape(N, 128, 2048), rng)
    return {"wc": c, "ws": p}
def setup_inputs(rng):
    return {**numbers_of(rng), **lists(rng), **weights(rng, layers(rng))}
def setup_inputs_ties(rng):
    d = numbers_of(rng)
    o = rng.permutation(N)
    k = rng.integers(-1, 2, (N, 8, 3, C)).astype(np.float32)
    k[o[1]] = 1
    x = d["x"].reshape(N, 8, 16, C, 4)
    x[:, :, :3] = 0
    x[:, :, :3, :, 0] = k.astype(BF)
    c = np.ones(N, np.float32)
    c[o[0]] = 0
    c[o[2]] = -1
    u = d["u"].reshape(N, 8, 16, 8, 16, 4)
    u[:, :, :, :, :3] = 0
    g = np.arange(8)
    for j in range(3): u[:, g, j, g, j, 0] = c.astype(BF)[:, None]
    w = layers(rng)
    w[:, :, :, :, :, :8] = 0
    return {"x": x.reshape(N, 128, 4 * C), "u": u.reshape(N, 128, 512), "v": d["v"], **lists(rng), **weights(rng, w)}
def setup_inputs_near(rng):
    d = numbers_of(rng)
    o = rng.permutation(N) % 3
    x = d["x"].astype(np.float32).reshape(N, 8, 16, C, 4)
    u = d["u"].astype(np.float32).reshape(N, 8, 16, 8, 16, 4)
    w = layers(rng, range(8))
    x[:, :, :8] = 0
    u[:, :, :, :, :3] = 0
    g = np.arange(8)
    for r in range(N):
        k, e = (1.0, 1.0) if o[r] == 0 else (2.0 ** -28, 2.0 ** -30)
        if o[r] == 2:
            x[r, :, 8:] = 0
            x[r, :, 8, :, 0] = k
            w[r] = 0
        for j in range(3):
            u[r, g, 6, g, j, 0] = e
            if o[r] < 2:
                s = rng.integers(-1, 2, (8, C)) * k
                x[r, :, 2 * j, :, 0] = 1.125 * s
                x[r, :, 2 * j + 1, :, 0] = -1.25 * s
                u[r, g, 2 * j, g, j, 0] = 1.125 * e
                u[r, g, 2 * j + 1, g, j, 0] = e
            else:
                x[r, :, 9 + j, :, 0] = k * rng.choice([-1.0, 1.0], (8, C))
                u[r, g, 12 + j, g, j, 0] = e
                w[r, g, 9 + j, 0, g, 12 + j, 0] = 2.0 ** -8
        at = [0, C - 1, int(rng.integers(C)), int(rng.integers(C))]
        for h, c in zip(rng.permutation(8)[:4], at): x[r, h, 6, c, 0] = 2.0 ** 30 * rng.choice([-1.0, 1.0])
    return {"x": x.reshape(N, 128, 4 * C).astype(BF), "u": u.reshape(N, 128, 512).astype(BF), "v": d["v"], **lists(rng), **weights(rng, w)}
def setup_inputs_odd(rng):
    d = numbers_of(rng)
    x = (1.0 + (2 * rng.integers(0, 64, (N, 16, 8, C, 4)) + 1) * 2.0 ** -7) * np.exp2(-rng.integers(0, 7, (N, 16, 8, C, 4)).astype(np.float64)) * rng.choice([-1.0, 1.0], (N, 16, 8, C, 4))
    x[:, :, 0, :, 0] = 1.96875 * 2.0 ** 8 * rng.choice([-1.0, 1.0], (N, 16, 1))
    u = d["u"].reshape(N, 16, 8, 128, 4)
    u[:, :, 0] = 0
    return {"x": x.astype(np.float32).reshape(N, 128, 4 * C).astype(BF), "u": u.reshape(N, 128, 512), "v": d["v"], **lists(rng), **weights(rng, layers(rng, (0, 8)))}
def setup_inputs_ends(rng):
    d = numbers_of(rng)
    o, e = rng.permutation(N) % 4, rng.permutation(N) % 4
    x = np.zeros((N, 8, 16, C, 4))
    u = d["u"].astype(np.float32).reshape(N, 8, 16, 8, 16, 4)
    v = d["v"].astype(np.float32)
    w = np.zeros((N, 8, 16, 4, 8, 16, 4), np.float32)
    k = np.tile(np.arange(C), (N, 8, 1))
    def sized(small, low, *q):
        return (1.0 + 0.125 * rng.integers(0, 8, q)) * 2.0 ** -30 if small else (low + 0.1 * rng.random(q)) * 2.0 ** 30
    for r in range(N):
        h = rng.permutation(8)
        c = np.where(h < 2, 0.0, h % 2 * 2.0 - 1.0)[:, None] * np.where((h > 5)[:, None], [1.0, -1.0, 1.0], 1.0)
        c = c[None, None, :, :, None]
        if o[r] == 3:
            x[r] = d["x"][r].astype(np.float32).reshape(8, 16, C, 4)[:, :, :1]
            u[r, :, :, :, :3] *= np.abs(c).astype(np.float32)
        else:
            small = o[r] == 2
            x[r] = sized(small, 0.7, 8, 16, C, 4) * (rng.choice([-1.0, 1.0], (C, 1)) if o[r] == 1 else -1.0)
            u[r, :, :, :, :3] = c * sized(small, 0.9, 8, 16, 8, 3, 4)
            v[r] = sized(small, 0.9, 128, 512) * rng.choice([-1.0, 1.0], (128, 512))
        if o[r] != 2: x[r, :, 14:] = 0
        i, last = np.arange(14), np.arange(14, 16)
        for g in range(8):
            for b in range(4):
                w[r, g, i, b, g, i, b] = 2.0 ** -8 if o[r] == 3 else 2.0
                if o[r] == 2: w[r, g, last, b, g, last, b] = 256.0
        if e[r] == 1: k[r] = C - 1 - np.arange(C)
        if e[r] == 2:
            k[r, :, :H] = 2 * np.arange(H)
            k[r, :, H:] = 2 * np.arange(H)[::-1] + 1
        if e[r] == 3: k[r] = rng.permuted(k[r], axis=1)
    return {"x": x.astype(np.float32).reshape(N, 128, 4 * C).astype(BF), "u": u.reshape(N, 128, 512).astype(BF), "v": v.astype(BF), **stored(k), **weights(rng, w.astype(BF))}
def setup_inputs_spread(rng):
    d = setup_inputs(rng)
    d["x"] = wide(rng, N, 128, 4 * C, cols=6)
    return d
def check_inputs(d):
    b = []
    for k in ("x", "u", "v"):
        a = np.abs(d[k].astype(np.float32))
        if not (np.isfinite(a).all() and ((a == 0) | (a >= 2.0 ** -30) & (a <= 2.0 ** 30)).all()): b.append("a value of " + k)
    none, least, most = [emit(mx_ref.quantize(np.full((128, 16), k, np.float32).astype(BF)))[1][0, 0] for k in (0.0, 2.0 ** -8, 2.0 ** 8)]
    for r in range(N):
        if (np.sort(gentries(d["nl"][r]), axis=1) != np.arange(C)).any(): b.append("nl: a list that is no permutation")
        if ((d["wc"][r] == 0x7F) | (d["wc"][r] == 0xFF)).any(): b.append("wc: a code that is no number")
        s = mx_ref.live(d["ws"][r])
        if ((s != none) & ((s < least) | (s > most))).any(): b.append("ws: a scale out of range")
        if (((d["wc"][r].reshape(16, 8, 512, 4) & 0x7F) != 0) & (s == none)[:, None, :, None]).any(): b.append("wc: a code other than zero under the scale of zeros")
    return b
def ends(n):
    return np.take_along_axis(np.argsort(n, axis=1), n ^ 1, axis=1)
def reference(x, u, v, nl, wc, ws):
    qu = [mx_ref.quantize(u[r]) for r in range(N)]
    lay = [pk(wc[r], ws[r]) for r in range(N)]
    name = [gentries(nl[r]).astype(np.int64) for r in range(N)]
    now = [x[r] for r in range(N)]
    for step in STEP:
        z = []
        for r in range(N):
            s = mx_ref.matmul(qu[r], mx_ref.quantize(now[r])).reshape(8, 16, C)
            for j in range(3):
                d = ends(name[r])
                h = np.where(name[r] % 2 == 0, np.arange(C), d)
                flag = np.take_along_axis(s[:, j], h, axis=1) > 0
                then = np.roll(name[r], -1, axis=0)
                name[r] = np.roll(np.where(flag, np.take_along_axis(then, d, axis=1), then), 1, axis=0)
            z.append(((gcols(now[r], name[r]).astype(np.float32) + gcols(now[r], ends(name[r])).astype(np.float32)) * np.float32(0.5)).astype(BF))
        made = []
        for r in range(N):
            p = (r - step) % N
            m = np.take_along_axis(np.argsort(name[p], axis=1), name[r], axis=1)
            far = gcols(decode(mx_ref.quantize(z[p])).astype(BF), m[:, :H])
            q = mx_ref.quantize(np.ascontiguousarray(np.concatenate([far, gcols(z[r], m[:, H:])], axis=1)))
            made.append(tile([now[r][:, b::4].astype(np.float32) + mx_ref.matmul(pick(lay[r], np.arange(128 * b, 128 * b + 128)), q) * np.float32(0.03125) for b in range(4)]))
        now = made
    y, nm = np.zeros((N, 128, C), np.float32), np.zeros((N, 8, C), np.float32)
    oc, osc = np.zeros((N, 128, 4 * C), np.uint8), np.zeros((N, 16, C), np.uint8)
    for r in range(N):
        q = mx_ref.quantize(now[r])
        y[r] = mx_ref.matmul(mx_ref.quantize(v[r]), q)
        nm[r] = name[r]
        oc[r], osc[r] = emit(q)
    return {"y": y, "nm": nm, "oc": oc, "osc": osc}

@@ -1,0 +1,311 @@
+import numpy as np
+from concourse.bass import DstId, RemoteDMATransfer
+from concourse.mybir import dt, AluOpType as OP, AxisListType, ActivationFunctionType as AF
+
+STEP = [1, 2, 4]
+BF, F32, I32, U16, U8, CODE = "bfloat16", "float32", "int32", "uint16", "uint8", "float8_e4m3fn_x4"
+SCRATCH = {
+    "nli": ("sbuf", [128, 20], I32), "ut": ("sbuf", [128, 512], BF), "vt": ("sbuf", [128, 512], BF),
+    "qu": ("sbuf", [128, 128], CODE), "qus": ("sbuf", [128, 128], U8), "qv": ("sbuf", [128, 128], CODE), "qvs": ("sbuf", [128, 128], U8),
+    "uv": ("sbuf", [128, 384], CODE), "uvs": ("sbuf", [128, 384], U8), "wq": ("sbuf", [128, 512], CODE), "wsp": ("sbuf", [128, 512], U8),
+    "et": ("sbuf", [128, 2048], BF), "eq": ("sbuf", [128, 512], CODE), "es": ("sbuf", [128, 512], U8),
+    "jmp": ("sbuf", [128, 16], I32), "jma": ("sbuf", [128, 16], I32),
+    "mk": ("sbuf", [128, 320], BF), "rz": ("sbuf", [128, 320], BF), "icf": ("sbuf", [128, 320], BF),
+    "pi": ("sbuf", [128, 20], I32), "pa": ("sbuf", [128, 20], I32), "qi": ("sbuf", [128, 20], I32), "cw": ("sbuf", [128, 20], F32), "ccw": ("sbuf", [128, 20], F32),
+    "ui": ("sbuf", [128, 24], I32), "ua": ("sbuf", [128, 24], I32), "uo": ("sbuf", [128, 24], U16),
+    "fw": ("sbuf", [128, 960], BF), "sg0": ("sbuf", [128, 320], BF), "sg1": ("sbuf", [128, 320], BF), "gf": ("sbuf", [128, 320], BF),
+    "nf0": ("sbuf", [128, 320], BF), "nf1": ("sbuf", [128, 320], BF), "xf0": ("sbuf", [128, 320], BF), "xf1": ("sbuf", [128, 320], BF),
+    "mo0": ("sbuf", [128, 320], BF), "mo1": ("sbuf", [128, 320], BF), "so0": ("sbuf", [128, 320], BF), "so1": ("sbuf", [128, 320], BF),
+    "lst": ("sbuf", [128, 1600], U16), "fs": ("sbuf", [128, 1600], F32), "ist": ("sbuf", [128, 1600], I32),
+    "pub0": ("sbuf", [128, 40], F32), "pub1": ("sbuf", [128, 40], F32), "shl": ("sbuf", [128, 40], F32),
+    "xh": ("sbuf", [128, 1280], BF), "xg": ("sbuf", [128, 1280], BF), "zn": ("sbuf", [128, 1280], BF), "ft": ("sbuf", [128, 640], BF), "vo": ("sbuf", [128, 640], BF), "vf": ("sbuf", [128, 640], BF),
+    "yo": ("sbuf", [128, 320], F32), "nmf": ("sbuf", [128, 320], F32),
+}
+for _k in range(4):
+    SCRATCH.update({"xt%d" % _k: ("sbuf", [128, 1280], BF), "yt%d" % _k: ("sbuf", [128, 1280], BF), "xq%d" % _k: ("sbuf", [128, 320], CODE), "xs%d" % _k: ("sbuf", [128, 320], U8)})
+for _k in range(3):
+    SCRATCH.update({"fq%d" % _k: ("sbuf", [128, 160], CODE), "fp%d" % _k: ("sbuf", [128, 160], U8), "lq%d" % _k: ("sbuf", [128, 160], CODE), "lp%d" % _k: ("sbuf", [128, 160], U8),
+                    "vq%d" % _k: ("sbuf", [128, 320], CODE), "vp%d" % _k: ("sbuf", [128, 320], U8), "ln%d" % _k: ("sbuf", [128, 10], U16), "li%d" % _k: ("sbuf", [128, 20], U16)})
+for _k in range(8):
+    SCRATCH["p%d" % _k] = ("psum", [128, 512], F32)
+QSEM = {"v": "qv_", "a": "qa_", "t": "qt_", "g": "qg_"}
+SEMAPHORES = list(QSEM.values()) + ["d_nl", "d_u", "d_x0", "d_x1", "d_w", "d_v", "d_sh", "d_os", "sent"] + ["r%s%d" % (a, k) for a in "nid" for k in range(3)]
+
+
+def rank_program(g, core, T, topo):
+    rank = T.rank_of(core)
+    if rank is None:
+        return
+    N = len(T.cores)
+    eng = {"v": g.vector, "a": g.scalar, "t": g.tensor, "g": g, "s": g.sync}
+    count, total = {q: 0 for q in QSEM}, {}
+    seen = {q: {} for q in eng}
+    log = {}
+
+    def need(q, reads, writes):
+        own, deps = QSEM.get(q), []
+        for wr, rs in ((False, reads), (True, writes)):
+            for r in rs:
+                ps = SCRATCH.get(r[0], ("x",))[0] == "psum"
+                for (lo, hi, w, sem, val, clk, st) in log.get(r[0], []):
+                    if not ps and (hi <= r[1] or lo >= r[2]): continue
+                    if not ps and st == r[3] > 2 and (lo - r[1]) % st: continue
+                    if not (w or wr or ps): continue
+                    if sem == own and not w: continue
+                    deps.append((sem, val, clk))
+        best = {}
+        for sem, val, clk in deps:
+            if val > best.get(sem, (0,))[0]: best[sem] = (val, clk)
+        for sem, (val, clk) in sorted(best.items(), key=lambda e: -len(e[1][1])):
+            if seen[q].get(sem, 0) >= val: continue
+            eng[q].wait_ge(T.sem[sem], val)
+            for s, v in list(clk.items()) + [(sem, val)]:
+                if seen[q].get(s, 0) < v: seen[q][s] = v
+
+    def note(accesses, w, sem, val, clk):
+        for r in accesses:
+            a = log.setdefault(r[0], [])
+            if w and r[3] == 1: a[:] = [e for e in a if not (r[1] <= e[0] and e[1] <= r[2])]
+            a.append((r[1], r[2], w, sem, val, clk, r[3]))
+
+    def op(q, fn, writes, reads):
+        need(q, reads, writes)
+        count[q] += 1
+        fn().then_inc(T.sem[QSEM[q]], 1)
+        clk = dict(seen[q])
+        clk[QSEM[q]] = count[q]
+        note(reads, False, QSEM[q], count[q], clk)
+        note(writes, True, QSEM[q], count[q], clk)
+
+    def dma(sem, moves):
+        for q, fn, writes, reads in moves: need(q, reads, writes)
+        clk = {}
+        for q, fn, writes, reads in moves:
+            fn(eng[q]).then_inc(T.sem[sem], 16)
+            total[sem] = total.get(sem, 0) + 16
+            for s, v in seen[q].items(): clk[s] = max(v, clk.get(s, 0))
+        for q, fn, writes, reads in moves:
+            note(reads, False, sem, total[sem], clk)
+        for q, fn, writes, reads in moves:
+            note([(r[0], r[1], r[2], 2) for r in writes], True, sem, total[sem], clk)
+
+    def arrives(sem, val, regions):
+        total[sem] = val
+        note(regions, True, sem, val, {})
+
+    def send(dst, out, inn, sem, region):
+        need("g", [region], [])
+        rid, pid, _ = topo.addr(dst)
+        es = topo.engines(core, dst)[:8]
+        g.remote_dma(out, inn, T.sem[sem], T.sem["sent"], pid, rid, sum(1 << e for e in es))
+        total["sent"] = total.get("sent", 0) + len(es)
+
+    ENG = 8
+
+    def R(name, lo=0, hi=None, st=1): return (name, lo, SCRATCH[name][1][1] if hi is None else hi, st)
+    def ap(r): return T[r[0]][:, r[1]:r[2]:r[3]] if r[3] != 1 else T[r[0]][:, r[1]:r[2]]
+    slots = {"lst": 0, "fs": 0, "ist": 0}
+    def new(name, n=20):
+        a = slots[name]
+        slots[name] += n
+        return R(name, a, a + n)
+    def part(r, a, b): return (r[0], r[1] + a, r[1] + b, 1)
+
+    def tt(out, a, b, o): op("v", lambda: g.vector.tensor_tensor(ap(out), ap(a), ap(b), o), [out], [a, b])
+    def ts(out, a, s1, o1, s2=None, o2=None):
+        if o2 is None: op("v", lambda: g.vector.tensor_scalar(ap(out), ap(a), s1, None, o1), [out], [a])
+        else: op("v", lambda: g.vector.tensor_scalar(ap(out), ap(a), s1, s2, o1, o2), [out], [a])
+    def cp(out, a): op("v", lambda: g.vector.tensor_copy(ap(out), ap(a)), [out], [a])
+    def gv(out, win, off): op("v", lambda: g.vector.tensor_copy(ap(out), ap(win).indirect(ap(off))), [out], [win, off])
+    def ga(out, win, off): op("a", lambda: g.scalar.activation(ap(out), ap(win).indirect(ap(off)), AF.Copy), [out], [win, off])
+    def gt(out, win, off, b, o): op("v", lambda: g.vector.tensor_tensor(ap(out), ap(win).indirect(ap(off)), ap(b), o), [out], [win, off, b])
+    def act(out, a, scale=1.0): op("a", lambda: g.scalar.activation(ap(out), ap(a), AF.Copy, scale=scale), [out], [a])
+    def quant(q, s, a): op("v", lambda: g.vector.quantize_mx(ap(q), ap(s), ap(a)), [q, s], [a])
+    def mm(out, l, ls, r, rs): op("t", lambda: g.tensor.matmul_mx(ap(out), ap(l), ap(ls), ap(r), ap(rs), True, True), [out], [l, ls, r, rs])
+    def iota(out, pattern, base, cm, flag=False):
+        op("g", lambda: g.iota(ap(out), pattern, base, cm, allow_small_or_imprecise_dtypes=True) if flag else g.iota(ap(out), pattern, base, cm), [out], [])
+    turn = [0]
+    def scan(n):
+        m, s = R("mo%d" % turn[0], 0, n), R("so%d" % turn[0], 0, n)
+        op("v", lambda: g.vector.tensor_tensor_scan(ap(s), T["rz"][:, 0:n], ap(m), 0.0, OP.mult, OP.add), [s], [m, R("rz", 0, n)])
+        turn[0] ^= 1
+        return (s[0], 15, n, 16)
+    def pick(win, off, n=320):
+        gt(R("mo%d" % turn[0], 0, n), win, off, R("mk", 0, n), OP.mult)
+        return scan(n)
+    def wrapped(v, n=20):
+        o = new("lst", n)
+        ts(o, v, 160.0, OP.add)
+        return o
+
+    dma("d_nl", [("s", lambda e: e.dma_start(T.nli[:], T.nl[:]), [R("nli")], [])])
+    dma("d_u", [("a", lambda e: e.dma_start(T.ut[:], T.u[:]), [R("ut")], [])])
+    for h, q in ((0, "s"), (1, "a")):
+        dma("d_x%d" % h, [(q, lambda e, h=h: e.dma_start(T.xt0[:, 640 * h:640 * h + 640], T.x[:, 640 * h:640 * h + 640]), [R("xt0", 640 * h, 640 * h + 640)], [])])
+    dma("d_w", [("s", lambda e: e.dma_start(T.wq[:, 0:512].bitcast(dt.uint8), T.wc[:, 0:2048]), [R("wq")], []),
+                ("s", lambda e: e.dma_start(T.wsp[:, 0:512], T.ws[:, 0:512]), [R("wsp")], [])])
+    dma("d_v", [("s", lambda e: e.dma_start(T.vt[:], T.v[:]), [R("vt")], [])])
+
+    iota(R("pi"), [[0, 20]], 0, 1)
+    iota(R("qi"), [[16, 20]], 0, 0)
+    iota(R("ui"), [[1, 3], [16, 8]], -16, 0)
+    iota(R("jmp"), [[1, 16]], 128, -1)
+    iota(R("icf"), [[1, 320]], -160, 0, True)
+    op("v", lambda: g.vector.memset(T.rz[:], 1.0), [R("rz")], [])
+    op("v", lambda: g.vector.memset(T.rz[:, 0:320:16], 0.0), [("rz", 0, 320, 16)], [])
+    ts(R("pa"), R("pi"), 15, OP.bitwise_and)
+    tt(R("cw"), R("pa"), R("qi"), OP.add)
+    ts(R("ccw"), R("cw"), -160.0, OP.add)
+    ts(R("ua"), R("ui"), 127, OP.bitwise_and)
+    cp(R("uo"), R("ua"))
+    ts(R("jma"), R("jmp"), 15, OP.bitwise_and)
+    ts(R("mk", 0, 16), R("jma"), 0.0, OP.is_equal)
+    for a, b in ((16, 32), (32, 64), (64, 128), (128, 256), (256, 320)): cp(R("mk", a, b), R("mk", 0, b - a))
+    nI = R("nli")
+    nW, par = new("lst"), new("ist")
+    cp(nW, nI)
+    ts(par, nI, 1, OP.bitwise_and)
+    def other(nI, par):
+        a, b, o = new("ist"), new("ist"), new("lst")
+        ts(a, par, -2.0, OP.mult, 1.0, OP.add)
+        tt(b, nI, a, OP.add)
+        cp(o, b)
+        return o
+    nxW = other(nI, par)
+    NF, XF, SG = [R("nf0"), R("nf1")], [R("xf0"), R("xf1")], [R("sg0"), R("sg1")]
+    ga(NF[0], R("icf"), nW)
+    op("v", lambda: g.vector.tensor_copy(ap(XF[0]).indirect(ap(nxW)), ap(R("icf"))), [XF[0]], [nxW, R("icf")])
+    at = [0]
+    def publish(xf, nW, par):
+        pub, c = "pub%d" % at[0], R("cw")
+        at[0] ^= 1
+        v = pick(xf, nW)
+        dmc, h, t = R(pub, 0, 20), R(pub, 20, 40), new("fs")
+        tt(dmc, v, R("ccw"), OP.subtract)
+        tt(t, par, dmc, OP.mult)
+        tt(h, t, c, OP.add)
+        dma("d_sh", [("s", lambda e: e.dma_start(T.shl[16:128, :], T[pub][0:112, :]), [R("shl")], [R(pub)]),
+                     ("s", lambda e: e.dma_start(T.shl[0:16, :], T[pub][112:128, :]), [R("shl")], [R(pub)])])
+    publish(XF[0], nW, par)
+    quant(R("qu"), R("qus"), R("ut"))
+    op("v", lambda: g.vector.tensor_copy(T.uv[:, 0:384].bitcast(dt.uint32), T.qu[:, 0:128].bitcast(dt.uint32).indirect(T.uo[:, 0:24])), [R("uv")], [R("qu"), R("uo")])
+    op("a", lambda: g.scalar.activation(T.uvs[:, 0:384], T.qus[:, 0:128].indirect(T.uo[:, 0:24]), AF.Copy), [R("uvs")], [R("qus"), R("uo")])
+
+    def bank(half, b): return R("p%d" % (4 * half + b), 0, 160)
+    def scores(k, half):
+        c = 160 * half
+        q, s = R("xq%d" % k, c, c + 160), R("xs%d" % k, c, c + 160)
+        quant(q, s, R("xt%d" % k, 4 * c, 4 * c + 640))
+        if k < 3:
+            for j in range(3):
+                mm(bank(half, j), R("uv", 128 * j, 128 * j + 128), R("uvs", 128 * j, 128 * j + 128), q, s)
+    def signs(half, j):
+        f = R("fw", 320 * j + 160 * half, 320 * j + 160 * half + 160)
+        op("a", lambda: g.scalar.activation(ap(f), ap(bank(half, j)), AF.Sign), [f], [bank(half, j)])
+        op("a", lambda: g.scalar.activation(ap(f), ap(f), AF.Relu), [f], [f])
+    def flags(half, j):
+        ts(R("fw", 320 * j + 160 * half, 320 * j + 160 * half + 160), bank(half, j), 0.0, OP.is_gt)
+    def halves(k):
+        act(R("xg"), R("xt%d" % k), 0.5)
+        for b in range(4): act(R("xh", 320 * b, 320 * b + 320), (("xt%d" % k), b, 1280, 4), 0.5)
+
+    scores(0, 0)
+    scores(0, 1)
+    tt(R("mo%d" % turn[0]), XF[0], R("mk"), OP.mult)
+    ixW = wrapped(scan(320))
+    for h in (0, 1): flags(h, 0)
+    cur = [0]
+    for k, s in enumerate(STEP):
+        src, dst = T.cores[(rank - s) % N], T.cores[(rank + s) % N]
+        rn, ri, rd = "rn%d" % k, "ri%d" % k, "rd%d" % k
+        for j in range(3):
+            last = j == 2
+            nf, xf, sg = NF[cur[0]], XF[cur[0]], SG[cur[0]]
+            cur[0] ^= 1
+            nf2, xf2 = NF[cur[0]], XF[cur[0]]
+            h, t, u, sW = new("lst"), new("fs"), new("fs"), new("lst")
+            cp(h, R("shl", 20, 40))
+            v = pick(R("fw", 320 * j, 320 * j + 320), h)
+            tt(t, v, R("shl", 0, 20), OP.mult)
+            tt(u, t, R("cw"), OP.add)
+            cp(sW, u)
+            ga(sg, R("icf"), sW)
+            ga(xf2, sg, ixW)
+            if j == 0:
+                for hh, jj in ((0, 1), (0, 2)) if k else ((0, 1), (1, 1), (0, 2), (1, 2)): signs(hh, jj)
+            v = pick(nf, sW)
+            nW = wrapped(v)
+            if last: send(src, T["ln%d" % k][:, 0:10], ap(part(nW, 0, 10)), rn, part(nW, 0, 10))
+            if not last:
+                nI, par = new("ist"), new("ist")
+                ts(nI, v, 160.0, OP.add)
+                ts(par, nI, 1, OP.bitwise_and)
+                publish(xf2, nW, par)
+                ixW = wrapped(pick(sg, ixW))
+                if j == 0:
+                    halves(k)
+                    if k == 0:
+                        op("v", lambda: g.vector.memset(T.et[:], 1.0), [R("et")], [])
+                        ts(R("yt0"), R("xt0"), 32.0, OP.mult)
+                        op("g", lambda: g.affine_select(T.et[:, 0:512], T.et[:, 0:512], [[1, 512]], OP.is_equal, 0.0, 0, -4), [R("et", 0, 512)], [R("et", 0, 512)])
+                        for b in range(1, 4):
+                            op("g", lambda b=b: g.affine_select(T.et[:, 512 * b:512 * b + 512], T.et[:, 512 * b:512 * b + 512], [[1, 512]], OP.is_equal, 0.0, -b, -4), [R("et", 512 * b, 512 * b + 512)], [R("et", 512 * b, 512 * b + 512)])
+                if j == 1 and k == 0: quant(R("eq"), R("es"), R("et"))
+                ga(nf2, nf, sW)
+            else:
+                nI, par = new("ist"), new("ist")
+                ixW = wrapped(pick(sg, ixW))
+                send(dst, T["li%d" % k][:, 0:20], ap(ixW), ri, ixW)
+                ga(nf2, nf, sW)
+                ts(nI, v, 160.0, OP.add)
+        for b in range(4):
+            w = R("xh", 320 * b, 320 * b + 320)
+            gt(R("zn", 320 * b, 320 * b + 320), w, ixW, ("xg", b, 1280, 4), OP.add)
+        arrives(rn, ENG, [R("ln%d" % k)])
+        for b in range(4):
+            (gv if b < 2 else ga)(("ft", b, 640, 4), R("zn", 320 * b, 320 * b + 320), R("ln%d" % k))
+        fq, fp = R("fq%d" % k), R("fp%d" % k)
+        quant(fq, fp, R("ft"))
+        send(dst, T["lq%d" % k][:, 0:160].bitcast(dt.uint8), ap(fq).bitcast(dt.uint8), rd, fq)
+        send(dst, T["lp%d" % k][:, 0:160], ap(fp), rd, fp)
+        ts(par, nI, 1, OP.bitwise_and)
+        nxW = other(nI, par)
+        arrives(ri, ENG, [R("li%d" % k)])
+        ga(R("gf"), nf2, R("li%d" % k))
+        kW = wrapped(pick(R("gf"), part(nxW, 10, 20), 160), 10)
+        for b in range(4):
+            ga(("vo", b, 640, 4), R("zn", 320 * b, 320 * b + 320), kW)
+        if k < 2: publish(xf2, nW, par)
+        def layer(half, tile):
+            c = 160 * half
+            q, p = R("vq%d" % k, c, c + 160), R("vp%d" % k, c, c + 160)
+            quant(q, p, R(tile))
+            for b in range(4): mm(bank(half, b), R("wq", 128 * b, 128 * b + 128), R("wsp", 128 * b, 128 * b + 128), q, p)
+            for b in range(4): tt(("yt%d" % (k + 1), 4 * c + b, 4 * c + 640, 4), bank(half, b), ("yt%d" % k, 4 * c + b, 4 * c + 640, 4), OP.add)
+            ts(R("xt%d" % (k + 1), 4 * c, 4 * c + 640), R("yt%d" % (k + 1), 4 * c, 4 * c + 640), 0.03125, OP.mult)
+            scores(k + 1, half)
+            if k < 2:
+                flags(half, 0)
+            else: out(half)
+        def out(half):
+            c = 160 * half
+            q, p = R("xq3", c, c + 160), R("xs3", c, c + 160)
+            mm(bank(half, 0), R("qv"), R("qvs"), q, p)
+            dma("d_os", [("s", lambda e: e.dma_start(T.oc[:, 4 * c:4 * c + 640], ap(q).bitcast(dt.uint8)), [], [q])] +
+                [("s", lambda e, i=i: e.dma_start(T.osc[4 * i:4 * i + 4, c:c + 160], T.xs3[32 * i:32 * i + 4, c:c + 160]), [], [p]) for i in range(4)])
+            y = R("yo", c, c + 160)
+            act(y, bank(half, 0))
+            dma("d_os", [("a", lambda e: e.dma_start(T.y[:, c:c + 160], ap(y)), [], [y])])
+        if k == 2:
+            quant(R("qv"), R("qvs"), R("vt"))
+            ts(R("nmf"), nf2, 160.0, OP.add)
+            dma("d_os", [("s", lambda e: e.dma_start(T.nm[:], T.nmf[0:128:16, :]), [], [R("nmf")])])
+        layer(1, "vo")
+        arrives(rd, 2 * ENG, [R("lq%d" % k), R("lp%d" % k)])
+        for b in range(4): mm(bank(0, b), R("eq", 128 * b, 128 * b + 128), R("es", 128 * b, 128 * b + 128), R("lq%d" % k), R("lp%d" % k))
+        for b in (0, 2, 1, 3): (cp if b % 2 else act)(("vf", b, 640, 4), bank(0, b))
+        if k < 2:
+            for jj in (1, 2): signs(1, jj)
+        layer(0, "vf")
+    for q, sem in QSEM.items(): total[sem] = count[q]
+    for sem, val in total.items(): g.wait_ge(T.sem[sem], val)

@@ -3,23 +3,21 @@ from concourse.bass import DstId, RemoteDMATransfer
 from concourse.mybir import dt, AluOpType as OP, AxisListType, ActivationFunctionType as AF
 
 STEP = [1, 2, 4]
-BF, F32, I32, U16, U8, CODE = "bfloat16", "float32", "int32", "uint16", "uint8", "float8_e4m3fn_x4"
+BF, F16, F32, I32, U16, U8, CODE = "bfloat16", "float16", "float32", "int32", "uint16", "uint8", "float8_e4m3fn_x4"
+ROT = [(17 * j - 48) % 128 for j in range(3)]
 SCRATCH = {
-    "nli": ("sbuf", [128, 20], I32), "ut": ("sbuf", [128, 512], BF), "vt": ("sbuf", [128, 512], BF),
-    "qu": ("sbuf", [128, 128], CODE), "qus": ("sbuf", [128, 128], U8), "qv": ("sbuf", [128, 128], CODE), "qvs": ("sbuf", [128, 128], U8),
-    "uv": ("sbuf", [128, 384], CODE), "uvs": ("sbuf", [128, 384], U8), "wq": ("sbuf", [128, 512], CODE), "wsp": ("sbuf", [128, 512], U8),
-    "et": ("sbuf", [128, 2048], BF), "eq": ("sbuf", [128, 512], CODE), "es": ("sbuf", [128, 512], U8),
-    "jmp": ("sbuf", [128, 16], I32), "jma": ("sbuf", [128, 16], I32),
-    "mk": ("sbuf", [128, 320], BF), "rz": ("sbuf", [128, 320], BF), "icf": ("sbuf", [128, 320], BF),
-    "pi": ("sbuf", [128, 20], I32), "pa": ("sbuf", [128, 20], I32), "qi": ("sbuf", [128, 20], I32), "cw": ("sbuf", [128, 20], F32), "ccw": ("sbuf", [128, 20], F32),
-    "ui": ("sbuf", [128, 24], I32), "ua": ("sbuf", [128, 24], I32), "uo": ("sbuf", [128, 24], U16),
-    "fw": ("sbuf", [128, 960], BF), "sg0": ("sbuf", [128, 320], BF), "sg1": ("sbuf", [128, 320], BF), "gf": ("sbuf", [128, 320], BF),
-    "nf0": ("sbuf", [128, 320], BF), "nf1": ("sbuf", [128, 320], BF), "xf0": ("sbuf", [128, 320], BF), "xf1": ("sbuf", [128, 320], BF),
-    "mo0": ("sbuf", [128, 320], BF), "mo1": ("sbuf", [128, 320], BF), "so0": ("sbuf", [128, 320], BF), "so1": ("sbuf", [128, 320], BF),
-    "lst": ("sbuf", [128, 1600], U16), "fs": ("sbuf", [128, 1600], F32), "ist": ("sbuf", [128, 1600], I32),
-    "pub0": ("sbuf", [128, 40], F32), "pub1": ("sbuf", [128, 40], F32), "shl": ("sbuf", [128, 40], F32),
+    "nls": ("sbuf", [128, 20], I32), "nlt": ("sbuf", [128, 20], I32), "ut": ("sbuf", [128, 648], BF), "vt": ("sbuf", [128, 512], BF),
+    "qu": ("sbuf", [128, 162], CODE), "qus": ("sbuf", [128, 162], U8), "qo": ("sbuf", [128, 128], CODE), "qos": ("sbuf", [128, 128], U8),
+    "qv": ("sbuf", [128, 128], CODE), "qvs": ("sbuf", [128, 128], U8), "wq": ("sbuf", [128, 512], CODE), "wsp": ("sbuf", [128, 512], U8),
+    "et": ("sbuf", [128, 528], BF), "eq": ("sbuf", [128, 512], CODE), "es": ("sbuf", [128, 512], U8),
+    "icf": ("sbuf", [128, 320], BF), "icx": ("sbuf", [128, 320], BF), "ci": ("sbuf", [128, 32], I32), "co": ("sbuf", [128, 8], U16),
+    "fw": ("sbuf", [128, 960], BF), "aa": ("sbuf", [128, 368], BF), "ah": ("sbuf", [128, 368], BF), "em": ("sbuf", [128, 160], F16), "dl": ("sbuf", [128, 160], F16),
+    "val": ("sbuf", [128, 320], BF), "bs": ("sbuf", [128, 352], BF), "bn": ("sbuf", [128, 352], BF), "bx": ("sbuf", [128, 352], BF), "bk": ("sbuf", [128, 192], BF),
+    "us": ("sbuf", [128, 672], BF), "un": ("sbuf", [128, 704], BF), "ua": ("sbuf", [128, 704], BF), "ux": ("sbuf", [128, 672], BF), "uk": ("sbuf", [128, 352], BF),
+    "nt": ("sbuf", [128, 320], BF), "it": ("sbuf", [128, 20], U16), "ns": ("sbuf", [128, 20], U16), "ow": ("sbuf", [128, 20], U16), "gf": ("sbuf", [128, 320], BF),
+    "lst": ("sbuf", [128, 1600], U16),
     "xh": ("sbuf", [128, 1280], BF), "xg": ("sbuf", [128, 1280], BF), "zn": ("sbuf", [128, 1280], BF), "ft": ("sbuf", [128, 640], BF), "vo": ("sbuf", [128, 640], BF), "vf": ("sbuf", [128, 640], BF),
-    "yo": ("sbuf", [128, 320], F32), "nmf": ("sbuf", [128, 320], F32),
+    "zt": ("sbuf", [128, 640], BF), "yo": ("sbuf", [128, 320], F32), "nmf": ("sbuf", [128, 320], F32),
 }
 for _k in range(4):
     SCRATCH.update({"xt%d" % _k: ("sbuf", [128, 1280], BF), "yt%d" % _k: ("sbuf", [128, 1280], BF), "xq%d" % _k: ("sbuf", [128, 320], CODE), "xs%d" % _k: ("sbuf", [128, 320], U8)})
@@ -29,7 +27,7 @@ for _k in range(3):
 for _k in range(8):
     SCRATCH["p%d" % _k] = ("psum", [128, 512], F32)
 QSEM = {"v": "qv_", "a": "qa_", "t": "qt_", "g": "qg_"}
-SEMAPHORES = list(QSEM.values()) + ["d_nl", "d_u", "d_x0", "d_x1", "d_w", "d_v", "d_sh", "d_os", "sent"] + ["r%s%d" % (a, k) for a in "nid" for k in range(3)]
+SEMAPHORES = list(QSEM.values()) + ["d_ns", "d_nt", "d_u", "d_x0", "d_x1", "d_w", "d_v", "d_c", "d_q", "d_i", "d_n", "d_s", "d_a", "d_os", "sent"] + ["r%s%d" % (a, k) for a in "nid" for k in range(3)]
 
 
 def rank_program(g, core, T, topo):
@@ -49,7 +47,7 @@ def rank_program(g, core, T, topo):
                 ps = SCRATCH.get(r[0], ("x",))[0] == "psum"
                 for (lo, hi, w, sem, val, clk, st) in log.get(r[0], []):
                     if not ps and (hi <= r[1] or lo >= r[2]): continue
-                    if not ps and st == r[3] > 2 and (lo - r[1]) % st: continue
+                    if not ps and st == r[3] > 1 and (lo - r[1]) % st: continue
                     if not (w or wr or ps): continue
                     if sem == own and not w: continue
                     deps.append((sem, val, clk))
@@ -87,7 +85,7 @@ def rank_program(g, core, T, topo):
         for q, fn, writes, reads in moves:
             note(reads, False, sem, total[sem], clk)
         for q, fn, writes, reads in moves:
-            note([(r[0], r[1], r[2], 2) for r in writes], True, sem, total[sem], clk)
+            note(writes, True, sem, total[sem], clk)
 
     def arrives(sem, val, regions):
         total[sem] = val
@@ -96,7 +94,7 @@ def rank_program(g, core, T, topo):
     def send(dst, out, inn, sem, region):
         need("g", [region], [])
         rid, pid, _ = topo.addr(dst)
-        es = topo.engines(core, dst)[:8]
+        es = topo.engines(core, dst)[:ENG]
         g.remote_dma(out, inn, T.sem[sem], T.sem["sent"], pid, rid, sum(1 << e for e in es))
         total["sent"] = total.get("sent", 0) + len(es)
 
@@ -104,8 +102,8 @@ def rank_program(g, core, T, topo):
 
     def R(name, lo=0, hi=None, st=1): return (name, lo, SCRATCH[name][1][1] if hi is None else hi, st)
     def ap(r): return T[r[0]][:, r[1]:r[2]:r[3]] if r[3] != 1 else T[r[0]][:, r[1]:r[2]]
-    slots = {"lst": 0, "fs": 0, "ist": 0}
-    def new(name, n=20):
+    slots = {"lst": 0, "ci": 0}
+    def new(name, n):
         a = slots[name]
         slots[name] += n
         return R(name, a, a + n)
@@ -119,148 +117,165 @@ def rank_program(g, core, T, topo):
     def gv(out, win, off): op("v", lambda: g.vector.tensor_copy(ap(out), ap(win).indirect(ap(off))), [out], [win, off])
     def ga(out, win, off): op("a", lambda: g.scalar.activation(ap(out), ap(win).indirect(ap(off)), AF.Copy), [out], [win, off])
     def gt(out, win, off, b, o): op("v", lambda: g.vector.tensor_tensor(ap(out), ap(win).indirect(ap(off)), ap(b), o), [out], [win, off, b])
-    def act(out, a, scale=1.0): op("a", lambda: g.scalar.activation(ap(out), ap(a), AF.Copy, scale=scale), [out], [a])
+    def act(out, a, scale=1.0, f=AF.Copy): op("a", lambda: g.scalar.activation(ap(out), ap(a), f, scale=scale), [out], [a])
+    def fill(out, c): op("v", lambda: g.vector.memset(ap(out), c), [out], [])
     def quant(q, s, a): op("v", lambda: g.vector.quantize_mx(ap(q), ap(s), ap(a)), [q, s], [a])
     def mm(out, l, ls, r, rs): op("t", lambda: g.tensor.matmul_mx(ap(out), ap(l), ap(ls), ap(r), ap(rs), True, True), [out], [l, ls, r, rs])
     def iota(out, pattern, base, cm, flag=False):
         op("g", lambda: g.iota(ap(out), pattern, base, cm, allow_small_or_imprecise_dtypes=True) if flag else g.iota(ap(out), pattern, base, cm), [out], [])
-    turn = [0]
-    def scan(n):
-        m, s = R("mo%d" % turn[0], 0, n), R("so%d" % turn[0], 0, n)
-        op("v", lambda: g.vector.tensor_tensor_scan(ap(s), T["rz"][:, 0:n], ap(m), 0.0, OP.mult, OP.add), [s], [m, R("rz", 0, n)])
-        turn[0] ^= 1
-        return (s[0], 15, n, 16)
-    def pick(win, off, n=320):
-        gt(R("mo%d" % turn[0], 0, n), win, off, R("mk", 0, n), OP.mult)
-        return scan(n)
-    def wrapped(v, n=20):
+    def turn(u, uo, b, bo, n):
+        for o, i in ((R(u, uo, uo + n), R(b, bo + 16, bo + 16 + n)), (R(u, uo + n, uo + 2 * n + 32), R(b, bo, bo + n + 32))):
+            op("v", lambda: g.vector.transpose(ap(o), ap(i)), [o], [i])
+    FULL, TWO, HALF, HALF8 = R("co", 0, 2), R("co", 2, 4), R("co", 4, 5), R("co", 6, 7)
+    def pick(win, c):
+        n = 16 * (c[2] - c[1])
         o = new("lst", n)
-        ts(o, v, 160.0, OP.add)
-        return o
+        op("v", lambda: g.vector.tensor_scalar(ap(o), ap(win).indirect(ap(c)), 160.0, None, OP.add), [o], [win, c])
+        return part(o, 0, 10 * (c[2] - c[1]))
+    def roll(sem, moves, q="s"):
+        ms = []
+        for o, i, up, st in moves:
+            d = 16 * (up % 8)
+            for a, b, c in ((d, 128, 0), (0, d, 128 - d)):
+                ms.append((q, lambda e, o=o, i=i, a=a, b=b, c=c, st=st: e.dma_start(T[o[0]][a:b:st, o[1]:o[2]], T[i[0]][c:c + b - a:st, i[1]:i[2]]), [o], [i]))
+        dma(sem, ms)
 
-    dma("d_nl", [("s", lambda e: e.dma_start(T.nli[:], T.nl[:]), [R("nli")], [])])
-    dma("d_u", [("a", lambda e: e.dma_start(T.ut[:], T.u[:]), [R("ut")], [])])
+    def rows(sem, q, out, up):
+        d = 16 * up
+        dma(sem, [(q, lambda e: e.dma_start(T[out][d:128, :], T.nl[0:128 - d, :]), [R(out)], []), (q, lambda e: e.dma_start(T[out][0:d, :], T.nl[128 - d:128, :]), [R(out)], [])])
+    rows("d_ns", "s", "nls", 3)
+    r0 = 4 * ROT[0]
+    dma("d_u", [("a", lambda e: e.dma_start(T.ut[:, 0:512 - r0], T.u[:, r0:512]), [R("ut")], []), ("a", lambda e: e.dma_start(T.ut[:, 512 - r0:648], T.u[:, 0:136 + r0]), [R("ut")], [])])
     for h, q in ((0, "s"), (1, "a")):
         dma("d_x%d" % h, [(q, lambda e, h=h: e.dma_start(T.xt0[:, 640 * h:640 * h + 640], T.x[:, 640 * h:640 * h + 640]), [R("xt0", 640 * h, 640 * h + 640)], [])])
+    rows("d_nt", "s", "nlt", 2)
+
+    p, t, q, h, a, s, m = [new("ci", 2) for _ in range(7)]
+    iota(p, [[0, 2]], 0, 1)
+    iota(t, [[256, 2]], 0, 0)
+    iota(R("icf"), [[1, 320]], -160, 0, True)
+    iota(R("icx"), [[2, 160], [-1, 2]], -159, 0, True)
+    dma("d_c", [("s", lambda e: e.dma_start(T.icx[0:128:16, :], T.icf[0:128:16, :]), [R("icx")], [R("icf")])])
+    ts(q, p, 15, OP.bitwise_and)
+    ts(h, p, 4, OP.arith_shift_right)
+    for b in ("aa", "ah", "bx"): fill(R(b), 0.0)
+    ts(q2 := new("ci", 2), q, 16.0, OP.mult)
+    tt(a, p, h, OP.add)
+    for b in ("bs", "bn"): fill(R(b), 0.0)
+    tt(m, q2, t, OP.add)
+    ts(s, a, 1, OP.bitwise_and)
+    for b in ("bk", "nt"): fill(R(b), 0.0)
+    s1, s2, ge, f1, f2, f3 = [new("ci", 2) for _ in range(6)]
+    ts(ge, m, 160.0, OP.is_ge, 192.0, OP.mult)
+    ts(s1, s, 336.0, OP.mult)
+    ts(s2, s, 176.0, OP.mult)
+    fill(R("et"), 1.0)
+    tt(f1, m, s1, OP.add)
+    tt(f2, m, s2, OP.add)
+    ts(FULL, f1, 671.0, OP.min)
+    tt(f3, f2, ge, OP.add)
+    ts(HALF, part(f2, 0, 1), 351.0, OP.min)
+    ts(HALF8, part(f2, 0, 1), 8.0, OP.add, 351.0, OP.min)
+    ts(TWO, f3, 703.0, OP.min)
+    op("g", lambda: g.affine_select(T.et[:], T.et[:], [[1, 528]], OP.is_equal, 0.0, -3, -4), [R("et")], [R("et")])
+
+    E, O = R("aa", 16, 176), R("aa", 192, 352)
+    def split(b, src, first):
+        cp(R(b, 16 + 176 * first, 176 + 176 * first), (src, 16, 336, 2))
+        cp(R(b, 192 - 176 * first, 352 - 176 * first), (src, 17, 336, 2))
+        turn("ua", 352, b, 176, 160)
+        turn("ua", 0, b, 0, 160)
+    nW, nT = new("lst", 20), new("lst", 20)
+    cp(nW, R("nls"))
+    op("v", lambda: g.vector.tensor_copy(T.bx[:, 16:336].indirect(ap(nW)), ap(R("icf"))), [R("bx", 16, 336)], [nW, R("icf")])
+    split("aa", "bx", 1)
+    tt(R("em"), E, O, OP.subtract)
+    iW = pick(R("ua"), TWO)
+    roll("d_i", [(R("it"), iW, -1, 1)])
+    quant(R("qu"), R("qus"), R("ut"))
+    o1 = ROT[1] - ROT[0]
+    dma("d_q", [("s", lambda e: e.dma_start(T.qo[:, 0:128].bitcast(dt.uint8), T.qu[:, o1:o1 + 128].bitcast(dt.uint8)), [R("qo")], [R("qu")]),
+                ("s", lambda e: e.dma_start(T.qos[:, 0:128], T.qus[:, o1:o1 + 128]), [R("qos")], [R("qus")])])
+    cp(nT, R("nlt"))
+    ga(R("nt"), R("icx"), nT)
+    oW = part(iW, 10, 20)
     dma("d_w", [("s", lambda e: e.dma_start(T.wq[:, 0:512].bitcast(dt.uint8), T.wc[:, 0:2048]), [R("wq")], []),
                 ("s", lambda e: e.dma_start(T.wsp[:, 0:512], T.ws[:, 0:512]), [R("wsp")], [])])
     dma("d_v", [("s", lambda e: e.dma_start(T.vt[:], T.v[:]), [R("vt")], [])])
 
-    iota(R("pi"), [[0, 20]], 0, 1)
-    iota(R("qi"), [[16, 20]], 0, 0)
-    iota(R("ui"), [[1, 3], [16, 8]], -16, 0)
-    iota(R("jmp"), [[1, 16]], 128, -1)
-    iota(R("icf"), [[1, 320]], -160, 0, True)
-    op("v", lambda: g.vector.memset(T.rz[:], 1.0), [R("rz")], [])
-    op("v", lambda: g.vector.memset(T.rz[:, 0:320:16], 0.0), [("rz", 0, 320, 16)], [])
-    ts(R("pa"), R("pi"), 15, OP.bitwise_and)
-    tt(R("cw"), R("pa"), R("qi"), OP.add)
-    ts(R("ccw"), R("cw"), -160.0, OP.add)
-    ts(R("ua"), R("ui"), 127, OP.bitwise_and)
-    cp(R("uo"), R("ua"))
-    ts(R("jma"), R("jmp"), 15, OP.bitwise_and)
-    ts(R("mk", 0, 16), R("jma"), 0.0, OP.is_equal)
-    for a, b in ((16, 32), (32, 64), (64, 128), (128, 256), (256, 320)): cp(R("mk", a, b), R("mk", 0, b - a))
-    nI = R("nli")
-    nW, par = new("lst"), new("ist")
-    cp(nW, nI)
-    ts(par, nI, 1, OP.bitwise_and)
-    def other(nI, par):
-        a, b, o = new("ist"), new("ist"), new("lst")
-        ts(a, par, -2.0, OP.mult, 1.0, OP.add)
-        tt(b, nI, a, OP.add)
-        cp(o, b)
-        return o
-    nxW = other(nI, par)
-    NF, XF, SG = [R("nf0"), R("nf1")], [R("xf0"), R("xf1")], [R("sg0"), R("sg1")]
-    ga(NF[0], R("icf"), nW)
-    op("v", lambda: g.vector.tensor_copy(ap(XF[0]).indirect(ap(nxW)), ap(R("icf"))), [XF[0]], [nxW, R("icf")])
-    at = [0]
-    def publish(xf, nW, par):
-        pub, c = "pub%d" % at[0], R("cw")
-        at[0] ^= 1
-        v = pick(xf, nW)
-        dmc, h, t = R(pub, 0, 20), R(pub, 20, 40), new("fs")
-        tt(dmc, v, R("ccw"), OP.subtract)
-        tt(t, par, dmc, OP.mult)
-        tt(h, t, c, OP.add)
-        dma("d_sh", [("s", lambda e: e.dma_start(T.shl[16:128, :], T[pub][0:112, :]), [R("shl")], [R(pub)]),
-                     ("s", lambda e: e.dma_start(T.shl[0:16, :], T[pub][112:128, :]), [R("shl")], [R(pub)])])
-    publish(XF[0], nW, par)
-    quant(R("qu"), R("qus"), R("ut"))
-    op("v", lambda: g.vector.tensor_copy(T.uv[:, 0:384].bitcast(dt.uint32), T.qu[:, 0:128].bitcast(dt.uint32).indirect(T.uo[:, 0:24])), [R("uv")], [R("qu"), R("uo")])
-    op("a", lambda: g.scalar.activation(T.uvs[:, 0:384], T.qus[:, 0:128].indirect(T.uo[:, 0:24]), AF.Copy), [R("uvs")], [R("qus"), R("uo")])
-
+    o2 = ROT[2] - ROT[0]
+    US = [(R("qu", 0, 128), R("qus", 0, 128)), (R("qo"), R("qos")), (R("qu", o2, o2 + 128), R("qus", o2, o2 + 128))]
     def bank(half, b): return R("p%d" % (4 * half + b), 0, 160)
-    def scores(k, half):
+    def scores(k, half, js):
         c = 160 * half
         q, s = R("xq%d" % k, c, c + 160), R("xs%d" % k, c, c + 160)
-        quant(q, s, R("xt%d" % k, 4 * c, 4 * c + 640))
+        if 0 in js or k == 3: quant(q, s, R("xt%d" % k, 4 * c, 4 * c + 640))
         if k < 3:
-            for j in range(3):
-                mm(bank(half, j), R("uv", 128 * j, 128 * j + 128), R("uvs", 128 * j, 128 * j + 128), q, s)
+            for j in js: mm(bank(half, j), US[j][0], US[j][1], q, s)
+    def fl(half, j): return R("fw", 320 * j + 160 * half, 320 * j + 160 * half + 160)
     def signs(half, j):
-        f = R("fw", 320 * j + 160 * half, 320 * j + 160 * half + 160)
-        op("a", lambda: g.scalar.activation(ap(f), ap(bank(half, j)), AF.Sign), [f], [bank(half, j)])
-        op("a", lambda: g.scalar.activation(ap(f), ap(f), AF.Relu), [f], [f])
-    def flags(half, j):
-        ts(R("fw", 320 * j + 160 * half, 320 * j + 160 * half + 160), bank(half, j), 0.0, OP.is_gt)
-    def halves(k):
-        act(R("xg"), R("xt%d" % k), 0.5)
-        for b in range(4): act(R("xh", 320 * b, 320 * b + 320), (("xt%d" % k), b, 1280, 4), 0.5)
+        act(fl(half, j), bank(half, j), f=AF.Sign)
+        act(fl(half, j), fl(half, j), f=AF.Relu)
+    def flags(half, j): ts(fl(half, j), bank(half, j), 0.0, OP.is_gt)
+    def halves(k, half, what):
+        c = 160 * half
+        if "g" in what: act(R("xg", 4 * c, 4 * c + 640), R("xt%d" % k, 4 * c, 4 * c + 640), 0.5)
+        if "h" in what:
+            for b in range(4): act(R("xh", 320 * b + c, 320 * b + c + 160), (("xt%d" % k), 4 * c + b, 4 * c + 640, 4), 0.5)
 
-    scores(0, 0)
-    scores(0, 1)
-    tt(R("mo%d" % turn[0]), XF[0], R("mk"), OP.mult)
-    ixW = wrapped(scan(320))
+    scores(0, 0, [0])
+    scores(0, 1, [0])
     for h in (0, 1): flags(h, 0)
-    cur = [0]
+    for h in (0, 1): scores(0, h, [2, 1])
+    SG, NF = R("bs", 16, 336), R("bn", 16, 336)
     for k, s in enumerate(STEP):
         src, dst = T.cores[(rank - s) % N], T.cores[(rank + s) % N]
         rn, ri, rd = "rn%d" % k, "ri%d" % k, "rd%d" % k
         for j in range(3):
-            last = j == 2
-            nf, xf, sg = NF[cur[0]], XF[cur[0]], SG[cur[0]]
-            cur[0] ^= 1
-            nf2, xf2 = NF[cur[0]], XF[cur[0]]
-            h, t, u, sW = new("lst"), new("fs"), new("fs"), new("lst")
-            cp(h, R("shl", 20, 40))
-            v = pick(R("fw", 320 * j, 320 * j + 320), h)
-            tt(t, v, R("shl", 0, 20), OP.mult)
-            tt(u, t, R("cw"), OP.add)
-            cp(sW, u)
-            ga(sg, R("icf"), sW)
-            ga(xf2, sg, ixW)
-            if j == 0:
-                for hh, jj in ((0, 1), (0, 2)) if k else ((0, 1), (1, 1), (0, 2), (1, 2)): signs(hh, jj)
-            v = pick(nf, sW)
-            nW = wrapped(v)
-            if last: send(src, T["ln%d" % k][:, 0:10], ap(part(nW, 0, 10)), rn, part(nW, 0, 10))
-            if not last:
-                nI, par = new("ist"), new("ist")
-                ts(nI, v, 160.0, OP.add)
-                ts(par, nI, 1, OP.bitwise_and)
-                publish(xf2, nW, par)
-                ixW = wrapped(pick(sg, ixW))
+            gt(R("dl"), R("fw", 320 * j, 320 * j + 320), oW, R("em"), OP.mult)
+            if j: turn("un", 0, "bn", 0, 320)
+            tt(("val", 0, 320, 2), O, R("dl"), OP.add)
+            tt(("val", 1, 320, 2), E, R("dl"), OP.subtract)
+            if j: nW = pick(R("un", 0, 672), FULL)
+            ga(part(SG, 160, 320), R("val"), part(nW, 10, 20))
+            gv(part(SG, 0, 160), R("val"), part(nW, 0, 10))
+            if j < 2:
+                ga(O, SG, R("it", 10, 20))
+                ga(E, SG, R("it", 0, 10))
+                turn("us", 0, "bs", 0, 320)
+                if j == 0 and k == 0: flags(0, 1)
+                sW = pick(R("us"), FULL)
+                turn("ua", 352, "aa", 176, 160)
+                ga(NF, R("nt"), sW)
+                turn("ua", 0, "aa", 0, 160)
+                tt(R("em"), E, O, OP.subtract)
+                iW = pick(R("ua"), TWO)
+                oW = part(iW, 10, 20)
+                roll("d_i", [(R("it"), iW, -1, 1)])
+                roll("d_n", [(R("nt"), NF, -1, 8)])
                 if j == 0:
-                    halves(k)
-                    if k == 0:
-                        op("v", lambda: g.vector.memset(T.et[:], 1.0), [R("et")], [])
-                        ts(R("yt0"), R("xt0"), 32.0, OP.mult)
-                        op("g", lambda: g.affine_select(T.et[:, 0:512], T.et[:, 0:512], [[1, 512]], OP.is_equal, 0.0, 0, -4), [R("et", 0, 512)], [R("et", 0, 512)])
-                        for b in range(1, 4):
-                            op("g", lambda b=b: g.affine_select(T.et[:, 512 * b:512 * b + 512], T.et[:, 512 * b:512 * b + 512], [[1, 512]], OP.is_equal, 0.0, -b, -4), [R("et", 512 * b, 512 * b + 512)], [R("et", 512 * b, 512 * b + 512)])
-                if j == 1 and k == 0: quant(R("eq"), R("es"), R("et"))
-                ga(nf2, nf, sW)
-            else:
-                nI, par = new("ist"), new("ist")
-                ixW = wrapped(pick(sg, ixW))
-                send(dst, T["li%d" % k][:, 0:20], ap(ixW), ri, ixW)
-                ga(nf2, nf, sW)
-                ts(nI, v, 160.0, OP.add)
+                    flags(1 if k == 0 else 0, 1)
+                    for hh in (0, 1) if k == 0 else (0,): signs(hh, 2)
+                    halves(k, 0, "g")
+                    if k == 0: halves(k, 1, "g")
+                else:
+                    halves(k, 0, "h")
+                    if k == 0: halves(k, 1, "h")
+        ga(("bx", 16, 336, 2), SG, R("it", 0, 10))
+        ga(("bx", 17, 336, 2), SG, R("it", 10, 20))
+        turn("us", 0, "bs", 0, 320)
+        sW = pick(R("us"), FULL)
+        ga(part(NF, 0, 160), R("nt"), part(sW, 0, 10))
+        turn("ux", 0, "bx", 0, 320)
+        turn("un", 0, "bn", 0, 160)
+        ixW = pick(R("ux"), FULL)
+        n0 = pick(R("un", 0, 352), HALF)
+        send(src, T["ln%d" % k][:, 0:10], ap(n0), rn, n0)
+        send(dst, T["li%d" % k][:, 0:20], ap(ixW), ri, ixW)
+        ga(part(NF, 160, 320), R("nt"), part(sW, 10, 20))
         for b in range(4):
-            w = R("xh", 320 * b, 320 * b + 320)
-            gt(R("zn", 320 * b, 320 * b + 320), w, ixW, ("xg", b, 1280, 4), OP.add)
+            gt(R("zn", 320 * b, 320 * b + 320), R("xh", 320 * b, 320 * b + 320), ixW, ("xg", b, 1280, 4), OP.add)
+        if k == 0: act(R("yt0"), R("xt0"), 32.0)
         arrives(rn, ENG, [R("ln%d" % k)])
         for b in range(4):
             (gv if b < 2 else ga)(("ft", b, 640, 4), R("zn", 320 * b, 320 * b + 320), R("ln%d" % k))
@@ -268,22 +283,37 @@ def rank_program(g, core, T, topo):
         quant(fq, fp, R("ft"))
         send(dst, T["lq%d" % k][:, 0:160].bitcast(dt.uint8), ap(fq).bitcast(dt.uint8), rd, fq)
         send(dst, T["lp%d" % k][:, 0:160], ap(fp), rd, fp)
-        ts(par, nI, 1, OP.bitwise_and)
-        nxW = other(nI, par)
         arrives(ri, ENG, [R("li%d" % k)])
-        ga(R("gf"), nf2, R("li%d" % k))
-        kW = wrapped(pick(R("gf"), part(nxW, 10, 20), 160), 10)
+        ga(R("gf"), NF, R("li%d" % k))
+        turn("un", 352, "bn", 160, 160)
+        nx = pick(R("un", 352, 704), HALF8)
+        ga(R("bk", 16, 176), R("gf"), nx)
+        if k < 2:
+            n2 = pick(R("un"), TWO)
+            split("ah", "bx", 0)
+            iW = pick(R("ua"), TWO)
+            roll("d_s", [(R("ns"), n2, 3, 1), (R("ow"), iW, 3, 1)])
+            roll("d_a", [(R("aa"), R("ah"), 3, 16)])
+            roll("d_i", [(R("it"), iW, 2, 1)])
+            roll("d_n", [(R("nt"), NF, 2, 8)])
+            nW, oW = R("ns"), R("ow", 10, 20)
+        turn("uk", 0, "bk", 0, 160)
+        kW = pick(R("uk"), HALF)
         for b in range(4):
-            ga(("vo", b, 640, 4), R("zn", 320 * b, 320 * b + 320), kW)
-        if k < 2: publish(xf2, nW, par)
+            (gv if b < 2 else ga)(("vo", b, 640, 4), R("zn", 320 * b, 320 * b + 320), kW)
+        if k == 0:
+            for b in range(4): quant(R("eq", 128 * b, 128 * b + 128), R("es", 128 * b, 128 * b + 128), R("et", 3 - b, 515 - b))
         def layer(half, tile):
             c = 160 * half
             q, p = R("vq%d" % k, c, c + 160), R("vp%d" % k, c, c + 160)
             quant(q, p, R(tile))
             for b in range(4): mm(bank(half, b), R("wq", 128 * b, 128 * b + 128), R("wsp", 128 * b, 128 * b + 128), q, p)
-            for b in range(4): tt(("yt%d" % (k + 1), 4 * c + b, 4 * c + 640, 4), bank(half, b), ("yt%d" % k, 4 * c + b, 4 * c + 640, 4), OP.add)
-            ts(R("xt%d" % (k + 1), 4 * c, 4 * c + 640), R("yt%d" % (k + 1), 4 * c, 4 * c + 640), 0.03125, OP.mult)
-            scores(k + 1, half)
+            for b in range(4):
+                y, x = ("yt%d" % (k + 1), 4 * c + b, 4 * c + 640, 4), ("xt%d" % (k + 1), 4 * c + b, 4 * c + 640, 4)
+                tt(y, bank(half, b), ("yt%d" % k, 4 * c + b, 4 * c + 640, 4), OP.add)
+                if b < 3: act(x, y, 0.03125)
+                else: ts(x, y, 0.03125, OP.mult)
+            scores(k + 1, half, [0, 1, 2])
             if k < 2:
                 flags(half, 0)
             else: out(half)
@@ -298,14 +328,17 @@ def rank_program(g, core, T, topo):
             dma("d_os", [("a", lambda e: e.dma_start(T.y[:, c:c + 160], ap(y)), [], [y])])
         if k == 2:
             quant(R("qv"), R("qvs"), R("vt"))
-            ts(R("nmf"), nf2, 160.0, OP.add)
+            ts(R("nmf"), NF, 160.0, OP.add)
             dma("d_os", [("s", lambda e: e.dma_start(T.nm[:], T.nmf[0:128:16, :]), [], [R("nmf")])])
         layer(1, "vo")
+        if k < 2:
+            tt(R("em"), E, O, OP.subtract)
+            flags(1, 1)
+            flags(1, 2)
         arrives(rd, 2 * ENG, [R("lq%d" % k), R("lp%d" % k)])
         for b in range(4): mm(bank(0, b), R("eq", 128 * b, 128 * b + 128), R("es", 128 * b, 128 * b + 128), R("lq%d" % k), R("lp%d" % k))
         for b in (0, 2, 1, 3): (cp if b % 2 else act)(("vf", b, 640, 4), bank(0, b))
-        if k < 2:
-            for jj in (1, 2): signs(1, jj)
         layer(0, "vf")
+        if k < 2: halves(k + 1, 1, "gh")
     for q, sem in QSEM.items(): total[sem] = count[q]
     for sem, val in total.items(): g.wait_ge(T.sem[sem], val)

@@ -5,19 +5,20 @@ from concourse.mybir import dt, AluOpType as OP, AxisListType, ActivationFunctio
 STEP = [1, 2, 4]
 BF, F16, F32, I32, U16, U8, CODE = "bfloat16", "float16", "float32", "int32", "uint16", "uint8", "float8_e4m3fn_x4"
 ROT = [(17 * j - 48) % 128 for j in range(3)]
+NV = 2
 SCRATCH = {
     "nls": ("sbuf", [128, 20], I32), "nlt": ("sbuf", [128, 20], I32), "ut": ("sbuf", [128, 648], BF), "vt": ("sbuf", [128, 512], BF),
     "qu": ("sbuf", [128, 162], CODE), "qus": ("sbuf", [128, 162], U8), "qo": ("sbuf", [128, 128], CODE), "qos": ("sbuf", [128, 128], U8),
     "qv": ("sbuf", [128, 128], CODE), "qvs": ("sbuf", [128, 128], U8), "wq": ("sbuf", [128, 512], CODE), "wsp": ("sbuf", [128, 512], U8),
     "et": ("sbuf", [128, 528], BF), "eq": ("sbuf", [128, 512], CODE), "es": ("sbuf", [128, 512], U8),
-    "icf": ("sbuf", [128, 320], BF), "icx": ("sbuf", [128, 320], BF), "ci": ("sbuf", [128, 32], I32), "co": ("sbuf", [128, 8], U16),
+    "icf": ("sbuf", [128, 320], BF), "ci": ("sbuf", [128, 32], I32), "co": ("sbuf", [128, 8], U16),
     "fw": ("sbuf", [128, 960], BF), "aa": ("sbuf", [128, 368], BF), "ah": ("sbuf", [128, 368], BF), "em": ("sbuf", [128, 160], F16), "dl": ("sbuf", [128, 160], F16),
-    "val": ("sbuf", [128, 320], BF), "bs": ("sbuf", [128, 352], BF), "bn": ("sbuf", [128, 352], BF), "bx": ("sbuf", [128, 352], BF), "bk": ("sbuf", [128, 192], BF),
-    "us": ("sbuf", [128, 672], BF), "un": ("sbuf", [128, 704], BF), "ua": ("sbuf", [128, 704], BF), "ux": ("sbuf", [128, 672], BF), "uk": ("sbuf", [128, 352], BF),
-    "nt": ("sbuf", [128, 320], BF), "it": ("sbuf", [128, 20], U16), "ns": ("sbuf", [128, 20], U16), "ow": ("sbuf", [128, 20], U16), "gf": ("sbuf", [128, 320], BF),
+    "val": ("sbuf", [128, 320], BF), "bs": ("sbuf", [128, 352], BF), "bn": ("sbuf", [128, 352], BF), "bx": ("sbuf", [128, 320], BF), "bk": ("sbuf", [128, 192], BF),
+    "us": ("sbuf", [128, 704], BF), "un": ("sbuf", [128, 704], BF), "ua": ("sbuf", [128, 704], BF), "uk": ("sbuf", [128, 352], BF),
+    "nt": ("sbuf", [128, 320], BF), "io_": ("sbuf", [128, 10], U16), "ie": ("sbuf", [128, 10], U16), "ns": ("sbuf", [128, 20], U16), "ow": ("sbuf", [128, 10], U16), "gf": ("sbuf", [128, 320], BF),
     "lst": ("sbuf", [128, 1600], U16),
     "xh": ("sbuf", [128, 1280], BF), "xg": ("sbuf", [128, 1280], BF), "zn": ("sbuf", [128, 1280], BF), "ft": ("sbuf", [128, 640], BF), "vo": ("sbuf", [128, 640], BF), "vf": ("sbuf", [128, 640], BF),
-    "zt": ("sbuf", [128, 640], BF), "yo": ("sbuf", [128, 320], F32), "nmf": ("sbuf", [128, 320], F32),
+    "zt": ("sbuf", [128, 1280], BF), "yo": ("sbuf", [128, 320], F32), "nmf": ("sbuf", [128, 320], F32),
 }
 for _k in range(4):
     SCRATCH.update({"xt%d" % _k: ("sbuf", [128, 1280], BF), "yt%d" % _k: ("sbuf", [128, 1280], BF), "xq%d" % _k: ("sbuf", [128, 320], CODE), "xs%d" % _k: ("sbuf", [128, 320], U8)})
@@ -27,7 +28,7 @@ for _k in range(3):
 for _k in range(8):
     SCRATCH["p%d" % _k] = ("psum", [128, 512], F32)
 QSEM = {"v": "qv_", "a": "qa_", "t": "qt_", "g": "qg_"}
-SEMAPHORES = list(QSEM.values()) + ["d_ns", "d_nt", "d_u", "d_x0", "d_x1", "d_w", "d_v", "d_c", "d_q", "d_i", "d_n", "d_s", "d_a", "d_os", "sent"] + ["r%s%d" % (a, k) for a in "nid" for k in range(3)]
+SEMAPHORES = list(QSEM.values()) + ["d_ns", "d_nt", "d_u", "d_x0", "d_x1", "d_w", "d_v", "d_q", "d_o", "d_e", "d_n", "d_s", "d_a", "d_os", "sent"] + ["r%s%d" % (a, k) for a in "nid" for k in range(3)]
 
 
 def rank_program(g, core, T, topo):
@@ -107,7 +108,7 @@ def rank_program(g, core, T, topo):
         a = slots[name]
         slots[name] += n
         return R(name, a, a + n)
-    def part(r, a, b): return (r[0], r[1] + a, r[1] + b, 1)
+    def part(r, a, b, st=1): return (r[0], r[1] + a, r[1] + b, st)
 
     def tt(out, a, b, o): op("v", lambda: g.vector.tensor_tensor(ap(out), ap(a), ap(b), o), [out], [a, b])
     def ts(out, a, s1, o1, s2=None, o2=None):
@@ -123,13 +124,15 @@ def rank_program(g, core, T, topo):
     def mm(out, l, ls, r, rs): op("t", lambda: g.tensor.matmul_mx(ap(out), ap(l), ap(ls), ap(r), ap(rs), True, True), [out], [l, ls, r, rs])
     def iota(out, pattern, base, cm, flag=False):
         op("g", lambda: g.iota(ap(out), pattern, base, cm, allow_small_or_imprecise_dtypes=True) if flag else g.iota(ap(out), pattern, base, cm), [out], [])
+    def gcopy(out, a):
+        op("g", lambda: g.affine_select(ap(out), ap(a), [[0, out[2] - out[1]]], OP.is_gt, 0.0, 1, 0), [out], [a])
     def turn(u, uo, b, bo, n):
         for o, i in ((R(u, uo, uo + n), R(b, bo + 16, bo + 16 + n)), (R(u, uo + n, uo + 2 * n + 32), R(b, bo, bo + n + 32))):
             op("v", lambda: g.vector.transpose(ap(o), ap(i)), [o], [i])
-    FULL, TWO, HALF, HALF8 = R("co", 0, 2), R("co", 2, 4), R("co", 4, 5), R("co", 6, 7)
-    def pick(win, c):
+    FULL, TWO, HALF = R("co", 0, 2), R("co", 2, 4), R("co", 4, 5)
+    def pick(win, c, o=None):
         n = 16 * (c[2] - c[1])
-        o = new("lst", n)
+        o = part(o, 0, n) if o else new("lst", n)
         op("v", lambda: g.vector.tensor_scalar(ap(o), ap(win).indirect(ap(c)), 160.0, None, OP.add), [o], [win, c])
         return part(o, 0, 10 * (c[2] - c[1]))
     def roll(sem, moves, q="s"):
@@ -144,89 +147,81 @@ def rank_program(g, core, T, topo):
         d = 16 * up
         dma(sem, [(q, lambda e: e.dma_start(T[out][d:128, :], T.nl[0:128 - d, :]), [R(out)], []), (q, lambda e: e.dma_start(T[out][0:d, :], T.nl[128 - d:128, :]), [R(out)], [])])
     rows("d_ns", "s", "nls", 3)
+    rows("d_nt", "a", "nlt", 2)
     r0 = 4 * ROT[0]
-    dma("d_u", [("a", lambda e: e.dma_start(T.ut[:, 0:512 - r0], T.u[:, r0:512]), [R("ut")], []), ("a", lambda e: e.dma_start(T.ut[:, 512 - r0:648], T.u[:, 0:136 + r0]), [R("ut")], [])])
+    dma("d_u", [("s", lambda e: e.dma_start(T.ut[:, 0:512 - r0], T.u[:, r0:512]), [R("ut")], []), ("a", lambda e: e.dma_start(T.ut[:, 512 - r0:648], T.u[:, 0:136 + r0]), [R("ut")], [])])
     for h, q in ((0, "s"), (1, "a")):
         dma("d_x%d" % h, [(q, lambda e, h=h: e.dma_start(T.xt0[:, 640 * h:640 * h + 640], T.x[:, 640 * h:640 * h + 640]), [R("xt0", 640 * h, 640 * h + 640)], [])])
-    rows("d_nt", "s", "nlt", 2)
 
-    p, t, q, h, a, s, m = [new("ci", 2) for _ in range(7)]
+    p, t, q, h, a, s, m, q2, s1, s2, ge, f1, f2, f3 = [new("ci", 2) for _ in range(14)]
     iota(p, [[0, 2]], 0, 1)
     iota(t, [[256, 2]], 0, 0)
     iota(R("icf"), [[1, 320]], -160, 0, True)
-    iota(R("icx"), [[2, 160], [-1, 2]], -159, 0, True)
-    dma("d_c", [("s", lambda e: e.dma_start(T.icx[0:128:16, :], T.icf[0:128:16, :]), [R("icx")], [R("icf")])])
-    ts(q, p, 15, OP.bitwise_and)
-    ts(h, p, 4, OP.arith_shift_right)
-    for b in ("aa", "ah", "bx"): fill(R(b), 0.0)
-    ts(q2 := new("ci", 2), q, 16.0, OP.mult)
-    tt(a, p, h, OP.add)
-    for b in ("bs", "bn"): fill(R(b), 0.0)
-    tt(m, q2, t, OP.add)
-    ts(s, a, 1, OP.bitwise_and)
-    for b in ("bk", "nt"): fill(R(b), 0.0)
-    s1, s2, ge, f1, f2, f3 = [new("ci", 2) for _ in range(6)]
-    ts(ge, m, 160.0, OP.is_ge, 192.0, OP.mult)
-    ts(s1, s, 336.0, OP.mult)
-    ts(s2, s, 176.0, OP.mult)
     fill(R("et"), 1.0)
-    tt(f1, m, s1, OP.add)
-    tt(f2, m, s2, OP.add)
-    ts(FULL, f1, 671.0, OP.min)
-    tt(f3, f2, ge, OP.add)
-    ts(HALF, part(f2, 0, 1), 351.0, OP.min)
-    ts(HALF8, part(f2, 0, 1), 8.0, OP.add, 351.0, OP.min)
-    ts(TWO, f3, 703.0, OP.min)
     op("g", lambda: g.affine_select(T.et[:], T.et[:], [[1, 528]], OP.is_equal, 0.0, -3, -4), [R("et")], [R("et")])
+    ts(h, p, 4, OP.arith_shift_right)
+    ts(q, p, 15, OP.bitwise_and)
+    fill(R("aa"), 0.0)
+    tt(a, p, h, OP.add)
+    ts(q2, q, 16.0, OP.mult)
+    fill(R("bs"), 0.0)
+    ts(s, a, 1, OP.bitwise_and)
+    tt(m, q2, t, OP.add)
+    fill(R("bn"), 0.0)
+    ts(s2, s, 176.0, OP.mult)
+    ts(s1, s, 336.0, OP.mult)
+    ts(ge, m, 160.0, OP.is_ge, 192.0, OP.mult)
+    tt(f2, m, s2, OP.add)
+    tt(f1, m, s1, OP.add)
+    ts(HALF, part(f2, 0, 1), 351.0, OP.min)
 
     E, O = R("aa", 16, 176), R("aa", 192, 352)
-    def split(b, src, first):
-        cp(R(b, 16 + 176 * first, 176 + 176 * first), (src, 16, 336, 2))
-        cp(R(b, 192 - 176 * first, 352 - 176 * first), (src, 17, 336, 2))
-        turn("ua", 352, b, 176, 160)
-        turn("ua", 0, b, 0, 160)
+    UE, UO = R("ua", 0, 352), R("ua", 352, 704)
     nW, nT = new("lst", 20), new("lst", 20)
     cp(nW, R("nls"))
-    op("v", lambda: g.vector.tensor_copy(T.bx[:, 16:336].indirect(ap(nW)), ap(R("icf"))), [R("bx", 16, 336)], [nW, R("icf")])
-    split("aa", "bx", 1)
-    tt(R("em"), E, O, OP.subtract)
-    iW = pick(R("ua"), TWO)
-    roll("d_i", [(R("it"), iW, -1, 1)])
+    cp(nT, R("nlt"))
+    op("v", lambda: g.vector.tensor_copy(T.bx[:, 0:320].indirect(ap(nW)), ap(R("icf"))), [R("bx")], [nW, R("icf")])
+    ga(R("nt"), R("icf"), nT)
+    tt(f3, f2, ge, OP.add)
+    cp(O, ("bx", 0, 320, 2))
+    act(E, ("bx", 1, 320, 2))
+    ts(FULL, f1, 671.0, OP.min)
+    turn("ua", 352, "aa", 176, 160)
+    oW = pick(UO, HALF)
+    roll("d_o", [(R("io_"), oW, -1, 1)])
+    o1, o2 = ROT[1] - ROT[0], ROT[2] - ROT[0]
     quant(R("qu"), R("qus"), R("ut"))
-    o1 = ROT[1] - ROT[0]
     dma("d_q", [("s", lambda e: e.dma_start(T.qo[:, 0:128].bitcast(dt.uint8), T.qu[:, o1:o1 + 128].bitcast(dt.uint8)), [R("qo")], [R("qu")]),
                 ("s", lambda e: e.dma_start(T.qos[:, 0:128], T.qus[:, o1:o1 + 128]), [R("qos")], [R("qus")])])
-    cp(nT, R("nlt"))
-    ga(R("nt"), R("icx"), nT)
-    oW = part(iW, 10, 20)
-    dma("d_w", [("s", lambda e: e.dma_start(T.wq[:, 0:512].bitcast(dt.uint8), T.wc[:, 0:2048]), [R("wq")], []),
-                ("s", lambda e: e.dma_start(T.wsp[:, 0:512], T.ws[:, 0:512]), [R("wsp")], [])])
-    dma("d_v", [("s", lambda e: e.dma_start(T.vt[:], T.v[:]), [R("vt")], [])])
-
-    o2 = ROT[2] - ROT[0]
     US = [(R("qu", 0, 128), R("qus", 0, 128)), (R("qo"), R("qos")), (R("qu", o2, o2 + 128), R("qus", o2, o2 + 128))]
     def bank(half, b): return R("p%d" % (4 * half + b), 0, 160)
+    def qx(k, half): return R("xq%d" % k, 160 * half, 160 * half + 160), R("xs%d" % k, 160 * half, 160 * half + 160)
+    def quantx(k, half): quant(*qx(k, half), R("xt%d" % k, 640 * half, 640 * half + 640))
     def scores(k, half, js):
-        c = 160 * half
-        q, s = R("xq%d" % k, c, c + 160), R("xs%d" % k, c, c + 160)
-        if 0 in js or k == 3: quant(q, s, R("xt%d" % k, 4 * c, 4 * c + 640))
-        if k < 3:
-            for j in js: mm(bank(half, j), US[j][0], US[j][1], q, s)
+        for j in js: mm(bank(half, j), *US[j], *qx(k, half))
     def fl(half, j): return R("fw", 320 * j + 160 * half, 320 * j + 160 * half + 160)
-    def signs(half, j):
-        act(fl(half, j), bank(half, j), f=AF.Sign)
-        act(fl(half, j), fl(half, j), f=AF.Relu)
+    def signs(j, hs):
+        for half in hs: act(fl(half, j), bank(half, j), f=AF.Sign)
+        act(R("fw", 320 * j, 320 * j + 320), R("fw", 320 * j, 320 * j + 320), f=AF.Relu)
     def flags(half, j): ts(fl(half, j), bank(half, j), 0.0, OP.is_gt)
-    def halves(k, half, what):
+    def halves(k, half):
         c = 160 * half
-        if "g" in what: act(R("xg", 4 * c, 4 * c + 640), R("xt%d" % k, 4 * c, 4 * c + 640), 0.5)
-        if "h" in what:
-            for b in range(4): act(R("xh", 320 * b + c, 320 * b + c + 160), (("xt%d" % k), 4 * c + b, 4 * c + 640, 4), 0.5)
+        for b in range(4): act(R("xh", 320 * b + c, 320 * b + c + 160), (("xt%d" % k), 4 * c + b, 4 * c + 640, 4), 0.5)
+    for h in (0, 1):
+        quantx(0, h)
+        scores(0, h, [0])
+    turn("ua", 0, "aa", 0, 160)
+    flags(0, 0)
+    eW = pick(UE, HALF)
+    flags(1, 0)
+    roll("d_e", [(R("ie"), eW, -1, 1)])
+    tt(R("em"), E, O, OP.subtract)
+    ts(TWO, f3, 703.0, OP.min)
+    for j in (2, 1):
+        for h in (0, 1): scores(0, h, [j])
+    halves(0, 1)
+    signs(1, (0, 1))
 
-    scores(0, 0, [0])
-    scores(0, 1, [0])
-    for h in (0, 1): flags(h, 0)
-    for h in (0, 1): scores(0, h, [2, 1])
     SG, NF = R("bs", 16, 336), R("bn", 16, 336)
     for k, s in enumerate(STEP):
         src, dst = T.cores[(rank - s) % N], T.cores[(rank + s) % N]
@@ -234,111 +229,137 @@ def rank_program(g, core, T, topo):
         for j in range(3):
             gt(R("dl"), R("fw", 320 * j, 320 * j + 320), oW, R("em"), OP.mult)
             if j: turn("un", 0, "bn", 0, 320)
+            if k == 0 and j == 0: fill(R("ah"), 0.0)
             tt(("val", 0, 320, 2), O, R("dl"), OP.add)
-            tt(("val", 1, 320, 2), E, R("dl"), OP.subtract)
             if j: nW = pick(R("un", 0, 672), FULL)
+            tt(("val", 1, 320, 2), E, R("dl"), OP.subtract)
             ga(part(SG, 160, 320), R("val"), part(nW, 10, 20))
             gv(part(SG, 0, 160), R("val"), part(nW, 0, 10))
-            if j < 2:
-                ga(O, SG, R("it", 10, 20))
-                ga(E, SG, R("it", 0, 10))
-                turn("us", 0, "bs", 0, 320)
-                if j == 0 and k == 0: flags(0, 1)
-                sW = pick(R("us"), FULL)
-                turn("ua", 352, "aa", 176, 160)
-                ga(NF, R("nt"), sW)
-                turn("ua", 0, "aa", 0, 160)
-                tt(R("em"), E, O, OP.subtract)
-                iW = pick(R("ua"), TWO)
-                oW = part(iW, 10, 20)
-                roll("d_i", [(R("it"), iW, -1, 1)])
-                roll("d_n", [(R("nt"), NF, -1, 8)])
-                if j == 0:
-                    flags(1 if k == 0 else 0, 1)
-                    for hh in (0, 1) if k == 0 else (0,): signs(hh, 2)
-                    halves(k, 0, "g")
-                    if k == 0: halves(k, 1, "g")
-                else:
-                    halves(k, 0, "h")
-                    if k == 0: halves(k, 1, "h")
-        ga(("bx", 16, 336, 2), SG, R("it", 0, 10))
-        ga(("bx", 17, 336, 2), SG, R("it", 10, 20))
-        turn("us", 0, "bs", 0, 320)
-        sW = pick(R("us"), FULL)
-        ga(part(NF, 0, 160), R("nt"), part(sW, 0, 10))
-        turn("ux", 0, "bx", 0, 320)
+            if j == 2: break
+            ga(O, SG, R("io_"))
+            ga(E, SG, R("ie"))
+            turn("us", 0, "bs", 0, 320)
+            turn("ua", 352, "aa", 176, 160)
+            sW = pick(R("us", 0, 672), FULL)
+            oW = pick(UO, HALF)
+            ga(NF, R("nt"), sW)
+            roll("d_o", [(R("io_"), oW, -1, 1)])
+            turn("ua", 0, "aa", 0, 160)
+            tt(R("em"), E, O, OP.subtract)
+            eW = pick(UE, HALF)
+            roll("d_e", [(R("ie"), eW, -1, 1)])
+            roll("d_n", [(R("nt"), NF, -1, 16)])
+            if j == 0:
+                signs(2, (0, 1))
+                if k == 0:
+                    dma("d_w", [("s", lambda e: e.dma_start(T.wq[:, 0:512].bitcast(dt.uint8), T.wc[:, 0:2048]), [R("wq")], []),
+                                ("s", lambda e: e.dma_start(T.wsp[:, 0:512], T.ws[:, 0:512]), [R("wsp")], [])])
+            else:
+                halves(k, 0)
+                gcopy(R("xg", 0, 320 * NV), R("xh", 0, 320 * NV))
+        turn("us", 0, "bs", 0, 160)
+        ga(R("ah", 192, 352), SG, R("io_"))
+        s0 = pick(R("us", 0, 352), HALF)
+        ga(part(NF, 0, 160), R("nt"), s0)
+        ga(R("ah", 16, 176), SG, R("ie"))
+        turn("ua", 352, "ah", 176, 160)
+        iW = new("lst", 32)
+        oW = pick(UO, HALF, iW)
         turn("un", 0, "bn", 0, 160)
-        ixW = pick(R("ux"), FULL)
+        def means(b, l, e):
+            if b < NV: gt(("zn", 320 * b + e, 320 * b + 320, 2), R("xh", 320 * b, 320 * b + 320), l, ("xg", 320 * b + e, 320 * b + 320, 2), OP.add)
+            else: ga(("zt", 320 * b + e, 320 * b + 320, 2), R("xh", 320 * b, 320 * b + 320), l)
+        for b in range(NV, 4): means(b, oW, 1)
         n0 = pick(R("un", 0, 352), HALF)
         send(src, T["ln%d" % k][:, 0:10], ap(n0), rn, n0)
-        send(dst, T["li%d" % k][:, 0:20], ap(ixW), ri, ixW)
-        ga(part(NF, 160, 320), R("nt"), part(sW, 10, 20))
-        for b in range(4):
-            gt(R("zn", 320 * b, 320 * b + 320), R("xh", 320 * b, 320 * b + 320), ixW, ("xg", b, 1280, 4), OP.add)
-        if k == 0: act(R("yt0"), R("xt0"), 32.0)
+        turn("ua", 0, "ah", 0, 160)
+        means(0, oW, 1)
+        eW = pick(UE, HALF, part(iW, 10, 26))
+        iW = part(iW, 0, 20)
+        send(dst, T["li%d" % k][:, 0:20], ap(iW), ri, iW)
+        for b in range(NV, 4): means(b, eW, 0)
+        for b in range(1, NV): means(b, oW, 1)
+        turn("us", 352, "bs", 160, 160)
+        means(0, eW, 0)
+        s1 = pick(R("us", 352, 704), HALF)
+        ga(part(NF, 160, 320), R("nt"), s1)
+        for b in range(1, NV): means(b, eW, 0)
+        for b in range(NV, 4): tt(R("zn", 320 * b, 320 * b + 320), R("zt", 320 * b, 320 * b + 320), R("xh", 320 * b, 320 * b + 320), OP.add)
+        turn("un", 352, "bn", 160, 160)
+        if k == 0:
+            act(R("yt0", 640, 1280), R("xt0", 640, 1280), 32.0)
+            fill(R("bk"), 0.0)
+        n2 = pick(R("un"), TWO)
+        if k == 0:
+            for b in range(4): quant(R("eq", 128 * b, 128 * b + 128), R("es", 128 * b, 128 * b + 128), R("et", 3 - b, 515 - b))
         arrives(rn, ENG, [R("ln%d" % k)])
         for b in range(4):
-            (gv if b < 2 else ga)(("ft", b, 640, 4), R("zn", 320 * b, 320 * b + 320), R("ln%d" % k))
+            (ga if b < 2 else gv)(("ft", b, 640, 4), R("zn", 320 * b, 320 * b + 320), R("ln%d" % k))
         fq, fp = R("fq%d" % k), R("fp%d" % k)
         quant(fq, fp, R("ft"))
         send(dst, T["lq%d" % k][:, 0:160].bitcast(dt.uint8), ap(fq).bitcast(dt.uint8), rd, fq)
         send(dst, T["lp%d" % k][:, 0:160], ap(fp), rd, fp)
         arrives(ri, ENG, [R("li%d" % k)])
-        ga(R("gf"), NF, R("li%d" % k))
-        turn("un", 352, "bn", 160, 160)
-        nx = pick(R("un", 352, 704), HALF8)
-        ga(R("bk", 16, 176), R("gf"), nx)
+        ga(("gf", 0, 320, 2), NF, R("li%d" % k, 0, 10))
+        ga(("gf", 1, 320, 2), NF, R("li%d" % k, 10, 20))
+        ga(R("bk", 16, 176), R("gf"), part(n2, 10, 20))
         if k < 2:
-            n2 = pick(R("un"), TWO)
-            split("ah", "bx", 0)
-            iW = pick(R("ua"), TWO)
-            roll("d_s", [(R("ns"), n2, 3, 1), (R("ow"), iW, 3, 1)])
             roll("d_a", [(R("aa"), R("ah"), 3, 16)])
-            roll("d_i", [(R("it"), iW, 2, 1)])
-            roll("d_n", [(R("nt"), NF, 2, 8)])
-            nW, oW = R("ns"), R("ow", 10, 20)
+            roll("d_s", [(R("ns"), n2, 3, 1), (R("ow"), oW, 3, 1)])
+            roll("d_o", [(R("io_"), oW, 2, 1)])
+            roll("d_e", [(R("ie"), eW, 2, 1)])
+            roll("d_n", [(R("nt"), NF, 2, 16)])
+            nW, oW = R("ns"), R("ow")
+        if k == 0:
+            act(R("yt0", 0, 640), R("xt0", 0, 640), 32.0)
+        if k == 2:
+            quant(R("qv"), R("qvs"), R("vt"))
+            ts(R("nmf"), NF, 160.0, OP.add)
+            dma("d_os", [("s", lambda e: e.dma_start(T.nm[:], T.nmf[0:128:16, :]), [], [R("nmf")])])
         turn("uk", 0, "bk", 0, 160)
         kW = pick(R("uk"), HALF)
         for b in range(4):
             (gv if b < 2 else ga)(("vo", b, 640, 4), R("zn", 320 * b, 320 * b + 320), kW)
-        if k == 0:
-            for b in range(4): quant(R("eq", 128 * b, 128 * b + 128), R("es", 128 * b, 128 * b + 128), R("et", 3 - b, 515 - b))
         def layer(half, tile):
             c = 160 * half
             q, p = R("vq%d" % k, c, c + 160), R("vp%d" % k, c, c + 160)
             quant(q, p, R(tile))
             for b in range(4): mm(bank(half, b), R("wq", 128 * b, 128 * b + 128), R("wsp", 128 * b, 128 * b + 128), q, p)
+        def state(half):
+            c = 160 * half
             for b in range(4):
                 y, x = ("yt%d" % (k + 1), 4 * c + b, 4 * c + 640, 4), ("xt%d" % (k + 1), 4 * c + b, 4 * c + 640, 4)
                 tt(y, bank(half, b), ("yt%d" % k, 4 * c + b, 4 * c + 640, 4), OP.add)
                 if b < 3: act(x, y, 0.03125)
                 else: ts(x, y, 0.03125, OP.mult)
-            scores(k + 1, half, [0, 1, 2])
-            if k < 2:
-                flags(half, 0)
-            else: out(half)
+            quantx(k + 1, half)
         def out(half):
             c = 160 * half
-            q, p = R("xq3", c, c + 160), R("xs3", c, c + 160)
+            q, p = qx(3, half)
             mm(bank(half, 0), R("qv"), R("qvs"), q, p)
             dma("d_os", [("s", lambda e: e.dma_start(T.oc[:, 4 * c:4 * c + 640], ap(q).bitcast(dt.uint8)), [], [q])] +
                 [("s", lambda e, i=i: e.dma_start(T.osc[4 * i:4 * i + 4, c:c + 160], T.xs3[32 * i:32 * i + 4, c:c + 160]), [], [p]) for i in range(4)])
             y = R("yo", c, c + 160)
             act(y, bank(half, 0))
             dma("d_os", [("a", lambda e: e.dma_start(T.y[:, c:c + 160], ap(y)), [], [y])])
-        if k == 2:
-            quant(R("qv"), R("qvs"), R("vt"))
-            ts(R("nmf"), NF, 160.0, OP.add)
-            dma("d_os", [("s", lambda e: e.dma_start(T.nm[:], T.nmf[0:128:16, :]), [], [R("nmf")])])
         layer(1, "vo")
-        if k < 2:
-            tt(R("em"), E, O, OP.subtract)
-            flags(1, 1)
-            flags(1, 2)
         arrives(rd, 2 * ENG, [R("lq%d" % k), R("lp%d" % k)])
         for b in range(4): mm(bank(0, b), R("eq", 128 * b, 128 * b + 128), R("es", 128 * b, 128 * b + 128), R("lq%d" % k), R("lp%d" % k))
-        for b in (0, 2, 1, 3): (cp if b % 2 else act)(("vf", b, 640, 4), bank(0, b))
+        state(1)
+        for b in (0, 2, 1, 3): (cp if b == 3 else act)(("vf", b, 640, 4), bank(0, b))
+        if k < 2: scores(k + 1, 1, [0, 1, 2])
         layer(0, "vf")
-        if k < 2: halves(k + 1, 1, "gh")
+        if k < 2:
+            flags(1, 0)
+            tt(R("em"), E, O, OP.subtract)
+        else: out(1)
+        state(0)
+        if k < 2:
+            scores(k + 1, 0, [0, 1, 2])
+            halves(k + 1, 1)
+            flags(0, 0)
+            signs(1, (1, 0))
+            if k == 0: dma("d_v", [("s", lambda e: e.dma_start(T.vt[:], T.v[:]), [R("vt")], [])])
+        else: out(0)
     for q, sem in QSEM.items(): total[sem] = count[q]
     for sem, val in total.items(): g.wait_ge(T.sem[sem], val)

@@ -4,8 +4,15 @@ from concourse.mybir import dt, AluOpType as OP, AxisListType, ActivationFunctio
 
 STEP = [1, 2, 4]
 BF, F16, F32, I32, U16, U8, CODE = "bfloat16", "float16", "float32", "int32", "uint16", "uint8", "float8_e4m3fn_x4"
-ROT = [(17 * j - 48) % 128 for j in range(3)]
 NV = 2
+ROT = [(17 * j - 48) % 128 for j in range(3)]
+V4 = 2
+V5 = 1
+VX = 2
+VF = 2
+V1 = 1
+V2 = 1
+V3 = 1
 SCRATCH = {
     "nls": ("sbuf", [128, 20], I32), "nlt": ("sbuf", [128, 20], I32), "ut": ("sbuf", [128, 648], BF), "vt": ("sbuf", [128, 512], BF),
     "qu": ("sbuf", [128, 162], CODE), "qus": ("sbuf", [128, 162], U8), "qo": ("sbuf", [128, 128], CODE), "qos": ("sbuf", [128, 128], U8),
@@ -126,8 +133,9 @@ def rank_program(g, core, T, topo):
         op("g", lambda: g.iota(ap(out), pattern, base, cm, allow_small_or_imprecise_dtypes=True) if flag else g.iota(ap(out), pattern, base, cm), [out], [])
     def gcopy(out, a):
         op("g", lambda: g.affine_select(ap(out), ap(a), [[0, out[2] - out[1]]], OP.is_gt, 0.0, 1, 0), [out], [a])
-    def turn(u, uo, b, bo, n):
-        for o, i in ((R(u, uo, uo + n), R(b, bo + 16, bo + 16 + n)), (R(u, uo + n, uo + 2 * n + 32), R(b, bo, bo + n + 32))):
+    def turn(u, uo, b, bo, n, which=(0, 1)):
+        for w in which:
+            o, i = ((R(u, uo, uo + n), R(b, bo + 16, bo + 16 + n)), (R(u, uo + n, uo + 2 * n + 32), R(b, bo, bo + n + 32)))[w]
             op("v", lambda: g.vector.transpose(ap(o), ap(i)), [o], [i])
     FULL, TWO, HALF = R("co", 0, 2), R("co", 2, 4), R("co", 4, 5)
     def pick(win, c, o=None):
@@ -159,21 +167,23 @@ def rank_program(g, core, T, topo):
     iota(R("icf"), [[1, 320]], -160, 0, True)
     fill(R("et"), 1.0)
     op("g", lambda: g.affine_select(T.et[:], T.et[:], [[1, 528]], OP.is_equal, 0.0, -3, -4), [R("et")], [R("et")])
+    for b, pads in (("aa", (0, 176, 352)), ("bs", (0, 336)), ("bn", (0, 336)), ("ah", (0, 176, 352)), ("bk", (0, 176))):
+        for c in pads: act(R(b, c, c + 16), R("icf", 0, 16), 0.0)
     ts(h, p, 4, OP.arith_shift_right)
     ts(q, p, 15, OP.bitwise_and)
-    fill(R("aa"), 0.0)
     tt(a, p, h, OP.add)
     ts(q2, q, 16.0, OP.mult)
-    fill(R("bs"), 0.0)
     ts(s, a, 1, OP.bitwise_and)
     tt(m, q2, t, OP.add)
-    fill(R("bn"), 0.0)
     ts(s2, s, 176.0, OP.mult)
     ts(s1, s, 336.0, OP.mult)
     ts(ge, m, 160.0, OP.is_ge, 192.0, OP.mult)
     tt(f2, m, s2, OP.add)
     tt(f1, m, s1, OP.add)
     ts(HALF, part(f2, 0, 1), 351.0, OP.min)
+    tt(f3, f2, ge, OP.add)
+    ts(FULL, f1, 671.0, OP.min)
+    ts(TWO, f3, 703.0, OP.min)
 
     E, O = R("aa", 16, 176), R("aa", 192, 352)
     UE, UO = R("ua", 0, 352), R("ua", 352, 704)
@@ -182,17 +192,12 @@ def rank_program(g, core, T, topo):
     cp(nT, R("nlt"))
     op("v", lambda: g.vector.tensor_copy(T.bx[:, 0:320].indirect(ap(nW)), ap(R("icf"))), [R("bx")], [nW, R("icf")])
     ga(R("nt"), R("icf"), nT)
-    tt(f3, f2, ge, OP.add)
-    cp(O, ("bx", 0, 320, 2))
-    act(E, ("bx", 1, 320, 2))
-    ts(FULL, f1, 671.0, OP.min)
-    turn("ua", 352, "aa", 176, 160)
-    oW = pick(UO, HALF)
-    roll("d_o", [(R("io_"), oW, -1, 1)])
-    o1, o2 = ROT[1] - ROT[0], ROT[2] - ROT[0]
     quant(R("qu"), R("qus"), R("ut"))
+    o1, o2 = ROT[1] - ROT[0], ROT[2] - ROT[0]
     dma("d_q", [("s", lambda e: e.dma_start(T.qo[:, 0:128].bitcast(dt.uint8), T.qu[:, o1:o1 + 128].bitcast(dt.uint8)), [R("qo")], [R("qu")]),
                 ("s", lambda e: e.dma_start(T.qos[:, 0:128], T.qus[:, o1:o1 + 128]), [R("qos")], [R("qus")])])
+    cp(O, ("bx", 0, 320, 2))
+    act(E, ("bx", 1, 320, 2))
     US = [(R("qu", 0, 128), R("qus", 0, 128)), (R("qo"), R("qos")), (R("qu", o2, o2 + 128), R("qus", o2, o2 + 128))]
     def bank(half, b): return R("p%d" % (4 * half + b), 0, 160)
     def qx(k, half): return R("xq%d" % k, 160 * half, 160 * half + 160), R("xs%d" % k, 160 * half, 160 * half + 160)
@@ -207,20 +212,26 @@ def rank_program(g, core, T, topo):
     def halves(k, half):
         c = 160 * half
         for b in range(4): act(R("xh", 320 * b + c, 320 * b + c + 160), (("xt%d" % k), 4 * c + b, 4 * c + 640, 4), 0.5)
-    for h in (0, 1):
-        quantx(0, h)
-        scores(0, h, [0])
+    quantx(0, 0)
+    scores(0, 0, [0])
+    turn("ua", 352, "aa", 176, 160)
     turn("ua", 0, "aa", 0, 160)
-    flags(0, 0)
+    oW = pick(UO, HALF)
+    quantx(0, 1)
+    scores(0, 1, [0])
     eW = pick(UE, HALF)
-    flags(1, 0)
+    roll("d_o", [(R("io_"), oW, -1, 1)])
     roll("d_e", [(R("ie"), eW, -1, 1)])
     tt(R("em"), E, O, OP.subtract)
-    ts(TWO, f3, 703.0, OP.min)
+    flags(0, 0)
+    flags(1, 0)
     for j in (2, 1):
         for h in (0, 1): scores(0, h, [j])
     halves(0, 1)
-    signs(1, (0, 1))
+    signs(2, (0, 1))
+    spare = [lambda: flags(0, 1), lambda: flags(1, 1)] + [lambda b=b: quant(R("eq", 128 * b, 128 * b + 128), R("es", 128 * b, 128 * b + 128), R("et", 3 - b, 515 - b)) for b in range(4)]
+    def filler():
+        if spare: spare.pop(0)()
 
     SG, NF = R("bs", 16, 336), R("bn", 16, 336)
     for k, s in enumerate(STEP):
@@ -229,12 +240,13 @@ def rank_program(g, core, T, topo):
         for j in range(3):
             gt(R("dl"), R("fw", 320 * j, 320 * j + 320), oW, R("em"), OP.mult)
             if j: turn("un", 0, "bn", 0, 320)
-            if k == 0 and j == 0: fill(R("ah"), 0.0)
             tt(("val", 0, 320, 2), O, R("dl"), OP.add)
             if j: nW = pick(R("un", 0, 672), FULL)
             tt(("val", 1, 320, 2), E, R("dl"), OP.subtract)
             ga(part(SG, 160, 320), R("val"), part(nW, 10, 20))
+            filler()
             gv(part(SG, 0, 160), R("val"), part(nW, 0, 10))
+            filler()
             if j == 2: break
             ga(O, SG, R("io_"))
             ga(E, SG, R("ie"))
@@ -250,7 +262,8 @@ def rank_program(g, core, T, topo):
             roll("d_e", [(R("ie"), eW, -1, 1)])
             roll("d_n", [(R("nt"), NF, -1, 16)])
             if j == 0:
-                signs(2, (0, 1))
+                if k: signs(2, (0, 1))
+                if k == 1: dma("d_v", [("s", lambda e: e.dma_start(T.vt[:], T.v[:]), [R("vt")], [])])
                 if k == 0:
                     dma("d_w", [("s", lambda e: e.dma_start(T.wq[:, 0:512].bitcast(dt.uint8), T.wc[:, 0:2048]), [R("wq")], []),
                                 ("s", lambda e: e.dma_start(T.wsp[:, 0:512], T.ws[:, 0:512]), [R("wsp")], [])])
@@ -259,12 +272,15 @@ def rank_program(g, core, T, topo):
                 gcopy(R("xg", 0, 320 * NV), R("xh", 0, 320 * NV))
         turn("us", 0, "bs", 0, 160)
         ga(R("ah", 192, 352), SG, R("io_"))
+        turn("us", 352, "bs", 160, 160, [0])
         s0 = pick(R("us", 0, 352), HALF)
         ga(part(NF, 0, 160), R("nt"), s0)
         ga(R("ah", 16, 176), SG, R("ie"))
         turn("ua", 352, "ah", 176, 160)
+        turn("us", 352, "bs", 160, 160, [1])
         iW = new("lst", 32)
         oW = pick(UO, HALF, iW)
+        s1 = pick(R("us", 352, 704), HALF)
         turn("un", 0, "bn", 0, 160)
         def means(b, l, e):
             if b < NV: gt(("zn", 320 * b + e, 320 * b + 320, 2), R("xh", 320 * b, 320 * b + 320), l, ("xg", 320 * b + e, 320 * b + 320, 2), OP.add)
@@ -273,28 +289,32 @@ def rank_program(g, core, T, topo):
         n0 = pick(R("un", 0, 352), HALF)
         send(src, T["ln%d" % k][:, 0:10], ap(n0), rn, n0)
         turn("ua", 0, "ah", 0, 160)
-        means(0, oW, 1)
+        if V1: means(0, oW, 1)
         eW = pick(UE, HALF, part(iW, 10, 26))
         iW = part(iW, 0, 20)
         send(dst, T["li%d" % k][:, 0:20], ap(iW), ri, iW)
+        if not V1: means(0, oW, 1)
+        ga(part(NF, 160, 320), R("nt"), s1)
         for b in range(NV, 4): means(b, eW, 0)
         for b in range(1, NV): means(b, oW, 1)
-        turn("us", 352, "bs", 160, 160)
-        means(0, eW, 0)
-        s1 = pick(R("us", 352, 704), HALF)
-        ga(part(NF, 160, 320), R("nt"), s1)
-        for b in range(1, NV): means(b, eW, 0)
+        for b in range(NV): means(b, eW, 0)
         for b in range(NV, 4): tt(R("zn", 320 * b, 320 * b + 320), R("zt", 320 * b, 320 * b + 320), R("xh", 320 * b, 320 * b + 320), OP.add)
-        turn("un", 352, "bn", 160, 160)
+        if k < 2:
+            roll("d_s", [(R("ow"), oW, 3, 1)])
+            roll("d_o", [(R("io_"), oW, 2, 1)])
+            roll("d_e", [(R("ie"), eW, 2, 1)])
+            roll("d_a", [(R("aa"), R("ah"), 3, 16)])
+            roll("d_n", [(R("nt"), NF, 2, 16)])
+        early = V2 or k == 0
         if k == 0:
             act(R("yt0", 640, 1280), R("xt0", 640, 1280), 32.0)
-            fill(R("bk"), 0.0)
-        n2 = pick(R("un"), TWO)
-        if k == 0:
-            for b in range(4): quant(R("eq", 128 * b, 128 * b + 128), R("es", 128 * b, 128 * b + 128), R("et", 3 - b, 515 - b))
+        if early:
+            turn("un", 352, "bn", 160, 160)
         arrives(rn, ENG, [R("ln%d" % k)])
         for b in range(4):
-            (ga if b < 2 else gv)(("ft", b, 640, 4), R("zn", 320 * b, 320 * b + 320), R("ln%d" % k))
+            (ga if b < V4 else gv)(("ft", b, 640, 4), R("zn", 320 * b, 320 * b + 320), R("ln%d" % k))
+        if early: n2 = pick(R("un"), TWO)
+        else: turn("un", 352, "bn", 160, 160, [0])
         fq, fp = R("fq%d" % k), R("fp%d" % k)
         quant(fq, fp, R("ft"))
         send(dst, T["lq%d" % k][:, 0:160].bitcast(dt.uint8), ap(fq).bitcast(dt.uint8), rd, fq)
@@ -302,20 +322,19 @@ def rank_program(g, core, T, topo):
         arrives(ri, ENG, [R("li%d" % k)])
         ga(("gf", 0, 320, 2), NF, R("li%d" % k, 0, 10))
         ga(("gf", 1, 320, 2), NF, R("li%d" % k, 10, 20))
-        ga(R("bk", 16, 176), R("gf"), part(n2, 10, 20))
+        if not early:
+            turn("un", 352, "bn", 160, 160, [1])
+            n2 = pick(R("un"), TWO)
+        if k == 2: quant(R("qv"), R("qvs"), R("vt"))
+        if V5:
+            ga(R("bk", 112, 176), R("gf"), part(n2, 16, 20))
+            gv(R("bk", 16, 112), R("gf"), part(n2, 10, 16))
+        else: ga(R("bk", 16, 176), R("gf"), part(n2, 10, 20))
         if k < 2:
-            roll("d_a", [(R("aa"), R("ah"), 3, 16)])
-            roll("d_s", [(R("ns"), n2, 3, 1), (R("ow"), oW, 3, 1)])
-            roll("d_o", [(R("io_"), oW, 2, 1)])
-            roll("d_e", [(R("ie"), eW, 2, 1)])
-            roll("d_n", [(R("nt"), NF, 2, 16)])
+            roll("d_q", [(R("ns"), n2, 3, 1)])
             nW, oW = R("ns"), R("ow")
         if k == 0:
             act(R("yt0", 0, 640), R("xt0", 0, 640), 32.0)
-        if k == 2:
-            quant(R("qv"), R("qvs"), R("vt"))
-            ts(R("nmf"), NF, 160.0, OP.add)
-            dma("d_os", [("s", lambda e: e.dma_start(T.nm[:], T.nmf[0:128:16, :]), [], [R("nmf")])])
         turn("uk", 0, "bk", 0, 160)
         kW = pick(R("uk"), HALF)
         for b in range(4):
@@ -325,14 +344,14 @@ def rank_program(g, core, T, topo):
             q, p = R("vq%d" % k, c, c + 160), R("vp%d" % k, c, c + 160)
             quant(q, p, R(tile))
             for b in range(4): mm(bank(half, b), R("wq", 128 * b, 128 * b + 128), R("wsp", 128 * b, 128 * b + 128), q, p)
-        def state(half):
-            c = 160 * half
-            for b in range(4):
-                y, x = ("yt%d" % (k + 1), 4 * c + b, 4 * c + 640, 4), ("xt%d" % (k + 1), 4 * c + b, 4 * c + 640, 4)
-                tt(y, bank(half, b), ("yt%d" % k, 4 * c + b, 4 * c + 640, 4), OP.add)
-                if b < 3: act(x, y, 0.03125)
+        def plane(name, half, b): return (name, 640 * half + b, 640 * half + 640, 4)
+        def adds(half):
+            for b in range(4): tt(plane("yt%d" % (k + 1), half, b), bank(half, b), plane("yt%d" % k, half, b), OP.add)
+        def scale(half, bs, q):
+            for b in bs:
+                y, x = plane("yt%d" % (k + 1), half, b), plane("xt%d" % (k + 1), half, b)
+                if q == "a": act(x, y, 0.03125)
                 else: ts(x, y, 0.03125, OP.mult)
-            quantx(k + 1, half)
         def out(half):
             c = 160 * half
             q, p = qx(3, half)
@@ -343,23 +362,46 @@ def rank_program(g, core, T, topo):
             act(y, bank(half, 0))
             dma("d_os", [("a", lambda e: e.dma_start(T.y[:, c:c + 160], ap(y)), [], [y])])
         layer(1, "vo")
+        if k == 2:
+            ts(R("nmf"), NF, 160.0, OP.add)
+            dma("d_os", [("s", lambda e: e.dma_start(T.nm[:], T.nmf[0:128:16, :]), [], [R("nmf")])])
+        else: tt(R("em"), E, O, OP.subtract)
         arrives(rd, 2 * ENG, [R("lq%d" % k), R("lp%d" % k)])
         for b in range(4): mm(bank(0, b), R("eq", 128 * b, 128 * b + 128), R("es", 128 * b, 128 * b + 128), R("lq%d" % k), R("lp%d" % k))
-        state(1)
-        for b in (0, 2, 1, 3): (cp if b == 3 else act)(("vf", b, 640, 4), bank(0, b))
-        if k < 2: scores(k + 1, 1, [0, 1, 2])
-        layer(0, "vf")
-        if k < 2:
-            flags(1, 0)
-            tt(R("em"), E, O, OP.subtract)
-        else: out(1)
-        state(0)
+        adds(1)
+        if V3 == 0:
+            scale(1, (0, 1, 2), "a")
+            scale(1, (3,), "v")
+            quantx(k + 1, 1)
+            for b in range(4): (cp if b % 2 else act)(("vf", b, 640, 4), bank(0, b))
+            if k < 2: scores(k + 1, 1, [0, 1, 2])
+            else: out(1)
+            layer(0, "vf")
+            if k < 2: flags(1, 0)
+            adds(0)
+        else:
+            if V3 == 1:
+                for b in range(4): (cp if b >= VF else act)(("vf", b, 640, 4), bank(0, b))
+                layer(0, "vf")
+                scale(1, (0, 1), "a")
+                scale(1, (2, 3), "v")
+            else:
+                ts(R("xt%d" % (k + 1), 640, 1280), R("yt%d" % (k + 1), 640, 1280), 0.03125, OP.mult)
+                for b in range(4): (cp if b == 3 else act)(("vf", b, 640, 4), bank(0, b))
+                layer(0, "vf")
+            quantx(k + 1, 1)
+            if k < 2: scores(k + 1, 1, [0, 1, 2])
+            else: out(1)
+            adds(0)
+        scale(0, range(VX), "a")
+        scale(0, range(VX, 4), "v")
+        quantx(k + 1, 0)
         if k < 2:
             scores(k + 1, 0, [0, 1, 2])
+            if V3: flags(1, 0)
             halves(k + 1, 1)
             flags(0, 0)
             signs(1, (1, 0))
-            if k == 0: dma("d_v", [("s", lambda e: e.dma_start(T.vt[:], T.v[:]), [R("vt")], [])])
         else: out(0)
     for q, sem in QSEM.items(): total[sem] = count[q]
     for sem, val in total.items(): g.wait_ge(T.sem[sem], val)

@@ -5,27 +5,27 @@ from concourse.mybir import dt, AluOpType as OP, AxisListType, ActivationFunctio
 STEP = [1, 2, 4]
 BF, F16, F32, I32, U16, U8, CODE = "bfloat16", "float16", "float32", "int32", "uint16", "uint8", "float8_e4m3fn_x4"
 NV = 2
-ROT = [(17 * j - 48) % 128 for j in range(3)]
-V4 = 2
-V5 = 1
-VX = 2
-VF = 2
-V1 = 1
-V2 = 1
-V3 = 1
+HV = 10
+LINK = "dl ns v0 nx v1 sa sv".split()
+TOLD = "Oa ss Ev sx na is em ix sd ri rn".split()
+TAIL = "s0s Oa s1s s0x Ev n0a s1x is n0s ix n0x sn si z2 z3 n1a m0 m1 a2 a3 n1s roll f f".split()
+MEET = "f0a f1a f2v f3v n1x fq g0a g1v qv f k1a k0v rn f ks em kx sd o0v o1v o2a o3a L1 nm".split()
+LAND = "U A1 c0v c1a c2v c3a L0 x10a x11a x12v x13v Q1 A0 x00a x01a S1 x02v x03v Q0".split()
+ROT = -48 % 128
+UP, DOWN = 1024.0, -4096.0
+LEAST = 2.0 ** -93
 SCRATCH = {
     "nls": ("sbuf", [128, 20], I32), "nlt": ("sbuf", [128, 20], I32), "ut": ("sbuf", [128, 648], BF), "vt": ("sbuf", [128, 512], BF),
-    "qu": ("sbuf", [128, 162], CODE), "qus": ("sbuf", [128, 162], U8), "qo": ("sbuf", [128, 128], CODE), "qos": ("sbuf", [128, 128], U8),
+    "qu": ("sbuf", [128, 162], CODE), "qus": ("sbuf", [128, 162], U8), "qp": ("sbuf", [128, 384], CODE), "qps": ("sbuf", [128, 384], U8),
     "qv": ("sbuf", [128, 128], CODE), "qvs": ("sbuf", [128, 128], U8), "wq": ("sbuf", [128, 512], CODE), "wsp": ("sbuf", [128, 512], U8),
     "et": ("sbuf", [128, 528], BF), "eq": ("sbuf", [128, 512], CODE), "es": ("sbuf", [128, 512], U8),
-    "icf": ("sbuf", [128, 320], BF), "ci": ("sbuf", [128, 32], I32), "co": ("sbuf", [128, 8], U16),
-    "fw": ("sbuf", [128, 960], BF), "aa": ("sbuf", [128, 368], BF), "ah": ("sbuf", [128, 368], BF), "em": ("sbuf", [128, 160], F16), "dl": ("sbuf", [128, 160], F16),
-    "val": ("sbuf", [128, 320], BF), "bs": ("sbuf", [128, 352], BF), "bn": ("sbuf", [128, 352], BF), "bx": ("sbuf", [128, 320], BF), "bk": ("sbuf", [128, 192], BF),
-    "us": ("sbuf", [128, 704], BF), "un": ("sbuf", [128, 704], BF), "ua": ("sbuf", [128, 704], BF), "uk": ("sbuf", [128, 352], BF),
-    "nt": ("sbuf", [128, 320], BF), "io_": ("sbuf", [128, 10], U16), "ie": ("sbuf", [128, 10], U16), "ns": ("sbuf", [128, 20], U16), "ow": ("sbuf", [128, 10], U16), "gf": ("sbuf", [128, 320], BF),
-    "lst": ("sbuf", [128, 1600], U16),
-    "xh": ("sbuf", [128, 1280], BF), "xg": ("sbuf", [128, 1280], BF), "zn": ("sbuf", [128, 1280], BF), "ft": ("sbuf", [128, 640], BF), "vo": ("sbuf", [128, 640], BF), "vf": ("sbuf", [128, 640], BF),
-    "zt": ("sbuf", [128, 1280], BF), "yo": ("sbuf", [128, 320], F32), "nmf": ("sbuf", [128, 320], F32),
+    "icf": ("sbuf", [128, 320], BF), "vtab": ("sbuf", [128, 320], BF), "ntab": ("sbuf", [128, 320], F32), "ci": ("sbuf", [128, 128], I32), "cf": ("sbuf", [128, 8], F32), "ul": ("sbuf", [128, 24], U16),
+    "mk": ("sbuf", [128, 320], BF), "mk2": ("sbuf", [128, 32], BF), "wr": ("sbuf", [128, 1280], F16), "lst": ("sbuf", [128, 1600], U16),
+    "fw": ("sbuf", [128, 960], BF), "oe": ("sbuf", [128, 320], BF), "oh": ("sbuf", [128, 320], BF), "em": ("sbuf", [128, 160], F16), "sd": ("sbuf", [128, 160], F16), "dl": ("sbuf", [128, 160], F16),
+    "val": ("sbuf", [128, 320], BF), "sg": ("sbuf", [128, 320], BF), "nf": ("sbuf", [128, 320], BF), "bk": ("sbuf", [128, 160], BF), "gf": ("sbuf", [128, 320], BF),
+    "nt": ("sbuf", [128, 320], BF), "it": ("sbuf", [128, 20], U16), "ns": ("sbuf", [128, 20], U16), "ow": ("sbuf", [128, 10], U16),
+    "yc": ("sbuf", [128, 1280], BF), "zt": ("sbuf", [128, 1280], BF), "zn": ("sbuf", [128, 1280], BF), "ft": ("sbuf", [128, 640], BF), "vo": ("sbuf", [128, 640], BF), "vf": ("sbuf", [128, 640], BF),
+    "yo": ("sbuf", [128, 320], F32), "nmf": ("sbuf", [128, 320], F32),
 }
 for _k in range(4):
     SCRATCH.update({"xt%d" % _k: ("sbuf", [128, 1280], BF), "yt%d" % _k: ("sbuf", [128, 1280], BF), "xq%d" % _k: ("sbuf", [128, 320], CODE), "xs%d" % _k: ("sbuf", [128, 320], U8)})
@@ -110,298 +110,244 @@ def rank_program(g, core, T, topo):
 
     def R(name, lo=0, hi=None, st=1): return (name, lo, SCRATCH[name][1][1] if hi is None else hi, st)
     def ap(r): return T[r[0]][:, r[1]:r[2]:r[3]] if r[3] != 1 else T[r[0]][:, r[1]:r[2]]
-    slots = {"lst": 0, "ci": 0}
+    def size(r): return (r[2] - r[1] + r[3] - 1) // r[3]
+    slots = {"lst": 0, "ci": 0, "wr": 0}
     def new(name, n):
+        if slots[name] + n > SCRATCH[name][1][1]: slots[name] = 0
         a = slots[name]
         slots[name] += n
         return R(name, a, a + n)
+    def newlist(n): return part(new("lst", 32), 0, n)
     def part(r, a, b, st=1): return (r[0], r[1] + a, r[1] + b, st)
 
     def tt(out, a, b, o): op("v", lambda: g.vector.tensor_tensor(ap(out), ap(a), ap(b), o), [out], [a, b])
     def ts(out, a, s1, o1, s2=None, o2=None):
-        if o2 is None: op("v", lambda: g.vector.tensor_scalar(ap(out), ap(a), s1, None, o1), [out], [a])
-        else: op("v", lambda: g.vector.tensor_scalar(ap(out), ap(a), s1, s2, o1, o2), [out], [a])
+        col = [s1] if isinstance(s1, tuple) else []
+        c1 = ap(s1) if col else s1
+        if o2 is None: op("v", lambda: g.vector.tensor_scalar(ap(out), ap(a), c1, None, o1), [out], [a] + col)
+        else: op("v", lambda: g.vector.tensor_scalar(ap(out), ap(a), c1, s2, o1, o2), [out], [a] + col)
     def cp(out, a): op("v", lambda: g.vector.tensor_copy(ap(out), ap(a)), [out], [a])
-    def gv(out, win, off): op("v", lambda: g.vector.tensor_copy(ap(out), ap(win).indirect(ap(off))), [out], [win, off])
-    def ga(out, win, off): op("a", lambda: g.scalar.activation(ap(out), ap(win).indirect(ap(off)), AF.Copy), [out], [win, off])
+    def gv(out, win, off, scale=1.0):
+        if scale == 1.0: op("v", lambda: g.vector.tensor_copy(ap(out), ap(win).indirect(ap(off))), [out], [win, off])
+        else: op("v", lambda: g.vector.tensor_scalar(ap(out), ap(win).indirect(ap(off)), scale, None, OP.mult), [out], [win, off])
+    def ga(out, win, off, scale=1.0):
+        if scale == 1.0: op("a", lambda: g.scalar.activation(ap(out), ap(win).indirect(ap(off)), AF.Copy), [out], [win, off])
+        else: op("a", lambda: g.scalar.activation(ap(out), ap(win).indirect(ap(off)), AF.Copy, scale=scale), [out], [win, off])
+    gather = {"v": gv, "a": ga}
     def gt(out, win, off, b, o): op("v", lambda: g.vector.tensor_tensor(ap(out), ap(win).indirect(ap(off)), ap(b), o), [out], [win, off, b])
-    def act(out, a, scale=1.0, f=AF.Copy): op("a", lambda: g.scalar.activation(ap(out), ap(a), f, scale=scale), [out], [a])
+    def act(out, a, scale=1.0): op("a", lambda: g.scalar.activation(ap(out), ap(a), AF.Copy, scale=scale), [out], [a])
     def fill(out, c): op("v", lambda: g.vector.memset(ap(out), c), [out], [])
+    def scan(out, d0, d1, o0, o1): op("v", lambda: g.vector.tensor_tensor_scan(ap(out), ap(d0), ap(d1), 0.0, o0, o1), [out], [d0, d1])
     def quant(q, s, a): op("v", lambda: g.vector.quantize_mx(ap(q), ap(s), ap(a)), [q, s], [a])
     def mm(out, l, ls, r, rs): op("t", lambda: g.tensor.matmul_mx(ap(out), ap(l), ap(ls), ap(r), ap(rs), True, True), [out], [l, ls, r, rs])
     def iota(out, pattern, base, cm, flag=False):
         op("g", lambda: g.iota(ap(out), pattern, base, cm, allow_small_or_imprecise_dtypes=True) if flag else g.iota(ap(out), pattern, base, cm), [out], [])
     def gcopy(out, a):
-        op("g", lambda: g.affine_select(ap(out), ap(a), [[0, out[2] - out[1]]], OP.is_gt, 0.0, 1, 0), [out], [a])
-    def turn(u, uo, b, bo, n, which=(0, 1)):
-        for w in which:
-            o, i = ((R(u, uo, uo + n), R(b, bo + 16, bo + 16 + n)), (R(u, uo + n, uo + 2 * n + 32), R(b, bo, bo + n + 32)))[w]
-            op("v", lambda: g.vector.transpose(ap(o), ap(i)), [o], [i])
-    FULL, TWO, HALF = R("co", 0, 2), R("co", 2, 4), R("co", 4, 5)
-    def pick(win, c, o=None):
-        n = 16 * (c[2] - c[1])
-        o = part(o, 0, n) if o else new("lst", n)
-        op("v", lambda: g.vector.tensor_scalar(ap(o), ap(win).indirect(ap(c)), 160.0, None, OP.add), [o], [win, c])
-        return part(o, 0, 10 * (c[2] - c[1]))
+        op("g", lambda: g.affine_select(ap(out), ap(a), [[0, size(out)]], OP.is_gt, 0.0, 1, 0), [out], [a])
+    LOW, SUNK = R("cf", 0, 1), R("cf", 1, 2)
+    def wrap(f, o=None):
+        n = size(f)
+        w, o = new("wr", n), o or newlist(n // 16)
+        return o, (lambda: scan(w, R("mk", 0, n), f, OP.add, OP.max)), (lambda: ts(o, part(w, 15, n, 16), SUNK, OP.add, 160.0, OP.add))
+    def run(order, calls):
+        for name in order:
+            if name in calls: calls[name]()
     def roll(sem, moves, q="s"):
         ms = []
-        for o, i, up, st in moves:
+        for o, i, up in moves:
             d = 16 * (up % 8)
             for a, b, c in ((d, 128, 0), (0, d, 128 - d)):
-                ms.append((q, lambda e, o=o, i=i, a=a, b=b, c=c, st=st: e.dma_start(T[o[0]][a:b:st, o[1]:o[2]], T[i[0]][c:c + b - a:st, i[1]:i[2]]), [o], [i]))
+                ms.append((q, lambda e, o=o, i=i, a=a, b=b, c=c: e.dma_start(T[o[0]][a:b, o[1]:o[2]], T[i[0]][c:c + b - a, i[1]:i[2]]), [o], [i]))
         dma(sem, ms)
 
-    def rows(sem, q, out, up):
+    def rows(sem, out, up):
         d = 16 * up
-        dma(sem, [(q, lambda e: e.dma_start(T[out][d:128, :], T.nl[0:128 - d, :]), [R(out)], []), (q, lambda e: e.dma_start(T[out][0:d, :], T.nl[128 - d:128, :]), [R(out)], [])])
-    rows("d_ns", "s", "nls", 3)
-    rows("d_nt", "a", "nlt", 2)
-    r0 = 4 * ROT[0]
+        dma(sem, [("s", lambda e: e.dma_start(T[out][d:128, :], T.nl[0:128 - d, :]), [R(out)], []), ("a", lambda e: e.dma_start(T[out][0:d, :], T.nl[128 - d:128, :]), [R(out)], [])])
+    rows("d_ns", "nls", 3)
+    rows("d_nt", "nlt", 2)
+    r0 = 4 * ROT
     dma("d_u", [("s", lambda e: e.dma_start(T.ut[:, 0:512 - r0], T.u[:, r0:512]), [R("ut")], []), ("a", lambda e: e.dma_start(T.ut[:, 512 - r0:648], T.u[:, 0:136 + r0]), [R("ut")], [])])
     for h, q in ((0, "s"), (1, "a")):
         dma("d_x%d" % h, [(q, lambda e, h=h: e.dma_start(T.xt0[:, 640 * h:640 * h + 640], T.x[:, 640 * h:640 * h + 640]), [R("xt0", 640 * h, 640 * h + 640)], [])])
 
-    p, t, q, h, a, s, m, q2, s1, s2, ge, f1, f2, f3 = [new("ci", 2) for _ in range(14)]
-    iota(p, [[0, 2]], 0, 1)
-    iota(t, [[256, 2]], 0, 0)
+    d0, d1, ui, t0, t1, t2 = new("ci", 16), new("ci", 16), new("ci", 24), new("ci", 20), new("ci", 20), new("ci", 20)
+    iota(d0, [[1, 16]], 128, -1)
     iota(R("icf"), [[1, 320]], -160, 0, True)
+    iota(ui, [[17, 3], [16, 8]], 0, 0)
+    iota(R("vtab"), [[1, 160], [160, 2]], -160, 0, True)
     fill(R("et"), 1.0)
+    ts(d1, d0, 15, OP.bitwise_and)
+    fill(LOW, -LEAST)
+    ts(R("mk2", 0, 16), d1, 0.0, OP.is_equal, DOWN, OP.mult)
+    ts(R("mk2", 16, 32), d1, 1.0, OP.is_equal, UP, OP.mult)
+    ts(SUNK, part(d1, 15, 16), 0.0, OP.not_equal, -UP, OP.mult)
+    tt(R("mk", 0, 16), R("mk2", 0, 16), R("mk2", 16, 32), OP.add)
+    for n in (16, 32, 64, 128, 256): act(R("mk", n, min(2 * n, 320)), R("mk", 0, min(n, 320 - n)))
     op("g", lambda: g.affine_select(T.et[:], T.et[:], [[1, 528]], OP.is_equal, 0.0, -3, -4), [R("et")], [R("et")])
-    for b, pads in (("aa", (0, 176, 352)), ("bs", (0, 336)), ("bn", (0, 336)), ("ah", (0, 176, 352)), ("bk", (0, 176))):
-        for c in pads: act(R(b, c, c + 16), R("icf", 0, 16), 0.0)
-    ts(h, p, 4, OP.arith_shift_right)
-    ts(q, p, 15, OP.bitwise_and)
-    tt(a, p, h, OP.add)
-    ts(q2, q, 16.0, OP.mult)
-    ts(s, a, 1, OP.bitwise_and)
-    tt(m, q2, t, OP.add)
-    ts(s2, s, 176.0, OP.mult)
-    ts(s1, s, 336.0, OP.mult)
-    ts(ge, m, 160.0, OP.is_ge, 192.0, OP.mult)
-    tt(f2, m, s2, OP.add)
-    tt(f1, m, s1, OP.add)
-    ts(HALF, part(f2, 0, 1), 351.0, OP.min)
-    tt(f3, f2, ge, OP.add)
-    ts(FULL, f1, 671.0, OP.min)
-    ts(TWO, f3, 703.0, OP.min)
 
-    E, O = R("aa", 16, 176), R("aa", 192, 352)
-    UE, UO = R("ua", 0, 352), R("ua", 352, 704)
-    nW, nT = new("lst", 20), new("lst", 20)
-    cp(nW, R("nls"))
+    O, E = ("oe", 0, 320, 2), ("oe", 1, 320, 2)
+    nN, nT, nW = newlist(20), newlist(20), newlist(20)
+    cp(R("ul"), ui)
+    cp(nN, R("nls"))
+    op("v", lambda: g.vector.tensor_copy(T.oe[:, 0:320].indirect(ap(nN)), ap(R("icf"))), [R("oe")], [nN, R("icf")])
     cp(nT, R("nlt"))
-    op("v", lambda: g.vector.tensor_copy(T.bx[:, 0:320].indirect(ap(nW)), ap(R("icf"))), [R("bx")], [nW, R("icf")])
-    ga(R("nt"), R("icf"), nT)
+    def upick(j, q):
+        c, s, l = R("qp", 128 * j, 128 * j + 128), R("qps", 128 * j, 128 * j + 128), R("ul", 8 * j, 8 * j + 8)
+        if q == "a": op("a", lambda: g.scalar.activation(ap(s), ap(R("qus")).indirect(ap(l)), AF.Copy), [s], [R("qus"), l])
+        else: op("v", lambda: g.vector.tensor_copy(ap(c).bitcast(dt.uint32), ap(R("qu")).bitcast(dt.uint32).indirect(ap(l))), [c], [R("qu"), l])
+    def bank(half, b, n=160): return R("p%d" % (4 * half + b), 0, n)
+    def qx(k, a, b): return R("xq%d" % k, 160 * a, 160 * b), R("xs%d" % k, 160 * a, 160 * b)
+    def quantx(k, half): quant(*qx(k, half, half + 1), R("xt%d" % k, 640 * half, 640 * half + 640))
+    def US(j): return R("qp", 128 * j, 128 * j + 128), R("qps", 128 * j, 128 * j + 128)
+    def score0(k, half): mm(bank(half, 0), *US(0), *qx(k, half, half + 1))
+    def score(k, j): mm(bank(1, j, 320), *US(j), *qx(k, 0, 2))
+    def sign(out, a): op("a", lambda: g.scalar.activation(ap(out), ap(a), AF.Sign, bias=ap(LOW)), [out], [a, LOW])
+    def sign0(half): sign(R("fw", 160 * half, 160 * half + 160), bank(half, 0))
+    def signs(j): sign(R("fw", 320 * j, 320 * j + 320), bank(1, j, 320))
+    def plane(name, b, a=0, n=320): return R(name, 320 * b + a, 320 * b + a + n)
+    def lay(k): gcopy(R("yc", 0, 320 * NV), R("yt%d" % k, 0, 320 * NV))
+    def em(): tt(R("em"), E, O, OP.subtract)
+    def sd(): tt(R("sd"), E, O, OP.add)
+    def ys(bs):
+        for b in bs: act(plane("yt0", b), ("xt0", b, 1280, 4), 32.0)
+    iW = newlist(20)
+    oW, o1, o2 = wrap(O, part(iW, 10, 20))
+    eW, e1, e2 = wrap(E, part(iW, 0, 10))
     quant(R("qu"), R("qus"), R("ut"))
-    o1, o2 = ROT[1] - ROT[0], ROT[2] - ROT[0]
-    dma("d_q", [("s", lambda e: e.dma_start(T.qo[:, 0:128].bitcast(dt.uint8), T.qu[:, o1:o1 + 128].bitcast(dt.uint8)), [R("qo")], [R("qu")]),
-                ("s", lambda e: e.dma_start(T.qos[:, 0:128], T.qus[:, o1:o1 + 128]), [R("qos")], [R("qus")])])
-    cp(O, ("bx", 0, 320, 2))
-    act(E, ("bx", 1, 320, 2))
-    US = [(R("qu", 0, 128), R("qus", 0, 128)), (R("qo"), R("qos")), (R("qu", o2, o2 + 128), R("qus", o2, o2 + 128))]
-    def bank(half, b): return R("p%d" % (4 * half + b), 0, 160)
-    def qx(k, half): return R("xq%d" % k, 160 * half, 160 * half + 160), R("xs%d" % k, 160 * half, 160 * half + 160)
-    def quantx(k, half): quant(*qx(k, half), R("xt%d" % k, 640 * half, 640 * half + 640))
-    def scores(k, half, js):
-        for j in js: mm(bank(half, j), *US[j], *qx(k, half))
-    def fl(half, j): return R("fw", 320 * j + 160 * half, 320 * j + 160 * half + 160)
-    def signs(j, hs):
-        for half in hs: act(fl(half, j), bank(half, j), f=AF.Sign)
-        act(R("fw", 320 * j, 320 * j + 320), R("fw", 320 * j, 320 * j + 320), f=AF.Relu)
-    def flags(half, j): ts(fl(half, j), bank(half, j), 0.0, OP.is_gt)
-    def halves(k, half):
-        c = 160 * half
-        for b in range(4): act(R("xh", 320 * b + c, 320 * b + c + 160), (("xt%d" % k), 4 * c + b, 4 * c + 640, 4), 0.5)
-    quantx(0, 0)
-    scores(0, 0, [0])
-    turn("ua", 352, "aa", 176, 160)
-    turn("ua", 0, "aa", 0, 160)
-    oW = pick(UO, HALF)
+    o1()
+    e1()
+    upick(0, "a")
+    upick(0, "v")
+    ga(R("nt"), R("vtab"), nT)
+    o2()
+    e2()
+    roll("d_o", [(R("it"), iW, -1)])
     quantx(0, 1)
-    scores(0, 1, [0])
-    eW = pick(UE, HALF)
-    roll("d_o", [(R("io_"), oW, -1, 1)])
-    roll("d_e", [(R("ie"), eW, -1, 1)])
-    tt(R("em"), E, O, OP.subtract)
-    flags(0, 0)
-    flags(1, 0)
-    for j in (2, 1):
-        for h in (0, 1): scores(0, h, [j])
-    halves(0, 1)
-    signs(2, (0, 1))
-    spare = [lambda: flags(0, 1), lambda: flags(1, 1)] + [lambda b=b: quant(R("eq", 128 * b, 128 * b + 128), R("es", 128 * b, 128 * b + 128), R("et", 3 - b, 515 - b)) for b in range(4)]
+    score0(0, 1)
+    quantx(0, 0)
+    score0(0, 0)
+    sign0(1)
+    sign0(0)
+    em()
+    sd()
+    ts(t0, R("nls"), 1, OP.bitwise_and)
+    ts(t1, R("nls"), 1, OP.arith_shift_right)
+    ts(t2, t0, 160.0, OP.mult)
+    ys((0, 1))
+    lay(0)
+    upick(1, "a")
+    spare = [lambda b=b: quant(R("eq", 128 * b, 128 * b + 128), R("es", 128 * b, 128 * b + 128), R("et", 3 - b, 515 - b)) for b in range(4)]
     def filler():
         if spare: spare.pop(0)()
 
-    SG, NF = R("bs", 16, 336), R("bn", 16, 336)
+    SG, NF, IE, IO = R("sg"), R("nf"), R("it", 0, 10), R("it", 10, 20)
     for k, s in enumerate(STEP):
         src, dst = T.cores[(rank - s) % N], T.cores[(rank + s) % N]
         rn, ri, rd = "rn%d" % k, "ri%d" % k, "rd%d" % k
         for j in range(3):
-            gt(R("dl"), R("fw", 320 * j, 320 * j + 320), oW, R("em"), OP.mult)
-            if j: turn("un", 0, "bn", 0, 320)
-            tt(("val", 0, 320, 2), O, R("dl"), OP.add)
-            if j: nW = pick(R("un", 0, 672), FULL)
-            tt(("val", 1, 320, 2), E, R("dl"), OP.subtract)
-            ga(part(SG, 160, 320), R("val"), part(nW, 10, 20))
-            filler()
-            gv(part(SG, 0, 160), R("val"), part(nW, 0, 10))
-            filler()
+            calls = {"dl": lambda: gt(R("dl"), R("fw", 320 * j, 320 * j + 320), oW, R("em"), OP.mult),
+                     "v0": lambda: tt(R("val", 0, 160), R("sd"), R("dl"), OP.add), "v1": lambda: tt(R("val", 160, 320), R("sd"), R("dl"), OP.subtract),
+                     "sa": lambda: ga(part(SG, 16 * HV, 320), R("val"), part(nW, HV, 20), 0.5), "sv": lambda: gv(part(SG, 0, 16 * HV), R("val"), part(nW, 0, HV), 0.5)}
+            if j: nW, calls["ns"], calls["nx"] = wrap(NF)
+            elif k == 0: calls.update({"ns": lambda: tt(t0, t1, t2, OP.add), "nx": lambda: cp(nW, t0)})
+            run(LINK, calls)
             if j == 2: break
-            ga(O, SG, R("io_"))
-            ga(E, SG, R("ie"))
-            turn("us", 0, "bs", 0, 320)
-            turn("ua", 352, "aa", 176, 160)
-            sW = pick(R("us", 0, 672), FULL)
-            oW = pick(UO, HALF)
-            ga(NF, R("nt"), sW)
-            roll("d_o", [(R("io_"), oW, -1, 1)])
-            turn("ua", 0, "aa", 0, 160)
-            tt(R("em"), E, O, OP.subtract)
-            eW = pick(UE, HALF)
-            roll("d_e", [(R("ie"), eW, -1, 1)])
-            roll("d_n", [(R("nt"), NF, -1, 16)])
-            if j == 0:
-                if k: signs(2, (0, 1))
-                if k == 1: dma("d_v", [("s", lambda e: e.dma_start(T.vt[:], T.v[:]), [R("vt")], [])])
-                if k == 0:
-                    dma("d_w", [("s", lambda e: e.dma_start(T.wq[:, 0:512].bitcast(dt.uint8), T.wc[:, 0:2048]), [R("wq")], []),
-                                ("s", lambda e: e.dma_start(T.wsp[:, 0:512], T.ws[:, 0:512]), [R("wsp")], [])])
-            else:
-                halves(k, 0)
-                gcopy(R("xg", 0, 320 * NV), R("xh", 0, 320 * NV))
-        turn("us", 0, "bs", 0, 160)
-        ga(R("ah", 192, 352), SG, R("io_"))
-        turn("us", 352, "bs", 160, 160, [0])
-        s0 = pick(R("us", 0, 352), HALF)
-        ga(part(NF, 0, 160), R("nt"), s0)
-        ga(R("ah", 16, 176), SG, R("ie"))
-        turn("ua", 352, "ah", 176, 160)
-        turn("us", 352, "bs", 160, 160, [1])
-        iW = new("lst", 32)
-        oW = pick(UO, HALF, iW)
-        s1 = pick(R("us", 352, 704), HALF)
-        turn("un", 0, "bn", 0, 160)
-        def means(b, l, e):
-            if b < NV: gt(("zn", 320 * b + e, 320 * b + 320, 2), R("xh", 320 * b, 320 * b + 320), l, ("xg", 320 * b + e, 320 * b + 320, 2), OP.add)
-            else: ga(("zt", 320 * b + e, 320 * b + 320, 2), R("xh", 320 * b, 320 * b + 320), l)
-        for b in range(NV, 4): means(b, oW, 1)
-        n0 = pick(R("un", 0, 352), HALF)
-        send(src, T["ln%d" % k][:, 0:10], ap(n0), rn, n0)
-        turn("ua", 0, "ah", 0, 160)
-        if V1: means(0, oW, 1)
-        eW = pick(UE, HALF, part(iW, 10, 26))
-        iW = part(iW, 0, 20)
-        send(dst, T["li%d" % k][:, 0:20], ap(iW), ri, iW)
-        if not V1: means(0, oW, 1)
-        ga(part(NF, 160, 320), R("nt"), s1)
-        for b in range(NV, 4): means(b, eW, 0)
-        for b in range(1, NV): means(b, oW, 1)
-        for b in range(NV): means(b, eW, 0)
-        for b in range(NV, 4): tt(R("zn", 320 * b, 320 * b + 320), R("zt", 320 * b, 320 * b + 320), R("xh", 320 * b, 320 * b + 320), OP.add)
-        if k < 2:
-            roll("d_s", [(R("ow"), oW, 3, 1)])
-            roll("d_o", [(R("io_"), oW, 2, 1)])
-            roll("d_e", [(R("ie"), eW, 2, 1)])
-            roll("d_a", [(R("aa"), R("ah"), 3, 16)])
-            roll("d_n", [(R("nt"), NF, 2, 16)])
-        early = V2 or k == 0
-        if k == 0:
-            act(R("yt0", 640, 1280), R("xt0", 640, 1280), 32.0)
-        if early:
-            turn("un", 352, "bn", 160, 160)
-        arrives(rn, ENG, [R("ln%d" % k)])
+            E, O = R("oe", 0, 160), R("oe", 160, 320)
+            if k == 0:
+                upick(j + 1, "v")
+                score(0, j + 1)
+            calls = {"Oa": lambda: ga(O, SG, IO), "Ea": lambda: ga(E, SG, IE), "Ev": lambda: gv(E, SG, IE), "Ov": lambda: gv(O, SG, IO), "em": em, "sd": sd, "f": filler,
+                     "na": lambda: (signs(j + 1) if k == 0 else None, ga(NF, R("nt"), sW)), "ri": lambda: roll("d_o", [(R("it"), iW, -1)]), "rn": lambda: roll("d_n", [(R("nt"), NF, -1)])}
+            sW, calls["ss"], calls["sx"] = wrap(SG)
+            iW, calls["is"], calls["ix"] = wrap(R("oe"))
+            oW = part(iW, 10, 20)
+            run(TOLD, calls)
+            if j == 0 and k: signs(2)
+            if j == 0 and k == 0:
+                ys((2, 3))
+                upick(2, "a")
+            if j == 1 and k == 0:
+                dma("d_w", [("s", lambda e: e.dma_start(T.wq[:, 0:512].bitcast(dt.uint8), T.wc[:, 0:2048]), [R("wq")], []),
+                            ("s", lambda e: e.dma_start(T.wsp[:, 0:512], T.ws[:, 0:512]), [R("wsp")], [])])
+            if j == 1 and k == 1: dma("d_v", [("s", lambda e: e.dma_start(T.vt[:], T.v[:]), [R("vt")], [])])
+        EH, OH, Y, Y1, X1 = R("oh", 0, 160), R("oh", 160, 320), "yt%d" % k, "yt%d" % (k + 1), "xt%d" % (k + 1)
+        iW, n2 = newlist(20), newlist(20)
+        eW, oW, n0 = part(iW, 0, 10), part(iW, 10, 20), part(n2, 0, 10)
+        def mean(b, e):
+            gt(plane("zn", b, 160 * e, 160), plane(Y, b), (eW, oW)[e], ("yc", 320 * b + e, 320 * b + 320, 2), OP.add)
+        def add(b, e): tt(plane("zn", b, 160 * e, 160), plane("zt", b, 160 * e, 160), (Y, 320 * b + e, 320 * b + 320, 2), OP.add)
+        def rolls():
+            roll("d_n", [(R("nt"), NF, 2)])
+            roll("d_a", [(R("oe"), R("oh"), 3)])
+            roll("d_s", [(R("ow"), oW, 3)])
+            roll("d_o", [(R("it"), iW, 2)])
+        calls = {"Oa": lambda: ga(OH, SG, IO), "Ea": lambda: ga(EH, SG, IE), "Ev": lambda: gv(EH, SG, IE), "Ov": lambda: gv(OH, SG, IO), "f": filler,
+                 "sn": lambda: send(src, T["ln%d" % k][:, 0:10], ap(n0), rn, n0), "si": lambda: send(dst, T["li%d" % k][:, 0:20], ap(iW), ri, iW)}
         for b in range(4):
-            (ga if b < V4 else gv)(("ft", b, 640, 4), R("zn", 320 * b, 320 * b + 320), R("ln%d" % k))
-        if early: n2 = pick(R("un"), TWO)
-        else: turn("un", 352, "bn", 160, 160, [0])
-        fq, fp = R("fq%d" % k), R("fp%d" % k)
-        quant(fq, fp, R("ft"))
-        send(dst, T["lq%d" % k][:, 0:160].bitcast(dt.uint8), ap(fq).bitcast(dt.uint8), rd, fq)
-        send(dst, T["lp%d" % k][:, 0:160], ap(fp), rd, fp)
-        arrives(ri, ENG, [R("li%d" % k)])
-        ga(("gf", 0, 320, 2), NF, R("li%d" % k, 0, 10))
-        ga(("gf", 1, 320, 2), NF, R("li%d" % k, 10, 20))
-        if not early:
-            turn("un", 352, "bn", 160, 160, [1])
-            n2 = pick(R("un"), TWO)
-        if k == 2: quant(R("qv"), R("qvs"), R("vt"))
-        if V5:
-            ga(R("bk", 112, 176), R("gf"), part(n2, 16, 20))
-            gv(R("bk", 16, 112), R("gf"), part(n2, 10, 16))
-        else: ga(R("bk", 16, 176), R("gf"), part(n2, 10, 20))
-        if k < 2:
-            roll("d_q", [(R("ns"), n2, 3, 1)])
-            nW, oW = R("ns"), R("ow")
-        if k == 0:
-            act(R("yt0", 0, 640), R("xt0", 0, 640), 32.0)
-        turn("uk", 0, "bk", 0, 160)
-        kW = pick(R("uk"), HALF)
-        for b in range(4):
-            (gv if b < 2 else ga)(("vo", b, 640, 4), R("zn", 320 * b, 320 * b + 320), kW)
+            calls.update({"z%d" % b: lambda b=b: ga(plane("zt", b), plane(Y, b), iW), "m%d" % b: lambda b=b: (mean(b, 1), mean(b, 0)), "a%d" % b: lambda b=b: (add(b, 1), add(b, 0))})
+        s0, calls["s0s"], calls["s0x"] = wrap(part(SG, 0, 160))
+        s1, calls["s1s"], calls["s1x"] = wrap(part(SG, 160, 320))
+        _, calls["is"], calls["ix"] = wrap(R("oh"), iW)
+        _, calls["n0s"], calls["n0x"] = wrap(part(NF, 0, 160), n0)
+        _, calls["n1s"], calls["n1x"] = wrap(part(NF, 160, 320), part(n2, 10, 20))
+        kW, calls["ks"], calls["kx"] = wrap(R("bk"))
+        fq, fp, ln, li = R("fq%d" % k), R("fp%d" % k), R("ln%d" % k), R("li%d" % k)
+        lq, lp = R("lq%d" % k), R("lp%d" % k)
+        def leave():
+            quant(fq, fp, R("ft"))
+            send(dst, ap(lq).bitcast(dt.uint8), ap(fq).bitcast(dt.uint8), rd, fq)
+            send(dst, ap(lp), ap(fp), rd, fp)
         def layer(half, tile):
             c = 160 * half
             q, p = R("vq%d" % k, c, c + 160), R("vp%d" % k, c, c + 160)
             quant(q, p, R(tile))
             for b in range(4): mm(bank(half, b), R("wq", 128 * b, 128 * b + 128), R("wsp", 128 * b, 128 * b + 128), q, p)
-        def plane(name, half, b): return (name, 640 * half + b, 640 * half + 640, 4)
         def adds(half):
-            for b in range(4): tt(plane("yt%d" % (k + 1), half, b), bank(half, b), plane("yt%d" % k, half, b), OP.add)
-        def scale(half, bs, q):
-            for b in bs:
-                y, x = plane("yt%d" % (k + 1), half, b), plane("xt%d" % (k + 1), half, b)
-                if q == "a": act(x, y, 0.03125)
-                else: ts(x, y, 0.03125, OP.mult)
-        def out(half):
+            for b in range(4): tt(plane(Y1, b, 160 * half, 160), bank(half, b), plane(Y, b, 160 * half, 160), OP.add)
+        def scale(half, b, q):
+            y, x = plane(Y1, b, 160 * half, 160), (X1, 640 * half + b, 640 * half + 640, 4)
+            if q == "a": act(x, y, 0.03125)
+            else: ts(x, y, 0.03125, OP.mult)
+        def unpack():
+            for b in range(4): mm(bank(0, b), R("eq", 128 * b, 128 * b + 128), R("es", 128 * b, 128 * b + 128), lq, lp)
+        def state(half):
             c = 160 * half
-            q, p = qx(3, half)
+            quantx(k + 1, half)
+            if k < 2: return score0(k + 1, half)
+            q, p = qx(3, half, half + 1)
             mm(bank(half, 0), R("qv"), R("qvs"), q, p)
             dma("d_os", [("s", lambda e: e.dma_start(T.oc[:, 4 * c:4 * c + 640], ap(q).bitcast(dt.uint8)), [], [q])] +
                 [("s", lambda e, i=i: e.dma_start(T.osc[4 * i:4 * i + 4, c:c + 160], T.xs3[32 * i:32 * i + 4, c:c + 160]), [], [p]) for i in range(4)])
             y = R("yo", c, c + 160)
             act(y, bank(half, 0))
             dma("d_os", [("a", lambda e: e.dma_start(T.y[:, c:c + 160], ap(y)), [], [y])])
-        layer(1, "vo")
-        if k == 2:
-            ts(R("nmf"), NF, 160.0, OP.add)
+        def names():
+            ga(R("nmf"), R("ntab"), n2)
             dma("d_os", [("s", lambda e: e.dma_start(T.nm[:], T.nmf[0:128:16, :]), [], [R("nmf")])])
-        else: tt(R("em"), E, O, OP.subtract)
-        arrives(rd, 2 * ENG, [R("lq%d" % k), R("lp%d" % k)])
-        for b in range(4): mm(bank(0, b), R("eq", 128 * b, 128 * b + 128), R("es", 128 * b, 128 * b + 128), R("lq%d" % k), R("lp%d" % k))
-        adds(1)
-        if V3 == 0:
-            scale(1, (0, 1, 2), "a")
-            scale(1, (3,), "v")
-            quantx(k + 1, 1)
-            for b in range(4): (cp if b % 2 else act)(("vf", b, 640, 4), bank(0, b))
-            if k < 2: scores(k + 1, 1, [0, 1, 2])
-            else: out(1)
-            layer(0, "vf")
-            if k < 2: flags(1, 0)
-            adds(0)
-        else:
-            if V3 == 1:
-                for b in range(4): (cp if b >= VF else act)(("vf", b, 640, 4), bank(0, b))
-                layer(0, "vf")
-                scale(1, (0, 1), "a")
-                scale(1, (2, 3), "v")
-            else:
-                ts(R("xt%d" % (k + 1), 640, 1280), R("yt%d" % (k + 1), 640, 1280), 0.03125, OP.mult)
-                for b in range(4): (cp if b == 3 else act)(("vf", b, 640, 4), bank(0, b))
-                layer(0, "vf")
-            quantx(k + 1, 1)
-            if k < 2: scores(k + 1, 1, [0, 1, 2])
-            else: out(1)
-            adds(0)
-        scale(0, range(VX), "a")
-        scale(0, range(VX, 4), "v")
-        quantx(k + 1, 0)
+        for q in "va":
+            calls.update({"n0" + q: lambda q=q: gather[q](part(NF, 0, 160), R("nt"), s0), "n1" + q: lambda q=q: gather[q](part(NF, 160, 320), R("nt"), s1),
+                          "g0" + q: lambda q=q: gather[q](R("gf", 0, 160), NF, part(li, 10, 20)), "g1" + q: lambda q=q: gather[q](R("gf", 160, 320), NF, part(li, 0, 10)),
+                          "k0" + q: lambda q=q: gather[q](R("bk", 0, 96), R("gf"), part(n2, 10, 16)), "k1" + q: lambda q=q: gather[q](R("bk", 96, 160), R("gf"), part(n2, 16, 20))})
+            for b in range(4):
+                calls.update({"f%d%s" % (b, q): lambda b=b, q=q: gather[q](("ft", b, 640, 4), plane("zn", b), ln, 1 / 64),
+                              "o%d%s" % (b, q): lambda b=b, q=q: gather[q](("vo", b, 640, 4), plane("zn", b), kW, 1 / 64),
+                              "c%d%s" % (b, q): lambda b=b, q=q: (cp if q == "v" else act)(("vf", b, 640, 4), bank(0, b)),
+                              "x0%d%s" % (b, q): lambda b=b, q=q: scale(0, b, q), "x1%d%s" % (b, q): lambda b=b, q=q: scale(1, b, q)})
+        calls.update({"fq": leave, "L0": lambda: layer(0, "vf"), "L1": lambda: layer(1, "vo"), "A0": lambda: adds(0), "A1": lambda: adds(1), "U": unpack,
+                      "Q0": lambda: state(0), "Q1": lambda: state(1)})
+        if k < 2: calls.update({"roll": rolls, "rn": lambda: roll("d_q", [(R("ns"), n2, 3)]), "em": em, "sd": sd, "S1": lambda: sign0(1)})
+        else: calls.update({"qv": lambda: quant(R("qv"), R("qvs"), R("vt")), "nm": names})
+        arrives(rn, ENG, [ln])
+        arrives(ri, ENG, [li])
+        arrives(rd, 2 * ENG, [lq, lp])
+        run(TAIL + MEET + LAND, calls)
+        nW, oW = R("ns"), R("ow")
+        if k == 0: iota(R("ntab"), [[1, 2], [2, 160]], 0, 0, True)
         if k < 2:
-            scores(k + 1, 0, [0, 1, 2])
-            if V3: flags(1, 0)
-            halves(k + 1, 1)
-            flags(0, 0)
-            signs(1, (1, 0))
-        else: out(0)
+            score(k + 1, 1)
+            score(k + 1, 2)
+            sign0(0)
+            signs(1)
+            lay(k + 1)
     for q, sem in QSEM.items(): total[sem] = count[q]
     for sem, val in total.items(): g.wait_ge(T.sem[sem], val)

@@ -6,11 +6,13 @@ STEP = [1, 2, 4]
 BF, F16, F32, I32, U16, U8, CODE = "bfloat16", "float16", "float32", "int32", "uint16", "uint8", "float8_e4m3fn_x4"
 NV = 2
 HV = 10
+START = "nN ul sc nT qu pa os es nt pv Q1 Q0 ox ex ri S1 S0 em F1 t0 t1 F0 t2 y0 y1 pb".split()
+FIRST = "dl dn v0 v1 w0 Oa Ev w1 na is em ix sd p2 ri rn".split()
 LINK = "dl ns v0 nx v1 sa sv".split()
 TOLD = "Oa ss Ev sx na is em ix sd ri rn".split()
-TAIL = "s0s Oa s1s s0x Ev n0a s1x is n0s ix n0x sn si z2 z3 n1a m0 m1 a2 a3 n1s roll f f".split()
-MEET = "f0a f1a f2v f3v n1x fq g0a g1v qv f k1a k0v rn f ks em kx sd o0v o1v o2a o3a L1 nm".split()
-LAND = "U A1 c0v c1a c2v c3a L0 x10a x11a x12v x13v Q1 A0 x00a x01a S1 x02v x03v Q0".split()
+TAIL = "s0s s1s s0x Oa s1x n0v Ea n0s is n0x sn ix si n1a z2 z3 n1s m0 m1 n1x a2 a3 roll e0 e1".split()
+MEET = "f0a f1a f2v f3v g1a g0v fq k1a k0v rn ks e2 kx e3 o0a o3a o1v o2v qv q1 P Q L1 nm A10 A11 A12 A13".split()
+LAND = "U x10a c0v c1a c2v c3v x12a q0 L0 x13v ps x11a Q1 A00 A01 A02 A03 x00a x01v x02v x03v F1 Q0 px en em y1 y0 F0".split()
 ROT = -48 % 128
 UP, DOWN = 1024.0, -4096.0
 LEAST = 2.0 ** -93
@@ -19,11 +21,12 @@ SCRATCH = {
     "qu": ("sbuf", [128, 162], CODE), "qus": ("sbuf", [128, 162], U8), "qp": ("sbuf", [128, 384], CODE), "qps": ("sbuf", [128, 384], U8),
     "qv": ("sbuf", [128, 128], CODE), "qvs": ("sbuf", [128, 128], U8), "wq": ("sbuf", [128, 512], CODE), "wsp": ("sbuf", [128, 512], U8),
     "et": ("sbuf", [128, 528], BF), "eq": ("sbuf", [128, 512], CODE), "es": ("sbuf", [128, 512], U8),
-    "icf": ("sbuf", [128, 320], BF), "vtab": ("sbuf", [128, 320], BF), "ntab": ("sbuf", [128, 320], F32), "ci": ("sbuf", [128, 128], I32), "cf": ("sbuf", [128, 8], F32), "ul": ("sbuf", [128, 24], U16),
-    "mk": ("sbuf", [128, 320], BF), "mk2": ("sbuf", [128, 32], BF), "wr": ("sbuf", [128, 1280], F16), "lst": ("sbuf", [128, 1600], U16),
+    "icf": ("sbuf", [128, 320], BF), "vtab": ("sbuf", [128, 320], BF), "ntab": ("sbuf", [128, 320], F32), "ci": ("sbuf", [128, 256], I32), "cf": ("sbuf", [128, 8], F32), "ul": ("sbuf", [128, 24], U16),
+    "mk": ("sbuf", [128, 320], BF), "mk2": ("sbuf", [128, 160], BF), "wr": ("sbuf", [128, 1280], F16), "lst": ("sbuf", [128, 1600], U16),
     "fw": ("sbuf", [128, 960], BF), "oe": ("sbuf", [128, 320], BF), "oh": ("sbuf", [128, 320], BF), "em": ("sbuf", [128, 160], F16), "sd": ("sbuf", [128, 160], F16), "dl": ("sbuf", [128, 160], F16),
     "val": ("sbuf", [128, 320], BF), "sg": ("sbuf", [128, 320], BF), "nf": ("sbuf", [128, 320], BF), "bk": ("sbuf", [128, 160], BF), "gf": ("sbuf", [128, 320], BF),
-    "nt": ("sbuf", [128, 320], BF), "it": ("sbuf", [128, 20], U16), "ns": ("sbuf", [128, 20], U16), "ow": ("sbuf", [128, 10], U16),
+    "nt": ("sbuf", [128, 320], BF), "it": ("sbuf", [128, 20], U16), "ns": ("sbuf", [128, 20], U16), "iq": ("sbuf", [128, 20], U16),
+    "nq": ("sbuf", [128, 320], BF), "pt": ("sbuf", [128, 320], BF), "qt": ("sbuf", [128, 320], BF), "en": ("sbuf", [128, 160], F16), "dn": ("sbuf", [128, 160], F16), "van": ("sbuf", [128, 320], BF),
     "yc": ("sbuf", [128, 1280], BF), "zt": ("sbuf", [128, 1280], BF), "zn": ("sbuf", [128, 1280], BF), "ft": ("sbuf", [128, 640], BF), "vo": ("sbuf", [128, 640], BF), "vf": ("sbuf", [128, 640], BF),
     "yo": ("sbuf", [128, 320], F32), "nmf": ("sbuf", [128, 320], F32),
 }
@@ -35,7 +38,7 @@ for _k in range(3):
 for _k in range(8):
     SCRATCH["p%d" % _k] = ("psum", [128, 512], F32)
 QSEM = {"v": "qv_", "a": "qa_", "t": "qt_", "g": "qg_"}
-SEMAPHORES = list(QSEM.values()) + ["d_ns", "d_nt", "d_u", "d_x0", "d_x1", "d_w", "d_v", "d_q", "d_o", "d_e", "d_n", "d_s", "d_a", "d_os", "sent"] + ["r%s%d" % (a, k) for a in "nid" for k in range(3)]
+SEMAPHORES = list(QSEM.values()) + ["d_ns", "d_nt", "d_u", "d_x0", "d_x1", "d_w", "d_v", "d_q", "d_o", "d_e", "d_n", "d_s", "d_a", "d_p", "d_os", "sent"] + ["r%s%d" % (a, k) for a in "nid" for k in range(3)]
 
 
 def rank_program(g, core, T, topo):
@@ -170,27 +173,23 @@ def rank_program(g, core, T, topo):
     for h, q in ((0, "s"), (1, "a")):
         dma("d_x%d" % h, [(q, lambda e, h=h: e.dma_start(T.xt0[:, 640 * h:640 * h + 640], T.x[:, 640 * h:640 * h + 640]), [R("xt0", 640 * h, 640 * h + 640)], [])])
 
-    d0, d1, ui, t0, t1, t2 = new("ci", 16), new("ci", 16), new("ci", 24), new("ci", 20), new("ci", 20), new("ci", 20)
-    iota(d0, [[1, 16]], 128, -1)
+    d0, d1, ui, t0, t1, t2 = new("ci", 80), new("ci", 80), new("ci", 24), new("ci", 20), new("ci", 20), new("ci", 20)
+    iota(d0, [[1, 80]], 128, -1)
     iota(R("icf"), [[1, 320]], -160, 0, True)
     iota(ui, [[17, 3], [16, 8]], 0, 0)
     iota(R("vtab"), [[1, 160], [160, 2]], -160, 0, True)
     fill(R("et"), 1.0)
     ts(d1, d0, 15, OP.bitwise_and)
     fill(LOW, -LEAST)
-    ts(R("mk2", 0, 16), d1, 0.0, OP.is_equal, DOWN, OP.mult)
-    ts(R("mk2", 16, 32), d1, 1.0, OP.is_equal, UP, OP.mult)
+    ts(R("mk2", 0, 80), d1, 0.0, OP.is_equal, DOWN, OP.mult)
+    ts(R("mk2", 80, 160), d1, 1.0, OP.is_equal, UP, OP.mult)
     ts(SUNK, part(d1, 15, 16), 0.0, OP.not_equal, -UP, OP.mult)
-    tt(R("mk", 0, 16), R("mk2", 0, 16), R("mk2", 16, 32), OP.add)
-    for n in (16, 32, 64, 128, 256): act(R("mk", n, min(2 * n, 320)), R("mk", 0, min(n, 320 - n)))
+    tt(R("mk", 0, 80), R("mk2", 0, 80), R("mk2", 80, 160), OP.add)
+    for n in (80, 160): act(R("mk", n, 2 * n), R("mk", 0, n))
     op("g", lambda: g.affine_select(T.et[:], T.et[:], [[1, 528]], OP.is_equal, 0.0, -3, -4), [R("et")], [R("et")])
 
     O, E = ("oe", 0, 320, 2), ("oe", 1, 320, 2)
     nN, nT, nW = newlist(20), newlist(20), newlist(20)
-    cp(R("ul"), ui)
-    cp(nN, R("nls"))
-    op("v", lambda: g.vector.tensor_copy(T.oe[:, 0:320].indirect(ap(nN)), ap(R("icf"))), [R("oe")], [nN, R("icf")])
-    cp(nT, R("nlt"))
     def upick(j, q):
         c, s, l = R("qp", 128 * j, 128 * j + 128), R("qps", 128 * j, 128 * j + 128), R("ul", 8 * j, 8 * j + 8)
         if q == "a": op("a", lambda: g.scalar.activation(ap(s), ap(R("qus")).indirect(ap(l)), AF.Copy), [s], [R("qus"), l])
@@ -202,40 +201,28 @@ def rank_program(g, core, T, topo):
     def score0(k, half): mm(bank(half, 0), *US(0), *qx(k, half, half + 1))
     def score(k, j): mm(bank(1, j, 320), *US(j), *qx(k, 0, 2))
     def sign(out, a): op("a", lambda: g.scalar.activation(ap(out), ap(a), AF.Sign, bias=ap(LOW)), [out], [a, LOW])
-    def sign0(half): sign(R("fw", 160 * half, 160 * half + 160), bank(half, 0))
+    def flag(half): ts(R("fw", 160 * half, 160 * half + 160), bank(half, 0), 0.0, OP.is_gt)
     def signs(j): sign(R("fw", 320 * j, 320 * j + 320), bank(1, j, 320))
     def plane(name, b, a=0, n=320): return R(name, 320 * b + a, 320 * b + a + n)
-    def lay(k): gcopy(R("yc", 0, 320 * NV), R("yt%d" % k, 0, 320 * NV))
+    def lay(k, bs=range(4)):
+        for b in bs:
+            for e in (0, 1): gcopy(plane("yc", b, 160 * e, 160), ("yt%d" % k, 320 * b + e, 320 * b + 320, 2))
     def em(): tt(R("em"), E, O, OP.subtract)
     def sd(): tt(R("sd"), E, O, OP.add)
     def ys(bs):
         for b in bs: act(plane("yt0", b), ("xt0", b, 1280, 4), 32.0)
     iW = newlist(20)
-    oW, o1, o2 = wrap(O, part(iW, 10, 20))
-    eW, e1, e2 = wrap(E, part(iW, 0, 10))
-    quant(R("qu"), R("qus"), R("ut"))
-    o1()
-    e1()
-    upick(0, "a")
-    upick(0, "v")
-    ga(R("nt"), R("vtab"), nT)
-    o2()
-    e2()
-    roll("d_o", [(R("it"), iW, -1)])
-    quantx(0, 1)
-    score0(0, 1)
-    quantx(0, 0)
-    score0(0, 0)
-    sign0(1)
-    sign0(0)
-    em()
-    sd()
-    ts(t0, R("nls"), 1, OP.bitwise_and)
-    ts(t1, R("nls"), 1, OP.arith_shift_right)
-    ts(t2, t0, 160.0, OP.mult)
-    ys((0, 1))
-    lay(0)
-    upick(1, "a")
+    oW = part(iW, 10, 20)
+    calls = {"nN": lambda: cp(nN, R("nls")), "nT": lambda: cp(nT, R("nlt")), "ul": lambda: cp(R("ul"), ui), "nt": lambda: ga(R("nt"), R("vtab"), nT),
+             "sc": lambda: op("v", lambda: g.vector.tensor_copy(T.oe[:, 0:320].indirect(ap(nN)), ap(R("icf"))), [R("oe")], [nN, R("icf")]),
+             "qu": lambda: quant(R("qu"), R("qus"), R("ut")), "pa": lambda: upick(0, "a"), "pv": lambda: upick(0, "v"), "pb": lambda: upick(1, "a"),
+             "ri": lambda: roll("d_o", [(R("it"), iW, -1)]), "em": em, "F0": lambda: flag(0), "F1": lambda: flag(1),
+             "Q0": lambda: quantx(0, 0), "Q1": lambda: quantx(0, 1), "S0": lambda: score0(0, 0), "S1": lambda: score0(0, 1),
+             "t0": lambda: ts(t0, R("nls"), 1, OP.bitwise_and), "t1": lambda: ts(t1, R("nls"), 1, OP.arith_shift_right), "t2": lambda: ts(t2, t0, 160.0, OP.mult),
+             "y0": lambda: (ys((0,)), lay(0, (0,))), "y1": lambda: (ys((1,)), lay(0, (1,)))}
+    _, calls["os"], calls["ox"] = wrap(O, oW)
+    _, calls["es"], calls["ex"] = wrap(E, part(iW, 0, 10))
+    run(START, calls)
     spare = [lambda b=b: quant(R("eq", 128 * b, 128 * b + 128), R("es", 128 * b, 128 * b + 128), R("et", 3 - b, 515 - b)) for b in range(4)]
     def filler():
         if spare: spare.pop(0)()
@@ -246,10 +233,19 @@ def rank_program(g, core, T, topo):
         rn, ri, rd = "rn%d" % k, "ri%d" % k, "rd%d" % k
         for j in range(3):
             calls = {"dl": lambda: gt(R("dl"), R("fw", 320 * j, 320 * j + 320), oW, R("em"), OP.mult),
-                     "v0": lambda: tt(R("val", 0, 160), R("sd"), R("dl"), OP.add), "v1": lambda: tt(R("val", 160, 320), R("sd"), R("dl"), OP.subtract),
-                     "sa": lambda: ga(part(SG, 16 * HV, 320), R("val"), part(nW, HV, 20), 0.5), "sv": lambda: gv(part(SG, 0, 16 * HV), R("val"), part(nW, 0, HV), 0.5)}
+                     "v0": lambda: tt(R("val", 0, 160), R("sd") if j else O, R("dl"), OP.add), "v1": lambda: tt(R("val", 160, 320), R("sd") if j else E, R("dl"), OP.subtract),
+                     "sa": lambda: ga(part(SG, 16 * HV, 320), R("val"), part(nW, HV, 20), 0.5 if j else 1.0), "sv": lambda: gv(part(SG, 0, 16 * HV), R("val"), part(nW, 0, HV), 0.5 if j else 1.0)}
             if j: nW, calls["ns"], calls["nx"] = wrap(NF)
             elif k == 0: calls.update({"ns": lambda: tt(t0, t1, t2, OP.add), "nx": lambda: cp(nW, t0)})
+            if j == 0 and k:
+                calls.update({"dn": lambda: gt(R("dn"), R("fw", 0, 320), oW, R("en"), OP.mult),
+                              "w0": lambda: tt(R("van", 0, 160), R("qt", 160, 320), R("dn"), OP.add), "w1": lambda: tt(R("van", 160, 320), R("qt", 0, 160), R("dn"), OP.subtract),
+                              "na": lambda: ga(NF, R("van"), nW), "em": em, "sd": sd, "ri": lambda: roll("d_o", [(R("it"), iW, -1)]), "rn": lambda: roll("d_n", [(R("nt"), NF, -1)]), "p2": lambda: signs(2)})
+                for q in "va": calls.update({"E" + q: lambda q=q: gather[q](E, R("val"), part(pW, 0, 10)), "O" + q: lambda q=q: gather[q](O, R("val"), part(pW, 10, 20))})
+                iW, calls["is"], calls["ix"] = wrap(R("oe"))
+                run(FIRST, calls)
+                oW = part(iW, 10, 20)
+                continue
             run(LINK, calls)
             if j == 2: break
             E, O = R("oe", 0, 160), R("oe", 160, 320)
@@ -262,9 +258,9 @@ def rank_program(g, core, T, topo):
             iW, calls["is"], calls["ix"] = wrap(R("oe"))
             oW = part(iW, 10, 20)
             run(TOLD, calls)
-            if j == 0 and k: signs(2)
             if j == 0 and k == 0:
                 ys((2, 3))
+                lay(0, (2, 3))
                 upick(2, "a")
             if j == 1 and k == 0:
                 dma("d_w", [("s", lambda e: e.dma_start(T.wq[:, 0:512].bitcast(dt.uint8), T.wc[:, 0:2048]), [R("wq")], []),
@@ -273,37 +269,35 @@ def rank_program(g, core, T, topo):
         EH, OH, Y, Y1, X1 = R("oh", 0, 160), R("oh", 160, 320), "yt%d" % k, "yt%d" % (k + 1), "xt%d" % (k + 1)
         iW, n2 = newlist(20), newlist(20)
         eW, oW, n0 = part(iW, 0, 10), part(iW, 10, 20), part(n2, 0, 10)
-        def mean(b, e):
-            gt(plane("zn", b, 160 * e, 160), plane(Y, b), (eW, oW)[e], ("yc", 320 * b + e, 320 * b + 320, 2), OP.add)
-        def add(b, e): tt(plane("zn", b, 160 * e, 160), plane("zt", b, 160 * e, 160), (Y, 320 * b + e, 320 * b + 320, 2), OP.add)
         def rolls():
-            roll("d_n", [(R("nt"), NF, 2)])
-            roll("d_a", [(R("oe"), R("oh"), 3)])
-            roll("d_s", [(R("ow"), oW, 3)])
+            need("s", [ln], [])
+            roll("d_p", [(R("nq"), NF, 3)])
             roll("d_o", [(R("it"), iW, 2)])
+            roll("d_n", [(R("nt"), NF, 2)])
+            roll("d_s", [(R("iq"), iW, 3)])
+            roll("d_a", [(R("oe"), R("oh"), 3)])
         calls = {"Oa": lambda: ga(OH, SG, IO), "Ea": lambda: ga(EH, SG, IE), "Ev": lambda: gv(EH, SG, IE), "Ov": lambda: gv(OH, SG, IO), "f": filler,
                  "sn": lambda: send(src, T["ln%d" % k][:, 0:10], ap(n0), rn, n0), "si": lambda: send(dst, T["li%d" % k][:, 0:20], ap(iW), ri, iW)}
         for b in range(4):
-            calls.update({"z%d" % b: lambda b=b: ga(plane("zt", b), plane(Y, b), iW), "m%d" % b: lambda b=b: (mean(b, 1), mean(b, 0)), "a%d" % b: lambda b=b: (add(b, 1), add(b, 0))})
+            calls.update({"z%d" % b: lambda b=b: ga(plane("zt", b), plane(Y, b), iW), "m%d" % b: lambda b=b: gt(plane("zn", b), plane(Y, b), iW, plane("yc", b), OP.add),
+                          "a%d" % b: lambda b=b: tt(plane("zn", b), plane("zt", b), plane("yc", b), OP.add)})
         s0, calls["s0s"], calls["s0x"] = wrap(part(SG, 0, 160))
         s1, calls["s1s"], calls["s1x"] = wrap(part(SG, 160, 320))
         _, calls["is"], calls["ix"] = wrap(R("oh"), iW)
         _, calls["n0s"], calls["n0x"] = wrap(part(NF, 0, 160), n0)
         _, calls["n1s"], calls["n1x"] = wrap(part(NF, 160, 320), part(n2, 10, 20))
         kW, calls["ks"], calls["kx"] = wrap(R("bk"))
+        if k < 2: pW, calls["ps"], calls["px"] = wrap(R("pt"))
         fq, fp, ln, li = R("fq%d" % k), R("fp%d" % k), R("ln%d" % k), R("li%d" % k)
         lq, lp = R("lq%d" % k), R("lp%d" % k)
         def leave():
             quant(fq, fp, R("ft"))
             send(dst, ap(lq).bitcast(dt.uint8), ap(fq).bitcast(dt.uint8), rd, fq)
             send(dst, ap(lp), ap(fp), rd, fp)
-        def layer(half, tile):
-            c = 160 * half
-            q, p = R("vq%d" % k, c, c + 160), R("vp%d" % k, c, c + 160)
-            quant(q, p, R(tile))
-            for b in range(4): mm(bank(half, b), R("wq", 128 * b, 128 * b + 128), R("wsp", 128 * b, 128 * b + 128), q, p)
-        def adds(half):
-            for b in range(4): tt(plane(Y1, b, 160 * half, 160), bank(half, b), plane(Y, b, 160 * half, 160), OP.add)
+        def vq(half): return R("vq%d" % k, 160 * half, 160 * half + 160), R("vp%d" % k, 160 * half, 160 * half + 160)
+        def layer(half):
+            for b in range(4): mm(bank(half, b), R("wq", 128 * b, 128 * b + 128), R("wsp", 128 * b, 128 * b + 128), *vq(half))
+        def add(half, b): tt(plane(Y1, b, 160 * half, 160), bank(half, b), plane(Y, b, 160 * half, 160), OP.add)
         def scale(half, b, q):
             y, x = plane(Y1, b, 160 * half, 160), (X1, 640 * half + b, 640 * half + 640, 4)
             if q == "a": act(x, y, 0.03125)
@@ -318,8 +312,10 @@ def rank_program(g, core, T, topo):
             mm(bank(half, 0), R("qv"), R("qvs"), q, p)
             dma("d_os", [("s", lambda e: e.dma_start(T.oc[:, 4 * c:4 * c + 640], ap(q).bitcast(dt.uint8)), [], [q])] +
                 [("s", lambda e, i=i: e.dma_start(T.osc[4 * i:4 * i + 4, c:c + 160], T.xs3[32 * i:32 * i + 4, c:c + 160]), [], [p]) for i in range(4)])
+        def scored(half, q):
+            c = 160 * half
             y = R("yo", c, c + 160)
-            act(y, bank(half, 0))
+            (cp if q == "v" else act)(y, bank(half, 0))
             dma("d_os", [("a", lambda e: e.dma_start(T.y[:, c:c + 160], ap(y)), [], [y])])
         def names():
             ga(R("nmf"), R("ntab"), n2)
@@ -332,21 +328,24 @@ def rank_program(g, core, T, topo):
                 calls.update({"f%d%s" % (b, q): lambda b=b, q=q: gather[q](("ft", b, 640, 4), plane("zn", b), ln, 1 / 64),
                               "o%d%s" % (b, q): lambda b=b, q=q: gather[q](("vo", b, 640, 4), plane("zn", b), kW, 1 / 64),
                               "c%d%s" % (b, q): lambda b=b, q=q: (cp if q == "v" else act)(("vf", b, 640, 4), bank(0, b)),
+                              "A0%d" % b: lambda b=b: add(0, b), "A1%d" % b: lambda b=b: add(1, b),
                               "x0%d%s" % (b, q): lambda b=b, q=q: scale(0, b, q), "x1%d%s" % (b, q): lambda b=b, q=q: scale(1, b, q)})
-        calls.update({"fq": leave, "L0": lambda: layer(0, "vf"), "L1": lambda: layer(1, "vo"), "A0": lambda: adds(0), "A1": lambda: adds(1), "U": unpack,
+        calls.update({"fq": leave, "q0": lambda: quant(*vq(0), R("vf")), "q1": lambda: quant(*vq(1), R("vo")), "L0": lambda: layer(0), "L1": lambda: layer(1), "U": unpack,
                       "Q0": lambda: state(0), "Q1": lambda: state(1)})
-        if k < 2: calls.update({"roll": rolls, "rn": lambda: roll("d_q", [(R("ns"), n2, 3)]), "em": em, "sd": sd, "S1": lambda: sign0(1)})
-        else: calls.update({"qv": lambda: quant(R("qv"), R("qvs"), R("vt")), "nm": names})
+        if k < 2: calls.update({"roll": rolls, "rn": lambda: roll("d_q", [(R("ns"), n2, 3)]), "em": em, "F1": lambda: flag(1), "F0": lambda: flag(0),
+                                  "en": lambda: tt(R("en"), R("qt", 0, 160), R("qt", 160, 320), OP.subtract),
+                                  "P": lambda: ga(R("pt"), R("nq"), R("it")), "Q": lambda: ga(R("qt"), R("nt"), R("iq"))})
+        else: calls.update({"qv": lambda: quant(R("qv"), R("qvs"), R("vt")), "nm": names, "y0": lambda: scored(0, "v"), "y1": lambda: scored(1, "a")})
+        if k == 0: calls.update({"e%d" % b: spare[b] for b in range(4)})
         arrives(rn, ENG, [ln])
         arrives(ri, ENG, [li])
         arrives(rd, 2 * ENG, [lq, lp])
         run(TAIL + MEET + LAND, calls)
-        nW, oW = R("ns"), R("ow")
+        nW, oW = R("ns"), R("iq", 10, 20)
         if k == 0: iota(R("ntab"), [[1, 2], [2, 160]], 0, 0, True)
         if k < 2:
             score(k + 1, 1)
             score(k + 1, 2)
-            sign0(0)
             signs(1)
             lay(k + 1)
     for q, sem in QSEM.items(): total[sem] = count[q]

import numpy as np
from concourse.bass import DstId, RemoteDMATransfer
from concourse.mybir import dt, AluOpType as OP, AxisListType, ActivationFunctionType as AF

STEP = [1, 2, 4]
BF, F16, F32, I32, U16, U8, CODE = "bfloat16", "float16", "float32", "int32", "uint16", "uint8", "float8_e4m3fn_x4"
NV = 2
HV = 10
START = "nN ul sc nT qu pa os es nt pv Q1 Q0 ox ex ri S1 S0 em F1 t0 t1 F0 t2 y0 y1 pb".split()
FIRST = "dl dn v0 v1 w0 Oa Ev w1 na is em ix sd p2 ri rn".split()
LINK = "dl ns v0 nx v1 sa sv".split()
TOLD = "Oa ss Ev sx na is em ix sd ri rn".split()
TAIL = "s0s s1s s0x Oa s1x n0v Ea n0s is n0x sn ix si n1a z2 z3 n1s m0 m1 n1x a2 a3 roll e0 e1".split()
MEET = "f0a f1a f2v f3v g1a g0v fq k1a k0v rn ks e2 kx e3 o0a o3a o1v o2v qv q1 P Q L1 nm A10 A11 A12 A13".split()
LAND = "U x10a c0v c1a c2v c3v x12a q0 L0 x13v ps x11a Q1 A00 A01 A02 A03 x00a x01v x02v x03v F1 Q0 px en em y1 y0 F0".split()
ROT = -48 % 128
UP, DOWN = 1024.0, -4096.0
LEAST = 2.0 ** -93
SCRATCH = {
    "nls": ("sbuf", [128, 20], I32), "nlt": ("sbuf", [128, 20], I32), "ut": ("sbuf", [128, 648], BF), "vt": ("sbuf", [128, 512], BF),
    "qu": ("sbuf", [128, 162], CODE), "qus": ("sbuf", [128, 162], U8), "qp": ("sbuf", [128, 384], CODE), "qps": ("sbuf", [128, 384], U8),
    "qv": ("sbuf", [128, 128], CODE), "qvs": ("sbuf", [128, 128], U8), "wq": ("sbuf", [128, 512], CODE), "wsp": ("sbuf", [128, 512], U8),
    "et": ("sbuf", [128, 528], BF), "eq": ("sbuf", [128, 512], CODE), "es": ("sbuf", [128, 512], U8),
    "icf": ("sbuf", [128, 320], BF), "vtab": ("sbuf", [128, 320], BF), "ntab": ("sbuf", [128, 320], F32), "ci": ("sbuf", [128, 256], I32), "cf": ("sbuf", [128, 8], F32), "ul": ("sbuf", [128, 24], U16),
    "mk": ("sbuf", [128, 320], BF), "mk2": ("sbuf", [128, 160], BF), "wr": ("sbuf", [128, 1280], F16), "lst": ("sbuf", [128, 1600], U16),
    "fw": ("sbuf", [128, 960], BF), "oe": ("sbuf", [128, 320], BF), "oh": ("sbuf", [128, 320], BF), "em": ("sbuf", [128, 160], F16), "sd": ("sbuf", [128, 160], F16), "dl": ("sbuf", [128, 160], F16),
    "val": ("sbuf", [128, 320], BF), "sg": ("sbuf", [128, 320], BF), "nf": ("sbuf", [128, 320], BF), "bk": ("sbuf", [128, 160], BF), "gf": ("sbuf", [128, 320], BF),
    "nt": ("sbuf", [128, 320], BF), "it": ("sbuf", [128, 20], U16), "ns": ("sbuf", [128, 20], U16), "iq": ("sbuf", [128, 20], U16),
    "nq": ("sbuf", [128, 320], BF), "pt": ("sbuf", [128, 320], BF), "qt": ("sbuf", [128, 320], BF), "en": ("sbuf", [128, 160], F16), "dn": ("sbuf", [128, 160], F16), "van": ("sbuf", [128, 320], BF),
    "yc": ("sbuf", [128, 1280], BF), "zt": ("sbuf", [128, 1280], BF), "zn": ("sbuf", [128, 1280], BF), "ft": ("sbuf", [128, 640], BF), "vo": ("sbuf", [128, 640], BF), "vf": ("sbuf", [128, 640], BF),
    "yo": ("sbuf", [128, 320], F32), "nmf": ("sbuf", [128, 320], F32),
}
for _k in range(4):
    SCRATCH.update({"xt%d" % _k: ("sbuf", [128, 1280], BF), "yt%d" % _k: ("sbuf", [128, 1280], BF), "xq%d" % _k: ("sbuf", [128, 320], CODE), "xs%d" % _k: ("sbuf", [128, 320], U8)})
for _k in range(3):
    SCRATCH.update({"fq%d" % _k: ("sbuf", [128, 160], CODE), "fp%d" % _k: ("sbuf", [128, 160], U8), "lq%d" % _k: ("sbuf", [128, 160], CODE), "lp%d" % _k: ("sbuf", [128, 160], U8),
                    "vq%d" % _k: ("sbuf", [128, 320], CODE), "vp%d" % _k: ("sbuf", [128, 320], U8), "ln%d" % _k: ("sbuf", [128, 10], U16), "li%d" % _k: ("sbuf", [128, 20], U16)})
for _k in range(8):
    SCRATCH["p%d" % _k] = ("psum", [128, 512], F32)
QSEM = {"v": "qv_", "a": "qa_", "t": "qt_", "g": "qg_"}
SEMAPHORES = list(QSEM.values()) + ["d_ns", "d_nt", "d_u", "d_x0", "d_x1", "d_w", "d_v", "d_q", "d_o", "d_e", "d_n", "d_s", "d_a", "d_p", "d_os", "sent"] + ["r%s%d" % (a, k) for a in "nid" for k in range(3)]


def rank_program(g, core, T, topo):
    rank = T.rank_of(core)
    if rank is None:
        return
    N = len(T.cores)
    eng = {"v": g.vector, "a": g.scalar, "t": g.tensor, "g": g, "s": g.sync}
    count, total = {q: 0 for q in QSEM}, {}
    seen = {q: {} for q in eng}
    log = {}

    def need(q, reads, writes):
        own, deps = QSEM.get(q), []
        for wr, rs in ((False, reads), (True, writes)):
            for r in rs:
                ps = SCRATCH.get(r[0], ("x",))[0] == "psum"
                for (lo, hi, w, sem, val, clk, st) in log.get(r[0], []):
                    if not ps and (hi <= r[1] or lo >= r[2]): continue
                    if not ps and st == r[3] > 1 and (lo - r[1]) % st: continue
                    if not (w or wr or ps): continue
                    if sem == own and not w: continue
                    deps.append((sem, val, clk))
        best = {}
        for sem, val, clk in deps:
            if val > best.get(sem, (0,))[0]: best[sem] = (val, clk)
        for sem, (val, clk) in sorted(best.items(), key=lambda e: -len(e[1][1])):
            if seen[q].get(sem, 0) >= val: continue
            eng[q].wait_ge(T.sem[sem], val)
            for s, v in list(clk.items()) + [(sem, val)]:
                if seen[q].get(s, 0) < v: seen[q][s] = v

    def note(accesses, w, sem, val, clk):
        for r in accesses:
            a = log.setdefault(r[0], [])
            if w and r[3] == 1: a[:] = [e for e in a if not (r[1] <= e[0] and e[1] <= r[2])]
            a.append((r[1], r[2], w, sem, val, clk, r[3]))

    def op(q, fn, writes, reads):
        need(q, reads, writes)
        count[q] += 1
        fn().then_inc(T.sem[QSEM[q]], 1)
        clk = dict(seen[q])
        clk[QSEM[q]] = count[q]
        note(reads, False, QSEM[q], count[q], clk)
        note(writes, True, QSEM[q], count[q], clk)

    def dma(sem, moves):
        for q, fn, writes, reads in moves: need(q, reads, writes)
        clk = {}
        for q, fn, writes, reads in moves:
            fn(eng[q]).then_inc(T.sem[sem], 16)
            total[sem] = total.get(sem, 0) + 16
            for s, v in seen[q].items(): clk[s] = max(v, clk.get(s, 0))
        for q, fn, writes, reads in moves:
            note(reads, False, sem, total[sem], clk)
        for q, fn, writes, reads in moves:
            note(writes, True, sem, total[sem], clk)

    def arrives(sem, val, regions):
        total[sem] = val
        note(regions, True, sem, val, {})

    def send(dst, out, inn, sem, region):
        need("g", [region], [])
        rid, pid, _ = topo.addr(dst)
        es = topo.engines(core, dst)[:ENG]
        g.remote_dma(out, inn, T.sem[sem], T.sem["sent"], pid, rid, sum(1 << e for e in es))
        total["sent"] = total.get("sent", 0) + len(es)

    ENG = 8

    def R(name, lo=0, hi=None, st=1): return (name, lo, SCRATCH[name][1][1] if hi is None else hi, st)
    def ap(r): return T[r[0]][:, r[1]:r[2]:r[3]] if r[3] != 1 else T[r[0]][:, r[1]:r[2]]
    def size(r): return (r[2] - r[1] + r[3] - 1) // r[3]
    slots = {"lst": 0, "ci": 0, "wr": 0}
    def new(name, n):
        if slots[name] + n > SCRATCH[name][1][1]: slots[name] = 0
        a = slots[name]
        slots[name] += n
        return R(name, a, a + n)
    def newlist(n): return part(new("lst", 32), 0, n)
    def part(r, a, b, st=1): return (r[0], r[1] + a, r[1] + b, st)

    def tt(out, a, b, o): op("v", lambda: g.vector.tensor_tensor(ap(out), ap(a), ap(b), o), [out], [a, b])
    def ts(out, a, s1, o1, s2=None, o2=None):
        col = [s1] if isinstance(s1, tuple) else []
        c1 = ap(s1) if col else s1
        if o2 is None: op("v", lambda: g.vector.tensor_scalar(ap(out), ap(a), c1, None, o1), [out], [a] + col)
        else: op("v", lambda: g.vector.tensor_scalar(ap(out), ap(a), c1, s2, o1, o2), [out], [a] + col)
    def cp(out, a): op("v", lambda: g.vector.tensor_copy(ap(out), ap(a)), [out], [a])
    def gv(out, win, off, scale=1.0):
        if scale == 1.0: op("v", lambda: g.vector.tensor_copy(ap(out), ap(win).indirect(ap(off))), [out], [win, off])
        else: op("v", lambda: g.vector.tensor_scalar(ap(out), ap(win).indirect(ap(off)), scale, None, OP.mult), [out], [win, off])
    def ga(out, win, off, scale=1.0):
        if scale == 1.0: op("a", lambda: g.scalar.activation(ap(out), ap(win).indirect(ap(off)), AF.Copy), [out], [win, off])
        else: op("a", lambda: g.scalar.activation(ap(out), ap(win).indirect(ap(off)), AF.Copy, scale=scale), [out], [win, off])
    gather = {"v": gv, "a": ga}
    def gt(out, win, off, b, o): op("v", lambda: g.vector.tensor_tensor(ap(out), ap(win).indirect(ap(off)), ap(b), o), [out], [win, off, b])
    def act(out, a, scale=1.0): op("a", lambda: g.scalar.activation(ap(out), ap(a), AF.Copy, scale=scale), [out], [a])
    def fill(out, c): op("v", lambda: g.vector.memset(ap(out), c), [out], [])
    def scan(out, d0, d1, o0, o1): op("v", lambda: g.vector.tensor_tensor_scan(ap(out), ap(d0), ap(d1), 0.0, o0, o1), [out], [d0, d1])
    def quant(q, s, a): op("v", lambda: g.vector.quantize_mx(ap(q), ap(s), ap(a)), [q, s], [a])
    def mm(out, l, ls, r, rs): op("t", lambda: g.tensor.matmul_mx(ap(out), ap(l), ap(ls), ap(r), ap(rs), True, True), [out], [l, ls, r, rs])
    def iota(out, pattern, base, cm, flag=False):
        op("g", lambda: g.iota(ap(out), pattern, base, cm, allow_small_or_imprecise_dtypes=True) if flag else g.iota(ap(out), pattern, base, cm), [out], [])
    def gcopy(out, a):
        op("g", lambda: g.affine_select(ap(out), ap(a), [[0, size(out)]], OP.is_gt, 0.0, 1, 0), [out], [a])
    LOW, SUNK = R("cf", 0, 1), R("cf", 1, 2)
    def wrap(f, o=None):
        n = size(f)
        w, o = new("wr", n), o or newlist(n // 16)
        return o, (lambda: scan(w, R("mk", 0, n), f, OP.add, OP.max)), (lambda: ts(o, part(w, 15, n, 16), SUNK, OP.add, 160.0, OP.add))
    def run(order, calls):
        for name in order:
            if name in calls: calls[name]()
    def roll(sem, moves, q="s"):
        ms = []
        for o, i, up in moves:
            d = 16 * (up % 8)
            for a, b, c in ((d, 128, 0), (0, d, 128 - d)):
                ms.append((q, lambda e, o=o, i=i, a=a, b=b, c=c: e.dma_start(T[o[0]][a:b, o[1]:o[2]], T[i[0]][c:c + b - a, i[1]:i[2]]), [o], [i]))
        dma(sem, ms)

    def rows(sem, out, up):
        d = 16 * up
        dma(sem, [("s", lambda e: e.dma_start(T[out][d:128, :], T.nl[0:128 - d, :]), [R(out)], []), ("a", lambda e: e.dma_start(T[out][0:d, :], T.nl[128 - d:128, :]), [R(out)], [])])
    rows("d_ns", "nls", 3)
    rows("d_nt", "nlt", 2)
    r0 = 4 * ROT
    dma("d_u", [("s", lambda e: e.dma_start(T.ut[:, 0:512 - r0], T.u[:, r0:512]), [R("ut")], []), ("a", lambda e: e.dma_start(T.ut[:, 512 - r0:648], T.u[:, 0:136 + r0]), [R("ut")], [])])
    for h, q in ((0, "s"), (1, "a")):
        dma("d_x%d" % h, [(q, lambda e, h=h: e.dma_start(T.xt0[:, 640 * h:640 * h + 640], T.x[:, 640 * h:640 * h + 640]), [R("xt0", 640 * h, 640 * h + 640)], [])])

    d0, d1, ui, t0, t1, t2 = new("ci", 80), new("ci", 80), new("ci", 24), new("ci", 20), new("ci", 20), new("ci", 20)
    iota(d0, [[1, 80]], 128, -1)
    iota(R("icf"), [[1, 320]], -160, 0, True)
    iota(ui, [[17, 3], [16, 8]], 0, 0)
    iota(R("vtab"), [[1, 160], [160, 2]], -160, 0, True)
    fill(R("et"), 1.0)
    ts(d1, d0, 15, OP.bitwise_and)
    fill(LOW, -LEAST)
    ts(R("mk2", 0, 80), d1, 0.0, OP.is_equal, DOWN, OP.mult)
    ts(R("mk2", 80, 160), d1, 1.0, OP.is_equal, UP, OP.mult)
    ts(SUNK, part(d1, 15, 16), 0.0, OP.not_equal, -UP, OP.mult)
    tt(R("mk", 0, 80), R("mk2", 0, 80), R("mk2", 80, 160), OP.add)
    for n in (80, 160): act(R("mk", n, 2 * n), R("mk", 0, n))
    op("g", lambda: g.affine_select(T.et[:], T.et[:], [[1, 528]], OP.is_equal, 0.0, -3, -4), [R("et")], [R("et")])

    O, E = ("oe", 0, 320, 2), ("oe", 1, 320, 2)
    nN, nT, nW = newlist(20), newlist(20), newlist(20)
    def upick(j, q):
        c, s, l = R("qp", 128 * j, 128 * j + 128), R("qps", 128 * j, 128 * j + 128), R("ul", 8 * j, 8 * j + 8)
        if q == "a": op("a", lambda: g.scalar.activation(ap(s), ap(R("qus")).indirect(ap(l)), AF.Copy), [s], [R("qus"), l])
        else: op("v", lambda: g.vector.tensor_copy(ap(c).bitcast(dt.uint32), ap(R("qu")).bitcast(dt.uint32).indirect(ap(l))), [c], [R("qu"), l])
    def bank(half, b, n=160): return R("p%d" % (4 * half + b), 0, n)
    def qx(k, a, b): return R("xq%d" % k, 160 * a, 160 * b), R("xs%d" % k, 160 * a, 160 * b)
    def quantx(k, half): quant(*qx(k, half, half + 1), R("xt%d" % k, 640 * half, 640 * half + 640))
    def US(j): return R("qp", 128 * j, 128 * j + 128), R("qps", 128 * j, 128 * j + 128)
    def score0(k, half): mm(bank(half, 0), *US(0), *qx(k, half, half + 1))
    def score(k, j): mm(bank(1, j, 320), *US(j), *qx(k, 0, 2))
    def sign(out, a): op("a", lambda: g.scalar.activation(ap(out), ap(a), AF.Sign, bias=ap(LOW)), [out], [a, LOW])
    def flag(half): ts(R("fw", 160 * half, 160 * half + 160), bank(half, 0), 0.0, OP.is_gt)
    def signs(j): sign(R("fw", 320 * j, 320 * j + 320), bank(1, j, 320))
    def plane(name, b, a=0, n=320): return R(name, 320 * b + a, 320 * b + a + n)
    def lay(k, bs=range(4)):
        for b in bs:
            for e in (0, 1): gcopy(plane("yc", b, 160 * e, 160), ("yt%d" % k, 320 * b + e, 320 * b + 320, 2))
    def em(): tt(R("em"), E, O, OP.subtract)
    def sd(): tt(R("sd"), E, O, OP.add)
    def ys(bs):
        for b in bs: act(plane("yt0", b), ("xt0", b, 1280, 4), 32.0)
    iW = newlist(20)
    oW = part(iW, 10, 20)
    calls = {"nN": lambda: cp(nN, R("nls")), "nT": lambda: cp(nT, R("nlt")), "ul": lambda: cp(R("ul"), ui), "nt": lambda: ga(R("nt"), R("vtab"), nT),
             "sc": lambda: op("v", lambda: g.vector.tensor_copy(T.oe[:, 0:320].indirect(ap(nN)), ap(R("icf"))), [R("oe")], [nN, R("icf")]),
             "qu": lambda: quant(R("qu"), R("qus"), R("ut")), "pa": lambda: upick(0, "a"), "pv": lambda: upick(0, "v"), "pb": lambda: upick(1, "a"),
             "ri": lambda: roll("d_o", [(R("it"), iW, -1)]), "em": em, "F0": lambda: flag(0), "F1": lambda: flag(1),
             "Q0": lambda: quantx(0, 0), "Q1": lambda: quantx(0, 1), "S0": lambda: score0(0, 0), "S1": lambda: score0(0, 1),
             "t0": lambda: ts(t0, R("nls"), 1, OP.bitwise_and), "t1": lambda: ts(t1, R("nls"), 1, OP.arith_shift_right), "t2": lambda: ts(t2, t0, 160.0, OP.mult),
             "y0": lambda: (ys((0,)), lay(0, (0,))), "y1": lambda: (ys((1,)), lay(0, (1,)))}
    _, calls["os"], calls["ox"] = wrap(O, oW)
    _, calls["es"], calls["ex"] = wrap(E, part(iW, 0, 10))
    run(START, calls)
    spare = [lambda b=b: quant(R("eq", 128 * b, 128 * b + 128), R("es", 128 * b, 128 * b + 128), R("et", 3 - b, 515 - b)) for b in range(4)]
    def filler():
        if spare: spare.pop(0)()

    SG, NF, IE, IO = R("sg"), R("nf"), R("it", 0, 10), R("it", 10, 20)
    for k, s in enumerate(STEP):
        src, dst = T.cores[(rank - s) % N], T.cores[(rank + s) % N]
        rn, ri, rd = "rn%d" % k, "ri%d" % k, "rd%d" % k
        for j in range(3):
            calls = {"dl": lambda: gt(R("dl"), R("fw", 320 * j, 320 * j + 320), oW, R("em"), OP.mult),
                     "v0": lambda: tt(R("val", 0, 160), R("sd") if j else O, R("dl"), OP.add), "v1": lambda: tt(R("val", 160, 320), R("sd") if j else E, R("dl"), OP.subtract),
                     "sa": lambda: ga(part(SG, 16 * HV, 320), R("val"), part(nW, HV, 20), 0.5 if j else 1.0), "sv": lambda: gv(part(SG, 0, 16 * HV), R("val"), part(nW, 0, HV), 0.5 if j else 1.0)}
            if j: nW, calls["ns"], calls["nx"] = wrap(NF)
            elif k == 0: calls.update({"ns": lambda: tt(t0, t1, t2, OP.add), "nx": lambda: cp(nW, t0)})
            if j == 0 and k:
                calls.update({"dn": lambda: gt(R("dn"), R("fw", 0, 320), oW, R("en"), OP.mult),
                              "w0": lambda: tt(R("van", 0, 160), R("qt", 160, 320), R("dn"), OP.add), "w1": lambda: tt(R("van", 160, 320), R("qt", 0, 160), R("dn"), OP.subtract),
                              "na": lambda: ga(NF, R("van"), nW), "em": em, "sd": sd, "ri": lambda: roll("d_o", [(R("it"), iW, -1)]), "rn": lambda: roll("d_n", [(R("nt"), NF, -1)]), "p2": lambda: signs(2)})
                for q in "va": calls.update({"E" + q: lambda q=q: gather[q](E, R("val"), part(pW, 0, 10)), "O" + q: lambda q=q: gather[q](O, R("val"), part(pW, 10, 20))})
                iW, calls["is"], calls["ix"] = wrap(R("oe"))
                run(FIRST, calls)
                oW = part(iW, 10, 20)
                continue
            run(LINK, calls)
            if j == 2: break
            E, O = R("oe", 0, 160), R("oe", 160, 320)
            if k == 0:
                upick(j + 1, "v")
                score(0, j + 1)
            calls = {"Oa": lambda: ga(O, SG, IO), "Ea": lambda: ga(E, SG, IE), "Ev": lambda: gv(E, SG, IE), "Ov": lambda: gv(O, SG, IO), "em": em, "sd": sd, "f": filler,
                     "na": lambda: (signs(j + 1) if k == 0 else None, ga(NF, R("nt"), sW)), "ri": lambda: roll("d_o", [(R("it"), iW, -1)]), "rn": lambda: roll("d_n", [(R("nt"), NF, -1)])}
            sW, calls["ss"], calls["sx"] = wrap(SG)
            iW, calls["is"], calls["ix"] = wrap(R("oe"))
            oW = part(iW, 10, 20)
            run(TOLD, calls)
            if j == 0 and k == 0:
                ys((2, 3))
                lay(0, (2, 3))
                upick(2, "a")
            if j == 1 and k == 0:
                dma("d_w", [("s", lambda e: e.dma_start(T.wq[:, 0:512].bitcast(dt.uint8), T.wc[:, 0:2048]), [R("wq")], []),
                            ("s", lambda e: e.dma_start(T.wsp[:, 0:512], T.ws[:, 0:512]), [R("wsp")], [])])
            if j == 1 and k == 1: dma("d_v", [("s", lambda e: e.dma_start(T.vt[:], T.v[:]), [R("vt")], [])])
        EH, OH, Y, Y1, X1 = R("oh", 0, 160), R("oh", 160, 320), "yt%d" % k, "yt%d" % (k + 1), "xt%d" % (k + 1)
        iW, n2 = newlist(20), newlist(20)
        eW, oW, n0 = part(iW, 0, 10), part(iW, 10, 20), part(n2, 0, 10)
        def rolls():
            need("s", [ln], [])
            roll("d_p", [(R("nq"), NF, 3)])
            roll("d_o", [(R("it"), iW, 2)])
            roll("d_n", [(R("nt"), NF, 2)])
            roll("d_s", [(R("iq"), iW, 3)])
            roll("d_a", [(R("oe"), R("oh"), 3)])
        calls = {"Oa": lambda: ga(OH, SG, IO), "Ea": lambda: ga(EH, SG, IE), "Ev": lambda: gv(EH, SG, IE), "Ov": lambda: gv(OH, SG, IO), "f": filler,
                 "sn": lambda: send(src, T["ln%d" % k][:, 0:10], ap(n0), rn, n0), "si": lambda: send(dst, T["li%d" % k][:, 0:20], ap(iW), ri, iW)}
        for b in range(4):
            calls.update({"z%d" % b: lambda b=b: ga(plane("zt", b), plane(Y, b), iW), "m%d" % b: lambda b=b: gt(plane("zn", b), plane(Y, b), iW, plane("yc", b), OP.add),
                          "a%d" % b: lambda b=b: tt(plane("zn", b), plane("zt", b), plane("yc", b), OP.add)})
        s0, calls["s0s"], calls["s0x"] = wrap(part(SG, 0, 160))
        s1, calls["s1s"], calls["s1x"] = wrap(part(SG, 160, 320))
        _, calls["is"], calls["ix"] = wrap(R("oh"), iW)
        _, calls["n0s"], calls["n0x"] = wrap(part(NF, 0, 160), n0)
        _, calls["n1s"], calls["n1x"] = wrap(part(NF, 160, 320), part(n2, 10, 20))
        kW, calls["ks"], calls["kx"] = wrap(R("bk"))
        if k < 2: pW, calls["ps"], calls["px"] = wrap(R("pt"))
        fq, fp, ln, li = R("fq%d" % k), R("fp%d" % k), R("ln%d" % k), R("li%d" % k)
        lq, lp = R("lq%d" % k), R("lp%d" % k)
        def leave():
            quant(fq, fp, R("ft"))
            send(dst, ap(lq).bitcast(dt.uint8), ap(fq).bitcast(dt.uint8), rd, fq)
            send(dst, ap(lp), ap(fp), rd, fp)
        def vq(half): return R("vq%d" % k, 160 * half, 160 * half + 160), R("vp%d" % k, 160 * half, 160 * half + 160)
        def layer(half):
            for b in range(4): mm(bank(half, b), R("wq", 128 * b, 128 * b + 128), R("wsp", 128 * b, 128 * b + 128), *vq(half))
        def add(half, b): tt(plane(Y1, b, 160 * half, 160), bank(half, b), plane(Y, b, 160 * half, 160), OP.add)
        def scale(half, b, q):
            y, x = plane(Y1, b, 160 * half, 160), (X1, 640 * half + b, 640 * half + 640, 4)
            if q == "a": act(x, y, 0.03125)
            else: ts(x, y, 0.03125, OP.mult)
        def unpack():
            for b in range(4): mm(bank(0, b), R("eq", 128 * b, 128 * b + 128), R("es", 128 * b, 128 * b + 128), lq, lp)
        def state(half):
            c = 160 * half
            quantx(k + 1, half)
            if k < 2: return score0(k + 1, half)
            q, p = qx(3, half, half + 1)
            mm(bank(half, 0), R("qv"), R("qvs"), q, p)
            dma("d_os", [("s", lambda e: e.dma_start(T.oc[:, 4 * c:4 * c + 640], ap(q).bitcast(dt.uint8)), [], [q])] +
                [("s", lambda e, i=i: e.dma_start(T.osc[4 * i:4 * i + 4, c:c + 160], T.xs3[32 * i:32 * i + 4, c:c + 160]), [], [p]) for i in range(4)])
        def scored(half, q):
            c = 160 * half
            y = R("yo", c, c + 160)
            (cp if q == "v" else act)(y, bank(half, 0))
            dma("d_os", [("a", lambda e: e.dma_start(T.y[:, c:c + 160], ap(y)), [], [y])])
        def names():
            ga(R("nmf"), R("ntab"), n2)
            dma("d_os", [("s", lambda e: e.dma_start(T.nm[:], T.nmf[0:128:16, :]), [], [R("nmf")])])
        for q in "va":
            calls.update({"n0" + q: lambda q=q: gather[q](part(NF, 0, 160), R("nt"), s0), "n1" + q: lambda q=q: gather[q](part(NF, 160, 320), R("nt"), s1),
                          "g0" + q: lambda q=q: gather[q](R("gf", 0, 160), NF, part(li, 10, 20)), "g1" + q: lambda q=q: gather[q](R("gf", 160, 320), NF, part(li, 0, 10)),
                          "k0" + q: lambda q=q: gather[q](R("bk", 0, 96), R("gf"), part(n2, 10, 16)), "k1" + q: lambda q=q: gather[q](R("bk", 96, 160), R("gf"), part(n2, 16, 20))})
            for b in range(4):
                calls.update({"f%d%s" % (b, q): lambda b=b, q=q: gather[q](("ft", b, 640, 4), plane("zn", b), ln, 1 / 64),
                              "o%d%s" % (b, q): lambda b=b, q=q: gather[q](("vo", b, 640, 4), plane("zn", b), kW, 1 / 64),
                              "c%d%s" % (b, q): lambda b=b, q=q: (cp if q == "v" else act)(("vf", b, 640, 4), bank(0, b)),
                              "A0%d" % b: lambda b=b: add(0, b), "A1%d" % b: lambda b=b: add(1, b),
                              "x0%d%s" % (b, q): lambda b=b, q=q: scale(0, b, q), "x1%d%s" % (b, q): lambda b=b, q=q: scale(1, b, q)})
        calls.update({"fq": leave, "q0": lambda: quant(*vq(0), R("vf")), "q1": lambda: quant(*vq(1), R("vo")), "L0": lambda: layer(0), "L1": lambda: layer(1), "U": unpack,
                      "Q0": lambda: state(0), "Q1": lambda: state(1)})
        if k < 2: calls.update({"roll": rolls, "rn": lambda: roll("d_q", [(R("ns"), n2, 3)]), "em": em, "F1": lambda: flag(1), "F0": lambda: flag(0),
                                  "en": lambda: tt(R("en"), R("qt", 0, 160), R("qt", 160, 320), OP.subtract),
                                  "P": lambda: ga(R("pt"), R("nq"), R("it")), "Q": lambda: ga(R("qt"), R("nt"), R("iq"))})
        else: calls.update({"qv": lambda: quant(R("qv"), R("qvs"), R("vt")), "nm": names, "y0": lambda: scored(0, "v"), "y1": lambda: scored(1, "a")})
        if k == 0: calls.update({"e%d" % b: spare[b] for b in range(4)})
        arrives(rn, ENG, [ln])
        arrives(ri, ENG, [li])
        arrives(rd, 2 * ENG, [lq, lp])
        run(TAIL + MEET + LAND, calls)
        nW, oW = R("ns"), R("iq", 10, 20)
        if k == 0: iota(R("ntab"), [[1, 2], [2, 160]], 0, 0, True)
        if k < 2:
            score(k + 1, 1)
            score(k + 1, 2)
            signs(1)
            lay(k + 1)
    for q, sem in QSEM.items(): total[sem] = count[q]
    for sem, val in total.items(): g.wait_ge(T.sem[sem], val)
